import numpy as np, ml_dtypes
CORES = [23,119,17,113]
N = 4
BF = ml_dtypes.bfloat16
def gentries(a):
    return np.ascontiguousarray(a.reshape(8, 16, -1).transpose(0, 2, 1)).reshape(8, -1)
def gtable(e):
    e = np.asarray(e); return np.ascontiguousarray(e.reshape(8, -1, 16).transpose(0, 2, 1)).reshape(128, -1).astype(np.int32)
G, C, K, RO, SH = 1024, 4096, 256, 6, 10
NONE = N * G
def batch(rng, keep=(), high=()):
    key = rng.random((8, C)) * np.where(np.arange(C) >> SH == 0, 3.0, 1.0)
    for c in keep: key[:, c] += 4
    for g in high: key[g, :1 << SH] += 4
    s = np.ascontiguousarray(np.argsort(key, axis=1)[:, :N * K]); w = rng.integers(0, NONE, (8, 16, 4)); ro = np.zeros((8, 16, N * K), np.int64)
    for r in range(N):
        for t in range(16):
            if t < RO: ro[:, t, r * K:(r + 1) * K] = (r + t) % N * G + np.argsort(rng.random((8, G)), axis=1)[:, :K]
            else: ro[:, t, r * K:(r + 1) * K] = np.take_along_axis(w[:, t], rng.integers(0, 4, (8, K)), 1)
    return s, ro, w
def living(rng, s, ro, w, share):
    pa = np.full((8, 16, C), NONE, np.int64); live, dead = [], []
    for g in range(8):
        rest = rng.permutation(np.setdiff1d(np.arange(C), s[g])); h = max(int(len(rest) * share), 8)
        a = rest[h:]; m = len(a); v = rng.integers(0, NONE, (16, m))
        for k in range(RO, 16): v[k] = w[g, k][rng.integers(0, 4, m)]
        v = np.where(rng.random((16, m)) < 0.8 * rng.random((1, m)), ro[g][:, np.arange(m) % (N * K)], v)
        no = rng.random((16, m)) < 0.9 * rng.random((1, m)); no[rng.integers(0, 16, m), np.arange(m)] = False
        pa[g][:, a] = np.where(no, NONE, v); live.append(a); dead.append(rest[:h])
    return pa, live, dead
def trunks(rng, s, ro, live, dead):
    op = rng.integers(0, N * K, (N, 8, G))
    for t in rng.permutation(RO):
        for q in range(N):
            r = int((q - t) % N); np.put_along_axis(op[q], ro[:, t, r * K:(r + 1) * K] - q * G, np.ascontiguousarray(np.broadcast_to(r * K + np.arange(K), (8, K))), 1)
    tr = np.zeros((N, 8, 16, G), np.int64); sh = (N, 16, G)
    for g in range(8):
        a = live[g]; m = len(a); top = np.sort(a)[-(m >> 3):]; x = a[rng.integers(0, m, sh)]
        x = np.where(rng.random(sh) < rng.choice(np.array([0.3, 0.6, 0.8, 0.9, 1.0]), (N, 1, G)), top[rng.integers(0, len(top), sh)], x)
        x = np.where(rng.random(sh) < rng.choice(np.array([0.0, 0.1, 0.25]), (N, 1, G)), a[(op[:, g][:, None, :] + N * K * rng.integers(0, 2, sh)) % m], x)
        gone = np.concatenate([dead[g], s[g][::4]])
        tr[:, g] = np.where(rng.random(sh) < rng.choice(np.array([0.0, 0.0, 0.1, 0.3]), (N, 1, G)), gone[rng.integers(0, len(gone), sh)], x)
    return tr
def pack(tr, pa, s, ro):
    return {"trunk": np.ascontiguousarray(tr.reshape(N, 128, G)).astype(np.int32), "paths": np.stack([pa.reshape(128, C)] * N).astype(np.int32),
            "calls": np.stack([gtable(s[:, r * K:(r + 1) * K]) for r in range(N)]), "routes": np.stack([ro[:, :, r * K:(r + 1) * K].reshape(128, K) for r in range(N)]).astype(np.int32)}
def setup_inputs(rng):
    s, ro, w = batch(rng); pa, live, dead = living(rng, s, ro, w, 0.05)
    return pack(trunks(rng, s, ro, live, dead), pa, s, ro)
def setup_inputs_ties(rng):
    edge = np.array([0, C - 1] + [e for b in range(1, C >> SH) for e in ((b << SH) - 1, b << SH)])
    s, ro, w = batch(rng, edge); pa, live, dead = living(rng, s, ro, w, 0.05); tr = trunks(rng, s, ro, live, dead); sh = (N, 16, G); k = np.arange(16)[None, :, None]
    for g in range(8):
        a = np.union1d(live[g], edge); d = np.setdiff1d(np.append(dead[g], s[g][0]), edge)
        few = pa[g][:, live[g][:3]]; pa[g][:, a] = few[:, rng.integers(0, 3, len(a))]
        x = tr[:, g].copy(); x[:, 8:] = x[:, :8][:, ::-1].copy()
        kind = rng.integers(0, 5, (N, 1, G)); end = rng.choice(np.array([0, 15]), (N, 1, G)); z = a[rng.integers(0, len(a), sh)]
        x = np.where(kind == 1, edge[rng.integers(0, len(edge), sh)], np.where(kind == 2, z, x))
        tr[:, g] = np.where(kind == 3, np.where(k == end, d[rng.integers(0, len(d), sh)], z), x)
        j = rng.permutation(N * K)[:64]; r = j // K; c = rng.permutation(live[g])[:64]
        pa[g][:, c] = ro[g][:, j]; tr[r, g, rng.integers(0, 16, 64), ro[g, 0, j] - r * G] = c
        u = rng.permutation(np.setdiff1d(np.nonzero(s[g] >> SH == (C - 1) >> SH)[0], j))[:16]; q = u // K; at = ro[g, 0, u] - q * G
        b = np.sort(rng.permutation(np.setdiff1d(live[g][live[g] >> SH == 0], np.append(edge, c)))[:32].reshape(2, 16), axis=0)
        pa[g][:, b[0]] = ro[g][:, u]; pa[g][:, b[1]] = ro[g][:, u]; h = rng.integers(0, 16, 16)
        pa[g, h, b[0]] = np.where(rng.random(16) < 0.5, NONE, (ro[g, h, u] + 1) % NONE)
        y = tr[:, g]; e = rng.integers(0, 16, 16)
        y[q, :, at] = b[rng.integers(0, 2, (16, 16)), np.arange(16)[:, None]]
        y[q, e, at] = b[1]; y[q, (e + 8) & 15, at] = b[0]
    return pack(tr, pa, s, ro)
def setup_inputs_same(rng):
    few = np.array([0, 1, 2, (1 << SH) - 1]); keep = np.append(few, C - 1)
    s, ro, w = batch(rng, keep, (5, 6, 7)); pa, live, dead = living(rng, s, ro, w, 0.05); tr = trunks(rng, s, ro, live, dead); sh = (N, 16, G)
    for g in range(8):
        pa[g][:, keep] = ro[g][:, rng.integers(0, N * K, len(keep))]
        top = np.union1d(live[g][live[g] >> SH == (C - 1) >> SH], np.array([C - 1])); x = top[rng.integers(0, len(top), sh)]
        if g > 4:
            low = rng.permutation(live[g][live[g] >> SH == 0]); n = rng.permutation(N * K); q = np.arange(N * K) // K; at = ro[g, 0] - q * G
            if g == 5: i = (n >= 256).astype(np.int64) + (n >= 768)
            elif g == 6: i = (n >= 1024).astype(np.int64)
            else: i = np.arange(N * K) % len(low)
            y = np.where(tr[:, g] >> SH == 0, x, tr[:, g]); y[q, :, at] = x[q, :, at]
            y[q, rng.integers(0, 16, N * K), at] = low[i]; tr[:, g] = y
            continue
        one = few[rng.integers(0, (1, 2, 4)[g % 3], (N, 1, G))]
        x = np.where(np.arange(16)[None, :, None] == rng.integers(0, 16, (N, 1, G)), one, x)
        tr[:, g] = np.where(rng.random((N, 1, G)) < (1.0 if g < 4 else 0.6), x, tr[:, g])
    return pack(tr, pa, s, ro)
def setup_inputs_block(rng):
    s, ro, w = batch(rng, [C - 1]); o = rng.permutation(8); f = int(o[4])
    if not np.any(s[f] == 0): s[f, int(rng.integers(0, N * K))] = 0
    for r in range(N):
        p = rng.permutation(G); v = (r - 1) % N
        ro[f, 0, r * K:(r + 1) * K] = r * G + p[:K]; ro[f, 1, v * K:(v + 1) * K] = r * G + p[K:2 * K]
    pa, live, dead = living(rng, s, ro, w, 0.05); tr = trunks(rng, s, ro, live, dead); sh = (N, 16, G); q = int(rng.integers(0, N))
    for h in range(5):
        g = int(o[h]); pa[g][:, C - 1] = ro[g][:, 0]
        top = np.union1d(live[g][live[g] >> SH == (C - 1) >> SH], np.array([C - 1])); d = np.setdiff1d(dead[g], np.array([C - 1]))
        full = top[rng.integers(0, len(top), sh)]; free = d[rng.integers(0, len(d), sh)]
        if h == 0: tr[:, g] = full
        if h == 1 or h == 2: tr[:, g] = free
        if h == 2: tr[q, g] = full[q]
        if h == 3: pa[g] = NONE
        if h == 4:
            a = np.arange(N * K) // K; b = (a + 1) % N; u = ro[g, 0] - a * G; v = ro[g, 1] - b * G; y = tr[:, g]
            y[a, rng.integers(0, 16, N * K), u] = d[rng.integers(0, len(d), N * K)]
            y[b, :, v] = full[b, :, v]; y[b[::4], rng.integers(0, 16, len(b[::4])), v[::4]] = s[g][::4]
    return pack(tr, pa, s, ro)
def setup_inputs_late(rng):
    s, ro, w = batch(rng); pa, live, dead = living(rng, s, ro, w, 0.05); tr = trunks(rng, s, ro, live, dead); sh = (N, 16, G)
    for g in range(8):
        tr[:, g] = np.where(rng.random(sh) < rng.choice(np.array([0.0, 0.5, 1.0]), (N, 1, G)), s[g][rng.integers(0, N * K, sh)], tr[:, g])
        u = np.argsort(s[g, :K])[:16]; v = K + np.argsort(s[g, K:2 * K])[-16:]
        y = tr[2, g]; y[:, ro[g, 1, v] - 2 * G] = s[g][u]
        for a, r, t in ((u, 0, 0), (v, 1, 0), (u, 0, 1)):
            y = tr[r + t, g]; y[:2, ro[g, t, a] - (r + t) * G] = dead[g][0]
        e = np.argsort(s[g, :K])[16:]; e = e[np.isin(ro[g, 1, e], ro[g, 0, K:2 * K], invert=True)]; lo, hi = e[:16], e[-16:]
        top = live[g][live[g] >> SH == (C - 1) >> SH]
        assert len(e) >= 32 and len(top) > 0 and np.all((s[g][lo] >> SH) < (s[g][hi] >> SH))
        assert np.all(np.any(pa[g][:, top] != NONE, axis=0)) and np.all(pa[g][:, dead[g][0]] == NONE)
        y = tr[0, g]; y[:2, ro[g, 0, np.append(lo, hi)]] = dead[g][0]
        y = tr[1, g]; y[:, ro[g, 1, lo] - G] = top[rng.integers(0, len(top), 16)]; y[:, ro[g, 1, hi] - G] = s[g][lo]
    return pack(tr, pa, s, ro)
def setup_inputs_spread(rng):
    s, ro, w = batch(rng); late = ro[:, RO:]; ro[:, RO:] = np.where(rng.random(late.shape) < 0.5, rng.integers(0, NONE, late.shape), late)
    pa, live, dead = living(rng, s, ro, w, 0.02); tr = trunks(rng, s, ro, live, dead)
    pa = np.where((pa != NONE) & (rng.random(pa.shape) < 0.5), np.minimum((NONE * rng.random(pa.shape) ** 4).astype(np.int64), NONE - 1), pa)
    x = np.minimum((C * rng.random(tr.shape) ** rng.choice(np.array([0.25, 1.0, 4.0]), (N, 8, 1, G))).astype(np.int64), C - 1)
    return pack(np.where(rng.random((N, 8, 1, G)) < 0.5, x, tr), pa, s, ro)
def check_inputs(d):
    bad = []
    for k, lo, hi in (("trunk", 0, C - 1), ("paths", 0, NONE), ("calls", 0, C - 1), ("routes", 0, NONE - 1)):
        if np.min(d[k]) < lo or np.max(d[k]) > hi: bad.append("range of " + k)
    if bad: return bad
    if np.any(d["paths"] != d["paths"][:1]): bad.append("paths alike on all ranks")
    s = np.concatenate([gentries(a) for a in d["calls"]], axis=1).astype(np.int64)
    if np.any(np.diff(np.sort(s, axis=1), axis=1) == 0): bad.append("calls of a group all different")
    if np.any(np.take_along_axis(d["paths"][0].reshape(8, 16, C), s[:, None, :], 2) != NONE): bad.append("paths of the seekers are none")
    own = (np.arange(N)[:, None] + np.arange(RO)[None, :]) % N
    at = d["routes"].astype(np.int64).reshape(N, 8, 16, K)[:, :, :RO] - own[:, None, :, None] * G
    if np.min(at) < 0 or np.max(at) > G - 1: bad.append("row t of routes names bundles of rank (r + t) mod N")
    if np.any(np.diff(np.sort(at, axis=3), axis=3) == 0): bad.append("row t of routes names different bundles")
    return bad
def reference(trunk, paths, calls, routes):
    tr = trunk.astype(np.int64).reshape(N, 8, 16, G); pa = paths[0].astype(np.int64).reshape(8, 16, C)
    sl = np.stack([gentries(a) for a in calls]).astype(np.int64); ro = routes.astype(np.int64).reshape(N, 8, 16, K)
    row = np.arange(16)[None, :, None]; D = C // N
    for t in range(RO):
        new = pa.copy(); gone = np.zeros((8, C), bool)
        for q in range(N):
            r = (q - t) % N; s = sl[r]; at = ro[r, :, t] - q * G
            hold = np.take_along_axis(tr[q], at[:, None, :], 2)
            hop = np.take_along_axis(pa, hold.reshape(8, 1, 16 * K), 2).reshape(8, 16, 16, K)
            dead = np.logical_not(np.any(hop != NONE, axis=1))
            like = np.add.reduce((hop == ro[r][:, :, None, :]).astype(np.int64), axis=1)
            may = (hold >> SH) < (s >> SH)[:, None, :]
            key = np.where(dead, 2 ** 22 + 15 - row, np.where(may, (like * C + C - 1 - hold) * 16 + 15 - row, -1))
            best = np.max(key, axis=1); p = 15 - (best & 15)
            go = np.any(np.take_along_axis(pa, s[:, None, :], 2) != NONE, axis=1) | (t == 0)
            won = go & (best >= 0); vic = np.take_along_axis(hold, p[:, None, :], 1)[:, 0]
            b, i = np.nonzero(won); tr[q, b, p[b, i], at[b, i]] = s[b, i]; new[b, t, s[b, i]] = ro[r, b, t, i]
            b, i = np.nonzero(won & (best < 2 ** 22)); gone[b, vic[b, i]] = True
            b, i = np.nonzero(go & (best < 0)); gone[b, s[b, i]] = True
        pa = np.where(gone[:, None, :], NONE, new)
    return {"yt": tr.reshape(N, 128, G).astype(np.float32), "yp": np.stack([pa[:, :, r * D:(r + 1) * D].reshape(128, D) for r in range(N)]).astype(np.float32)}

@@ -1,0 +1,523 @@
+import math
+import numpy as np
+from concourse.bass import DstId, RemoteDMATransfer
+from concourse.mybir import AluOpType as A, ActivationFunctionType as F
+
+N, RO, K = 4, 6, 256
+CUT = 72
+SHARE = (5, 4)
+LN2 = math.log(2.0)
+ROUTE, SX, SXB, AT, CL, SLO, SELF, P2S, PKW = 0, 256, 512, 768, 864, 880, 896, 912, 928
+
+SCRATCH = {
+    "ptab": ("sbuf", [128, 4096], "int32"), "tin": ("sbuf", [128, 1024], "int32"), "ttab": ("sbuf", [128, 1024], "float32"),
+    "cin": ("sbuf", [128, 16], "int32"), "rin": ("sbuf", [128, 256], "int32"),
+    "pk0": ("sbuf", [128, PKW], "float32"), "pk1": ("sbuf", [128, PKW], "float32"),
+    "pk2": ("sbuf", [128, PKW], "float32"), "pk3": ("sbuf", [128, PKW], "float32"),
+    "ls0": ("sbuf", [128, 128], "uint16"), "ls1": ("sbuf", [128, 128], "uint16"),
+    "ls2": ("sbuf", [128, 128], "uint16"), "ls3": ("sbuf", [128, 128], "uint16"),
+    "re0": ("sbuf", [128, 4096], "float32"), "re1": ("sbuf", [128, 4096], "float32"),
+    "re2": ("sbuf", [128, 4096], "float32"), "re3": ("sbuf", [128, 4096], "float32"),
+    "nn": ("sbuf", [128, 4096], "bfloat16"), "eq": ("sbuf", [128, 4096], "bfloat16"), "al": ("sbuf", [128, 4096], "bfloat16"),
+    "als": ("sbuf", [128, 256], "bfloat16"), "tb": ("sbuf", [128, 256], "bfloat16"), "tq": ("sbuf", [128, 256], "bfloat16"),
+    "hb": ("sbuf", [128, RO * 256], "bfloat16"), "lh": ("sbuf", [128, RO * N * 256], "bfloat16"),
+    "ones": ("sbuf", [128, 512], "bfloat16"), "onef": ("sbuf", [128, 512], "float32"), "rb": ("sbuf", [128, 2048], "bfloat16"),
+    "i16": ("sbuf", [128, 16], "bfloat16"), "rm": ("sbuf", [128, 16], "float32"),
+    "idb": ("sbuf", [128, 128], "bfloat16"), "idf": ("sbuf", [128, 128], "float32"), "idq": ("sbuf", [128, 128], "bfloat16"),
+    "idn": ("sbuf", [128, 128], "float32"), "idp": ("sbuf", [128, 128], "float32"), "idm": ("sbuf", [128, 128], "bfloat16"),
+    "bda": ("sbuf", [128, 128], "bfloat16"), "bd": ("sbuf", [128, 128], "bfloat16"),
+    "wa": ("sbuf", [128, 144], "bfloat16"), "wb": ("sbuf", [128, 144], "bfloat16"), "wc": ("sbuf", [128, 144], "bfloat16"),
+    "mw": ("sbuf", [128, 8], "bfloat16"), "ml": ("sbuf", [128, 8], "bfloat16"), "ma": ("sbuf", [128, 512], "bfloat16"),
+    "ex": ("sbuf", [128, 256], "bfloat16"), "prm": ("sbuf", [128, 512], "float32"), "prn": ("sbuf", [128, 512], "float32"),
+    "ch": ("sbuf", [128, 224], "bfloat16"), "clo": ("sbuf", [128, 128], "bfloat16"), "zz": ("sbuf", [128, 256], "bfloat16"),
+    "cra": ("sbuf", [128, 128], "bfloat16"), "crb": ("sbuf", [128, 128], "bfloat16"), "cr": ("sbuf", [128, 128], "bfloat16"),
+    "pfa": ("sbuf", [128, 128], "float32"), "pfac": ("sbuf", [128, 144], "float32"),
+    "rwi": ("sbuf", [128, 8], "int32"), "col": ("sbuf", [128, 64], "float32"), "pwb": ("sbuf", [128, 8], "bfloat16"),
+    "ci": ("sbuf", [128, 96], "int32"), "cb": ("sbuf", [128, 96], "bfloat16"), "tr": ("sbuf", [128, 256], "float32"),
+    "ati": ("sbuf", [128, 192], "int32"), "hf": ("sbuf", [128, 256], "float32"),
+    "lf": ("sbuf", [128, 256], "uint16"), "ll": ("sbuf", [128, 256], "uint16"), "h2": ("sbuf", [128, 256], "bfloat16"),
+    "nm": ("sbuf", [128, 256], "bfloat16"), "p2": ("sbuf", [128, 272], "bfloat16"), "ab": ("sbuf", [128, 1024], "bfloat16"),
+    "y": ("sbuf", [128, 272], "int32"), "ya": ("sbuf", [128, 272], "int32"), "dd": ("sbuf", [128, 272], "float32"),
+    "kk": ("sbuf", [128, 272], "float32"), "m1": ("sbuf", [128, 128], "float32"), "m2": ("sbuf", [128, 64], "float32"),
+    "m3": ("sbuf", [128, 32], "float32"), "m4": ("sbuf", [128, 16], "float32"), "bi": ("sbuf", [128, 16], "int32"),
+    "hl": ("sbuf", [128, 32], "int32"), "hlf": ("sbuf", [128, 32], "float32"), "si": ("sbuf", [128, 16], "int32"),
+    "oh": ("sbuf", [128, 2048], "bfloat16"), "ol": ("sbuf", [128, 2048], "bfloat16"),
+    "cdi": ("sbuf", [128, 16], "int32"), "cdb": ("sbuf", [128, 16], "bfloat16"), "ct": ("sbuf", [128, 128], "bfloat16"),
+    "t1": ("sbuf", [128, 256], "float32"), "t2": ("sbuf", [128, 256], "float32"),
+    "val": ("sbuf", [128, 1024], "float32"), "out": ("sbuf", [128, 1024], "float32"),
+    "key0": ("psum", [128, 512], "float32"), "key1": ("psum", [128, 512], "float32"),
+    "wd0": ("psum", [128, 512], "float32"), "wd1": ("psum", [128, 512], "float32"),
+    "his": ("psum", [128, 512], "float32"), "tm": ("psum", [128, 512], "float32"),
+    "ms": ("psum", [128, 512], "float32"), "mt": ("psum", [128, 512], "float32"),
+}
+PSUM = [k for k in SCRATCH if SCRATCH[k][0] == "psum"]
+SEMAPHORES = (["cv", "cs", "ct", "cg", "sent"] + ["d%d" % i for i in range(16)] + ["k%d" % r for r in range(N)]
+              + ["p%d" % r for r in range(N)] + ["h%d_%d" % (t, r) for t in range(RO) for r in range(N)])
+
+
+def scheduler(g, T):
+    queues = {"v": g.vector, "s": g.scalar, "t": g.tensor, "g": g, "y": g.sync}
+    count, seen, snap, log, dmas = {}, {k: {} for k in queues}, {}, {}, [0]
+
+    def wait(qn, need):
+        for s, n in need.items():
+            if seen[qn].get(s, 0) >= n: continue
+            queues[qn].wait_ge(T.sem[s], n)
+            known = dict(snap.get((s, n), {})); known[s] = n
+            for a, b in known.items():
+                if seen[qn].get(a, 0) < b: seen[qn][a] = b
+
+    def needs(reads, writes):
+        need = {}
+        reads, writes = list(reads), list(writes)
+        writes += [r for r in reads if r[0] in PSUM]
+        span = [(w[0], 0, 512) if w[0] in PSUM else w for w in writes]
+        for acc, wr in [(r, False) for r in reads if r[0] not in PSUM] + [(w, True) for w in span]:
+            for lo, hi, w, s, n in log.get(acc[0], []):
+                if lo < acc[2] and acc[1] < hi and (w or wr): need[s] = max(need.get(s, 0), n)
+        return need, [r for r in reads if r[0] not in PSUM], span
+
+    def record(reads, writes, s, n):
+        for b, lo, hi in writes:
+            log[b] = [e for e in log.get(b, []) if not (lo <= e[0] and e[1] <= hi)] + [(lo, hi, True, s, n)]
+        for b, lo, hi in reads:
+            log[b] = [e for e in log.get(b, []) if e[2] or e[3] != s or not (lo <= e[0] and e[1] <= hi)] + [(lo, hi, False, s, n)]
+
+    def op(qn, reads, writes, *fns):
+        need, rd, wr = needs(reads, writes)
+        wait(qn, need)
+        for f in fns: ins = f()
+        s = "c" + qn
+        count[s] = count.get(s, 0) + 1
+        ins.then_inc(T.sem[s], 1)
+        snap[(s, count[s])] = dict(seen[qn])
+        record(rd, wr, s, count[s])
+
+    def dma(qn, reads, writes, out, in_):
+        need, rd, wr = needs(reads, writes)
+        wait(qn, need)
+        s = "d%d" % dmas[0]
+        dmas[0] += 1
+        queues[qn].dma_start(out, in_).then_inc(T.sem[s], 16)
+        count[s] = 16
+        snap[(s, 16)] = dict(seen[qn])
+        record(rd, wr, s, 16)
+
+    def arrives(writes, s, n):
+        count[s] = n
+        record([], writes, s, n)
+
+    def send(reads, f):
+        wait("g", needs(reads, [])[0])
+        f()
+
+    def finish():
+        wait("g", count)
+    return op, dma, arrives, send, finish
+
+
+def rank_program(g, core, T, topo):
+    q = T.rank_of(core)
+    if q is None: return
+    op, dma, arrives, send, finish = scheduler(g, T)
+    V, S, P = g.vector, g.scalar, g.tensor
+    pk = [T["pk%d" % r] for r in range(N)]
+    ls = [T["ls%d" % r] for r in range(N)]
+    rx = [T["re%d" % r] for r in range(N)]
+    key, wd = [T.key0, T.key1], [T.wd0, T.wd1]
+    mm = P.matmul
+    own = pk[q]
+    po = "pk%d" % q
+
+    def vop(reads, writes, f): op("v", reads, writes, f)
+
+    def sop(reads, writes, f): op("s", reads, writes, f)
+
+    def ways(c):
+        w, used, plan = {}, set(), []
+        for d in T.cores:
+            if d != c: w.setdefault(tuple(topo.engines(c, d)), []).append(d)
+        for es in sorted(w, key=len):
+            e = [x for x in es if x not in used]
+            e = e[:1 << (len(e).bit_length() - 1)]
+            used |= set(e)
+            plan.append((e, w[es]))
+        return plan
+    plan = ways(core)
+    near = {r: [len(e) for e, ds in ways(T.cores[r]) if core in ds][0] for r in range(N) if r != q}
+    sent = [0]
+
+    def broadcast(src, dst, sem):
+        trs = [RemoteDMATransfer(dst_ids=[DstId(rid=topo.addr(d)[0], pnc=topo.addr(d)[1]) for d in ds],
+                                 dma_engine_mask=sum(1 << x for x in e), remote_sem=T.sem[sem],
+                                 srcs=[src], dsts=[dst] * len(ds)) for e, ds in plan]
+        sent[0] += sum(len(e) for e, ds in plan)
+        return lambda: g.remote_dma_fused(trs, local_sem=T.sem.sent)
+
+    def tell(a, b, sem):
+        send([(po, a, b)], broadcast(own[:, a:b], own[:, a:b], "%s%d" % (sem, q)))
+        for r in near: arrives([("pk%d" % r, a, b)], "%s%d" % (sem, r), near[r])
+
+    dma("y", [], [("cin", 0, 16)], T.cin[:], T.calls[:])
+    dma("y", [], [("rin", 0, 256)], T.rin[:], T.routes[:])
+    dma("y", [], [("tin", 0, 1024)], T.tin[:], T.trunk[:])
+    for c in range(4):
+        dma("y", [], [("ptab", 1024 * c, 1024 * c + 1024)], T.ptab[:, 1024 * c:1024 * c + 1024], T.paths[:, 1024 * c:1024 * c + 1024])
+
+    def select(dst, w, src, pattern, cmp, fill, base, cm, lo=0):
+        op("g", [(src, lo, lo + w)], [(dst, lo, lo + w)],
+           lambda: g.affine_select(T[dst][:, lo:lo + w], T[src][:, lo:lo + w], pattern, cmp, fill, base, cm))
+
+    def iota(dst, w, pattern, base, cm):
+        op("g", [], [(dst, 0, w)], lambda: g.iota(T[dst][:, 0:w], pattern, base, cm, allow_small_or_imprecise_dtypes=True))
+    COL = {15 * LN2: 8, 144 * LN2: 16, 32896.5: 32, 1.0: 40}
+
+    def cc(x): return T.col[:, COL[x]:COL[x] + 1]
+
+    def cn(x): return ("col", COL[x], COL[x] + 1)
+    vop([], [("ones", 0, 512)], lambda: V.memset(T.ones[:], 1.0))
+    vop([], [("onef", 0, 512)], lambda: V.memset(T.onef[:], 1.0))
+    iota("rwi", 1, [[0, 1]], 0, 1)
+    iota("i16", 16, [[1, 16]], 0, 0)
+    select("bda", 128, "ones", [[-16, 8], [0, 16]], A.is_ge, 0.0, 0, 1)
+    select("bd", 128, "bda", [[16, 8], [0, 16]], A.is_ge, 0.0, 15, -1)
+    select("idf", 128, "onef", [[-1, 128]], A.is_equal, 0.0, 0, 1)
+    select("prm", 512, "onef", [[-16, 2], [16, 2], [-1, 128]], A.is_equal, 0.0, 0, 1)
+    for b in range(4):
+        select("prn", 128, "prm", [[0, 4], [1, 2], [0, 16]], A.is_equal, 0.0, -(b % 2), 0, 128 * b)
+    iota("ch", 224, [[-1, 224]], 127, 0)
+    iota("clo", 128, [[-1, 128]], 127, 0)
+    select("idb", 128, "ones", [[-1, 128]], A.is_equal, 0.0, 0, 1)
+    vop([], [("zz", 0, 256)], lambda: V.memset(T.zz[:], 0.0))
+    for x in COL: vop([], [cn(x)], lambda: V.memset(cc(x), x))
+    vop([], [("pfac", 0, 16)], lambda: V.memset(T.pfac[:, 0:16], (8388608.0 + 16) / 32768))
+
+    ci, cb, ati = T.ci, T.cb, T.ati
+    vop([("rwi", 0, 1)], [("rwi", 4, 5)], lambda: V.tensor_scalar(T.rwi[:, 4:5], T.rwi[:, 0:1], 15, None, A.bitwise_and))
+    vop([("rwi", 4, 5)], [("col", 0, 1)], lambda: V.tensor_copy(T.col[:, 0:1], T.rwi[:, 4:5]))
+    sop([("col", 0, 1)], [("pwb", 0, 1)], lambda: S.activation(T.pwb[:, 0:1], T.col[:, 0:1], F.Exp, scale=LN2))
+    vop([("i16", 0, 16), ("col", 0, 1)], [("rm", 0, 16)], lambda: V.tensor_scalar(T.rm[:], T.i16[:], T.col[:, 0:1], None, A.is_equal))
+    for x in range(16):
+        vop([("bd", 0, 128), ("rm", 0, 16)], [("rb", 128 * x, 128 * x + 128)],
+            lambda: V.tensor_scalar(T.rb[:, 128 * x:128 * x + 128], T.bd[:], T.rm[:, x:x + 1], None, A.mult))
+    for i, m in ((0, 255), (1, 3840), (2, 3072)):
+        vop([("cin", 0, 16)], [("ci", 16 * i, 16 * i + 16)], lambda: V.tensor_scalar(ci[:, 16 * i:16 * i + 16], T.cin[:], m, None, A.bitwise_and))
+    vop([("ci", 0, 48)], [("cb", 0, 48)], lambda: V.tensor_copy(cb[:, 0:48], ci[:, 0:48]))
+    vop([("rin", 0, 256)], [(po, 0, 256)], lambda: V.tensor_copy(own[:, 0:256], T.rin[:]))
+    vop([(po, 0, 256)], [("tr", 0, 256)], lambda: V.transpose(T.tr[:], own[:, 0:256]))
+    tell(ROUTE, SX, "k")
+    select("wa", 144, "ones", [[0, 9], [1, 16]], A.is_equal, 0.0, -15, 0)
+    select("wb", 144, "wa", [[-16, 9], [0, 16]], A.is_ge, 0.0, 0, 1)
+    select("wc", 144, "wb", [[16, 9], [0, 16]], A.is_ge, 0.0, 15, -1)
+    iota("cra", 128, [[0, 8], [-1, 16]], -17, 0)
+    select("crb", 128, "cra", [[0, 128]], A.is_equal, 0.0, -1, 1)
+    select("cr", 128, "crb", [[0, 128]], A.not_equal, 262144.0, 0, 1)
+    iota("pfa", 128, [[0, 8], [-1, 16]], 4194304 + 15, 0)
+    select("ma", 512, "ones", [[128, 2], [-1, 2], [-2, 128]], A.is_equal, 0.0, 0, 1)
+    select("ex", 256, "ones", [[-1, 16], [0, 16]], A.is_equal, 0.0, 0, 1)
+
+    def expand(r, lo, hi):
+        for p in range(lo, hi):
+            sop([("pk%d" % r, 0, 256)], [("re%d" % r, 256 * p, 256 * p + 256)],
+                lambda: S.activation(rx[r][:, p::16], pk[r][:, 0:256], F.Copy))
+    expand(q, 0, 16)
+    op("t", [("cb", 0, 32), ("rb", 0, 2048)], [("ms", 0, 512)],
+       *[(lambda x=x, h=h: mm(T.ms[:, x:256:16], T.rb[:, 128 * x:128 * x + 128], cb[:, 16 * h:16 * h + 16], h == 0, h == 1))
+         for x in range(16) for h in range(2)])
+    vop([("ms", 0, 512)], [(po, SX, SX + 256)], lambda: V.tensor_copy(own[:, SX:SX + 256], T.ms[:, 0:256]))
+    op("t", [(po, SX, SX + 256), ("idf", 0, 128)], [("wd1", 0, 512)],
+       *[(lambda h=h: mm(T.wd1[:, 8 * h:8 * h + 8], own[:, SX + 128 * h:SX + 128 * h + 128], T.idf[:, 0::16], True, True)) for h in range(2)])
+
+    def opened(bank, bname, ts):
+        op("t", [("tr", 0, 256), ("prn", 0, 512)], [(bname, 0, 512)],
+           *[(lambda t=t, y=y, b=b: mm(bank[:, 16 * t + y:16 * t + 16:2], T.prn[:, 256 * y + 128 * b:256 * y + 128 * b + 128],
+                                       T.tr[:, 16 * b + t::32], b == 0, b == 1)) for t in ts for y in range(2) for b in range(2)])
+
+    def opened_lists(bank, bname, ts):
+        a, b = 16 * ts[0], 16 * ts[-1] + 16
+        vop([(bname, 0, 512)], [("ati", a, b)], lambda: V.tensor_copy(ati[:, a:b], bank[:, a:b]))
+        vop([("ati", a, b)], [("ati", 96 + a, 96 + b)], lambda: V.tensor_scalar(ati[:, 96 + a:96 + b], ati[:, a:b], 1023, None, A.bitwise_and))
+        vop([("ati", 96 + a, 96 + b)], [("ls%d" % q, a, b)], lambda: V.tensor_copy(ls[q][:, a:b], ati[:, 96 + a:96 + b]))
+    opened(T.wd0, "wd0", [0])
+    opened_lists(T.wd0, "wd0", [0])
+    op("t", [("cb", 32, 48), ("rb", 0, 2048)], [("mt", 0, 512)],
+       *[(lambda x=x: mm(T.mt[:, x:256:16], T.rb[:, 128 * x:128 * x + 128], cb[:, 32:48], True, True)) for x in range(16)])
+    opened(T.tm, "tm", [1, 2, 3, 4, 5])
+    vop([("mt", 0, 512)], [(po, SXB, SXB + 256)], lambda: V.tensor_copy(own[:, SXB:SXB + 256], T.mt[:, 0:256]))
+    vop([("wd1", 0, 512)], [(po, SELF, SELF + 16)], lambda: V.tensor_scalar(own[:, SELF:SELF + 16], T.wd1[:, 0:16], -32.0, 4095.0 * 32 + 16, A.mult, A.add))
+    vop([("wd1", 0, 512)], [("ci", 48, 64)], lambda: V.tensor_copy(ci[:, 48:64], T.wd1[:, 0:16]))
+    vop([("ci", 48, 64)], [("ci", 64, 80)], lambda: V.tensor_scalar(ci[:, 64:80], ci[:, 48:64], 3840, None, A.bitwise_and))
+    vop([("ci", 64, 80)], [("cb", 48, 64)], lambda: V.tensor_copy(cb[:, 48:64], ci[:, 64:80]))
+    sop([("cb", 48, 64), cn(15 * LN2)], [("cb", 64, 80)], lambda: S.activation(cb[:, 64:80], cb[:, 48:64], F.Exp, bias=cc(15 * LN2), scale=-LN2 / 256))
+    sop([("cb", 64, 80)], [(po, P2S, P2S + 16)], lambda: S.activation(own[:, P2S:P2S + 16], cb[:, 64:80], F.Copy))
+
+    def lists(r):
+        vop([("pk%d" % r, AT, SELF)], [("ls%d" % r, 0, 128)], lambda: V.tensor_copy(ls[r][:], pk[r][:, AT:SELF]))
+
+    def package():
+        opened_lists(T.tm, "tm", [1, 2, 3, 4, 5])
+        vop([("ati", 96, 192)], [(po, AT, AT + 96)], lambda: V.tensor_copy(own[:, AT:AT + 96], ati[:, 96:192]))
+        vop([("cin", 0, 16)], [(po, CL, CL + 16)], lambda: V.tensor_copy(own[:, CL:CL + 16], T.cin[:]))
+        vop([("ci", 0, 16)], [(po, SLO, SLO + 16)], lambda: V.tensor_copy(own[:, SLO:SLO + 16], ci[:, 0:16]))
+        vop([(po, CL, SELF)], [("ls%d" % q, 96, 128)], lambda: V.tensor_copy(ls[q][:, 96:128], own[:, CL:SELF]))
+        tell(SX, PKW, "p")
+    vop([("tin", 0, 1024)], [("ttab", 0, 1024)], lambda: V.tensor_copy(T.ttab[:], T.tin[:]))
+    vop([("idf", 0, 128)], [("idn", 0, 128)], lambda: V.tensor_scalar(T.idn[:], T.idf[:], -32.0, None, A.mult))
+    vop([("idf", 0, 128)], [("idp", 0, 128)], lambda: V.tensor_scalar(T.idp[:], T.idf[:], -1.0, None, A.mult))
+    vop([("idb", 0, 128)], [("idq", 0, 128)], lambda: V.tensor_scalar(T.idq[:], T.idb[:], -1.0, None, A.mult))
+    vop([("idb", 0, 128)], [("idm", 0, 128)], lambda: V.tensor_scalar(T.idm[:], T.idb[:], -4194304.0, None, A.mult))
+    vop([("bd", 0, 128), ("pwb", 0, 1)], [("mw", 0, 8)], lambda: V.tensor_scalar(T.mw[:], T.bd[:, 0::16], T.pwb[:, 0:1], None, A.mult))
+    vop([("bd", 0, 128)], [("ml", 0, 8)], lambda: V.tensor_scalar(T.ml[:], T.bd[:, 0::16], 131072.0, None, A.mult))
+    vop([("pfa", 0, 128)], [("pfac", 16, 144)], lambda: V.tensor_scalar(T.pfac[:, 16:144], T.pfa[:], 1.0 / 32768, None, A.mult))
+    vop([("pfac", 0, 144)], [("mt", 0, 512)], lambda: V.tensor_copy(T.mt[:, 256:400], T.pfac[:]))
+    vop([("col", 0, 1)], [("col", 1, 2)], lambda: V.tensor_scalar(T.col[:, 1:2], T.col[:, 0:1], -1.0, 15.0, A.mult, A.add))
+    vop([("col", 0, 1)], [("col", 2, 3)], lambda: V.tensor_scalar(T.col[:, 2:3], T.col[:, 0:1], 6.0, None, A.is_lt))
+    vop([("col", 0, 1)], [("col", 3, 4)], lambda: V.tensor_scalar(T.col[:, 3:4], T.col[:, 0:1], 6.0, 4096.0, A.is_ge, A.mult))
+
+    def clear_hist():
+        op("t", [("ones", 0, 128), ("zz", 0, 256)], [("his", 0, 512)], lambda: mm(T.his[:, 0:256], T.ones[:, 0:128], T.zz[:], True, False))
+
+    def histogram(half, bname, buf, sign, last, share):
+        o = 16 * half
+        vop([(bname, 8 * half, 8 * half + 8)], [("hl", o, o + 8)],
+            lambda: V.tensor_scalar(T.hl[:, o:o + 8], buf[:, 8 * half:8 * half + 8], 12, 0xC1F, A.logical_shift_right, A.bitwise_and))
+        vop([(bname, 8 * half, 8 * half + 8)], [("hl", o + 8, o + 16)],
+            lambda: V.tensor_scalar(T.hl[:, o + 8:o + 16], buf[:, 8 * half:8 * half + 8], 5, 127, A.logical_shift_right, A.bitwise_and))
+        vop([("hl", o, o + 16)], [("hlf", o, o + 16)], lambda: V.tensor_copy(T.hlf[:, o:o + 16], T.hl[:, o:o + 16]))
+        a = 512 * half
+        for n in range(share, 8):
+            d = a + 128 * (n - share)
+            sop([("clo", 0, 128), ("hlf", o, o + 16)], [("ab", d, d + 128)],
+                lambda: S.activation(T.ab[:, d:d + 128], T.clo[:], F.Abs, bias=T.hlf[:, o + 8 + n:o + 9 + n], scale=-1.0))
+        if share < 8:
+            d, w = 1024 * half + 1024, 128 * (8 - share)
+            sop([("ab", a, a + w), cn(1.0)], [("ol", d - w, d)],
+                lambda: S.activation(T.ol[:, d - w:d], T.ab[:, a:a + w], F.Relu, bias=cc(1.0), scale=-1.0))
+        for n in range(8):
+            c = 128 * (8 * half + n)
+            k = 96 - 32 * (n % 4)
+            if sign > 0:
+                vop([("ch", 0, 224), ("hlf", o, o + 16)], [("oh", c, c + 128)],
+                    lambda: V.tensor_scalar(T.oh[:, c:c + 128], T.ch[:, k:k + 128], T.hlf[:, o + n:o + n + 1], None, A.is_equal))
+            else:
+                vop([("ch", 0, 224), ("hlf", o, o + 16)], [("oh", c, c + 128)],
+                    lambda: V.tensor_scalar(T.oh[:, c:c + 128], T.ch[:, k:k + 128], T.hlf[:, o + n:o + n + 1], -1.0, A.is_equal, A.mult))
+            if n < share:
+                vop([("clo", 0, 128), ("hlf", o, o + 16)], [("ol", c, c + 128)],
+                    lambda: V.tensor_scalar(T.ol[:, c:c + 128], T.clo[:], T.hlf[:, o + 8 + n:o + 9 + n], None, A.is_equal))
+        for n in range(8):
+            c, j = 128 * (8 * half + n), 128 * (n // 4)
+            op("t", [("oh", c, c + 128), ("ol", c, c + 128)], [("his", 0, 512)],
+               lambda: mm(T.his[:, j:j + 128], T.oh[:, c:c + 128], T.ol[:, c:c + 128], False, last and n == 7))
+
+    def fetch(t):
+        r = (q - t) % N
+        at = ls[r][:, 16 * t:16 * t + 16]
+        lsn = ("ls%d" % r, 0, 128)
+        vop([("ttab", 0, 1024), lsn], [("lf", 0, 256)], lambda: V.tensor_copy(T.lf[:], T.ttab[:].indirect(at)))
+        sop([("ttab", 0, 1024), lsn], [("hf", 0, 256)], lambda: S.activation(T.hf[:], T.ttab[:].indirect(at), F.Copy))
+
+    def parts(t):
+        pr = "pk%d" % ((q - t) % N)
+        ps = pk[(q - t) % N][:, P2S:P2S + 16]
+        sop([("hf", 0, 256), cn(32896.5)], [("h2", 0, 256)], lambda: S.activation(T.h2[:], T.hf[:], F.Identity, bias=cc(32896.5)))
+        op("t", [("h2", 0, 256), ("idb", 0, 128)], [("ms", 0, 512)],
+           *[(lambda h=h: mm(T.ms[:, 128 * h:128 * h + 128], T.h2[:, 128 * h:128 * h + 128], T.idb[:], True, True)) for h in range(2)])
+        op("t", [("hf", 0, 256), ("h2", 0, 256), ("idf", 0, 128), ("idq", 0, 128)], [("ms", 0, 512)],
+           lambda: mm(T.ms[:, 256:512], T.idf[:], T.hf[:], True, False),
+           lambda: mm(T.ms[:, 256:512], T.idq[:], T.h2[:], False, True))
+        sop([("ms", 0, 512), cn(144 * LN2)], [("p2", 16, 272)], lambda: S.activation(T.p2[:, 16:272], T.ms[:, 0:256], F.Exp, bias=cc(144 * LN2), scale=-LN2 / 256))
+        if t > 0: sop([(pr, P2S, P2S + 16)], [("p2", 0, 16)], lambda: S.activation(T.p2[:, 0:16], ps, F.Copy))
+
+    def low_list():
+        vop([("ms", 0, 512)], [("ll", 0, 256)], lambda: V.tensor_scalar(T.ll[:], T.ms[:, 256:512], 33024.0, None, A.add))
+
+    def classes(t):
+        pr = "pk%d" % ((q - t) % N)
+        sb = pk[(q - t) % N][:, SXB:SXB + 256]
+        vop([("hf", 0, 256), (pr, SXB, SXB + 256)], [("nm", 0, 256)], lambda: V.tensor_tensor(T.nm[:], T.hf[:], sb, A.is_ge))
+
+    def key_base(t, h):
+        pr = "pk%d" % ((q - t) % N)
+        se = pk[(q - t) % N][:, SELF:SELF + 16]
+        if t > 0 and h == 0: op("t", [(pr, SELF, SELF + 16), ("idf", 0, 128)], [("key0", 0, 512)], lambda: mm(T.key0[:, 0:16], T.idf[:], se, True, True))
+        c = 128 * h
+        k = key[h][:, 16 - 16 * h:144 - 16 * h]
+        op("t", [("ones", 0, 128), ("cr", 0, 128), ("hf", c, c + 128), ("idn", 0, 128), ("nm", c, c + 128), ("idm", 0, 128)], [("key%d" % h, 0, 512)],
+           lambda: mm(k, T.ones[:, 0:128], T.cr[:], True, False),
+           lambda: mm(k, T.hf[:, c:c + 128], T.idn[:], False, False),
+           lambda: mm(k, T.nm[:, c:c + 128], T.idm[:], False, False))
+
+    def difference(t):
+        pr = "pk%d" % ((q - t) % N)
+        sx = pk[(q - t) % N][:, SX:SX + 256]
+        op("t", [("idf", 0, 128), (pr, SX, SX + 256), ("idp", 0, 128), ("hf", 0, 256)], [("ms", 0, 512)],
+           lambda: mm(T.ms[:, 256:512], T.idf[:], sx, True, False),
+           lambda: mm(T.ms[:, 256:512], T.idp[:], T.hf[:], False, True))
+
+    def like(t, h):
+        r = (q - t) % N
+        c = 2048 * h
+        vop([("ptab", 0, 4096), ("lf", 0, 256), ("re%d" % r, 0, 4096)], [("eq", c, c + 2048)],
+            lambda: V.tensor_tensor(T.eq[:, c:c + 2048], T.ptab[:].indirect(T.lf[:, 128 * h:128 * h + 128]), rx[r][:, c:c + 2048], A.is_equal))
+
+    def like_sum(h):
+        c = 2048 * h
+        op("t", [("eq", c, c + 2048), ("ml", 0, 8)], [("key%d" % h, 0, 512)],
+           *[(lambda p=p: mm(key[h][:, 16 - 16 * h + p:144 - 16 * h:16], T.eq[:, c + p:c + 2048:16], T.ml[:], False, p == 15)) for p in range(16)])
+
+    def dead(a, b):
+        sop([("tb", 0, 256), ("ll", 0, 256)], [("al", 16 * a, 16 * b)],
+            lambda: S.activation(T.al[:, 16 * a:16 * b], T.tb[:].indirect(T.ll[:, a:b]), F.Sign))
+
+    def dead_too(a, b):
+        vop([("tb", 0, 256), ("ll", 0, 256)], [("al", 16 * a, 16 * b)],
+            lambda: V.tensor_scalar(T.al[:, 16 * a:16 * b], T.tb[:].indirect(T.ll[:, a:b]), 0.0, None, A.is_gt))
+
+    def words(h):
+        c = 2048 * h
+        op("t", [("al", c, c + 2048), ("mw", 0, 8)], [("wd%d" % h, 0, 512)],
+           *[(lambda p=p: mm(wd[h][:, 16 - 16 * h + p:144 - 16 * h:16], T.al[:, c + p:c + 2048:16], T.mw[:], True, True)) for p in range(16)])
+
+    def dead_seekers(t):
+        r = (q - t) % N
+        vop([("tb", 0, 256), ("ls%d" % r, 0, 128)], [("als", 0, 256)],
+            lambda: V.tensor_scalar(T.als[:], T.tb[:].indirect(ls[r][:, SLO - AT:SLO - AT + 16]), 0.0, None, A.is_gt))
+
+    def seeker_words():
+        op("t", [("als", 0, 256), ("mw", 0, 8)], [("wd0", 0, 512)],
+           *[(lambda h=h: mm(T.wd0[:, 8 * h:8 * h + 8], T.als[:, 128 * h:128 * h + 128], T.mw[:], True, True)) for h in range(2)])
+
+    def decide(t, h):
+        a = 0 if h == 0 and t > 0 else 16
+        e0, e1 = (a, 144) if h == 0 else (144, 272)
+        f0, f1 = (a, 144) if h == 0 else (0, 128)
+        pf = T.mt[:, 256 + a:400] if h == 0 else T.mt[:, 272:400]
+        if h == 0 and t == 0: vop([(po, SELF, SELF + 16)], [("kk", 0, 16)], lambda: V.tensor_copy(T.kk[:, 0:16], own[:, SELF:SELF + 16]))
+        vop([("wd%d" % h, 0, 512), ("p2", e0, e1)], [("y", e0, e1)], lambda: V.tensor_tensor(T.y[:, e0:e1], wd[h][:, f0:f1], T.p2[:, e0:e1], A.mult))
+        vop([("y", e0, e1)], [("ya", e0, e1)], lambda: V.tensor_scalar(T.ya[:, e0:e1], T.y[:, e0:e1], 32768, None, A.bitwise_and))
+        vop([("ya", e0, e1), ("mt", 0, 512)], [("dd", e0, e1)], lambda: V.tensor_tensor(T.dd[:, e0:e1], pf, T.ya[:, e0:e1], A.mult))
+        vop([("key%d" % h, 0, 512), ("dd", e0, e1)], [("kk", e0, e1)], lambda: V.tensor_tensor(T.kk[:, e0:e1], key[h][:, f0:f1], T.dd[:, e0:e1], A.max))
+        src, w, off = "kk", 128, 16
+        for dst in ("m1", "m2", "m3", "m4"):
+            a, b, d = off + h * w, off + h * w + w, h * w // 2
+            vop([(src, a, b)], [(dst, d, d + w // 2)],
+                lambda: V.tensor_tensor(T[dst][:, d:d + w // 2], T[src][:, a:b:2], T[src][:, a + 1:b:2], A.max))
+            src, w, off = dst, w // 2, 0
+        a = 8 * h
+        vop([("m4", a, a + 8), ("kk", a, a + 8)], [("bi", a, a + 8)], lambda: V.tensor_tensor(T.bi[:, a:a + 8], T.m4[:, a:a + 8], T.kk[:, a:a + 8], A.max))
+
+    def codes():
+        vop([("bi", 0, 16)], [("cdi", 0, 16)], lambda: V.tensor_scalar(T.cdi[:], T.bi[:], 31, None, A.bitwise_and))
+        vop([("cdi", 0, 16)], [("cdb", 0, 16)], lambda: V.tensor_copy(T.cdb[:], T.cdi[:]))
+        op("t", [("cdb", 0, 16), ("idb", 0, 128)], [("ms", 0, 512)], lambda: mm(T.ms[0:16, 0:128], T.cdb[:], T.idb[:], True, True))
+        sop([("ms", 0, 512)], [("ct", 0, 128)], lambda: S.activation(T.ct[0:16, :], T.ms[0:16, 0:128], F.Copy))
+        op("t", [("ct", 0, 128), ("ex", 0, 256)], [("mt", 0, 512)],
+           *[(lambda h=h: mm(T.mt[:, 128 * h:128 * h + 128], T.ex[0:16, 128 * h:128 * h + 128], T.ct[0:16, :], True, True)) for h in range(2)])
+
+    def update(t):
+        r = (q - t) % N
+        vop([("mt", 0, 512), ("col", 1, 2)], [("t1", 0, 256)], lambda: V.tensor_scalar(T.t1[:], T.mt[:, 0:256], T.col[:, 1:2], None, A.is_equal))
+        vop([("t1", 0, 256), ("ms", 0, 512)], [("t2", 0, 256)], lambda: V.tensor_tensor(T.t2[:], T.ms[:, 256:512], T.t1[:], A.mult))
+        vop([("t2", 0, 256), ("hf", 0, 256), ("ls%d" % r, 0, 128)], [("ttab", 0, 1024)],
+            lambda: V.tensor_tensor(T.ttab[:].indirect(ls[r][:, 16 * t:16 * t + 16]), T.t2[:], T.hf[:], A.add))
+
+    def exchange(t):
+        c = 256 * t
+        sop([("his", 0, 512)], [("hb", c, c + 256)], lambda: S.activation(T.hb[:, c:c + 256], T.his[:, 0:256], F.Copy))
+        o = 256 * (N * t + q)
+        send([("hb", c, c + 256)], broadcast(T.hb[:, c:c + 256], T.lh[:, o:o + 256], "h%d_%d" % (t, q)))
+        for r in near: arrives([("lh", 256 * (N * t + r), 256 * (N * t + r) + 256)], "h%d_%d" % (t, r), near[r])
+
+    def merge(t):
+        def part(buf, c, last):
+            return [(lambda b=b, s=s: mm(T.tm[:, 128 * b:128 * b + 128], T.ma[:, 256 * s + 128 * b:256 * s + 128 * b + 128],
+                                         buf[:, c + 128 * s:c + 128 * s + 128], False, last and b == 1 and s == 1)) for b in range(2) for s in range(2)]
+        op("t", [("tb", 0, 256), ("idb", 0, 128), ("hb", 256 * t, 256 * t + 256), ("ma", 0, 512)], [("tm", 0, 512)],
+           lambda: mm(T.tm[:, 0:256], T.idb[:], T.tb[:], True, False), *part(T.hb, 256 * t, False))
+        order = sorted(near, key=lambda r: topo.chip(T.cores[r]) != topo.chip(core))
+        for r in order:
+            c = 256 * (N * t + r)
+            op("t", [("lh", c, c + 256), ("ma", 0, 512)], [("tm", 0, 512)], *part(T.lh, c, r == order[-1]))
+
+    todo = [((q - d) % N, p) for d in (1, 2, 3) for p in range(16)]
+
+    def expand_some(n):
+        for i in range(min(n, len(todo))):
+            r, p = todo.pop(0)
+            expand(r, p, p + 1)
+
+    def living(c):
+        vop([("ptab", 1024 * c, 1024 * c + 1024)], [("nn", 1024 * c, 1024 * c + 1024)],
+            lambda: V.tensor_scalar(T.nn[:, 1024 * c:1024 * c + 1024], T.ptab[:, 1024 * c:1024 * c + 1024], 4096.0, None, A.not_equal))
+        op("t", [("nn", 1024 * c, 1024 * c + 1024), ("wc", 0, 144)], [("tm", 0, 512)],
+           *[(lambda x=x: mm(T.tm[:, 0:256], T.wc[:, 15 - x:143 - x], T.nn[:, 256 * x:256 * x + 256], x == 0, x == 15)) for x in range(4 * c, 4 * c + 4)])
+
+    clear_hist()
+    vop([(po, SELF, SELF + 16)], [("si", 0, 16)], lambda: V.tensor_copy(T.si[:], own[:, SELF:SELF + 16]))
+    for h in range(2): histogram(h, "si", T.si, -1, False, 4)
+    package()
+    for c in range(3): living(c)
+    fetch(0)
+    parts(0)
+    living(3)
+    low_list()
+    vop([("tm", 0, 512)], [("tb", 0, 256)], lambda: V.tensor_scalar(T.tb[:], T.tm[:, 0:256], 0.0, None, A.is_equal))
+
+    for t in range(RO):
+        cut = 128 if t == 0 else CUT
+        dead(0, cut)
+        dead(128, 256)
+        if t == 0:
+            like(t, 0)
+            classes(t)
+        key_base(t, 0)
+        like_sum(0)
+        key_base(t, 1)
+        like(t, 1)
+        like_sum(1)
+        if t > 0:
+            dead_seekers(t)
+            dead_too(cut, 128)
+            seeker_words()
+        words(0)
+        words(1)
+        difference(t)
+        expand_some(16 if t == 0 else 6)
+        if t > 0: clear_hist()
+        decide(t, 0)
+        histogram(0, "bi", T.bi, 1, False, 8 if t == 0 else SHARE[0])
+        decide(t, 1)
+        codes()
+        histogram(1, "bi", T.bi, 1, True, 8 if t == 0 else SHARE[1])
+        exchange(t)
+        update(t)
+        if t < 3: lists((q - t - 1) % N)
+        if t + 1 < RO:
+            fetch(t + 1)
+            parts(t + 1)
+            like(t + 1, 0)
+            low_list()
+            classes(t + 1)
+            expand_some(11)
+        else:
+            dma("y", [("ttab", 0, 1024)], [], T.yt[:], T.ttab[:])
+            for r in range(N):
+                pr = "pk%d" % r
+                vop([(pr, 0, 256), ("col", 2, 4)], [("val", 256 * r, 256 * r + 256)],
+                    lambda: V.tensor_scalar(T.val[:, 256 * r:256 * r + 256], pk[r][:, 0:256], T.col[:, 2:3], T.col[:, 3:4], A.mult, A.add))
+                vop([("val", 256 * r, 256 * r + 256), ("ls%d" % r, 0, 128)], [("ptab", 0, 4096)],
+                    lambda: V.tensor_copy(T.ptab[:].indirect(ls[r][:, CL - AT:CL - AT + 16]), T.val[:, 256 * r:256 * r + 256]))
+        merge(t)
+        if t + 1 < RO: sop([("tm", 0, 512)], [("tb", 0, 256)], lambda: S.activation(T.tb[:], T.tm[:, 0:256], F.Copy))
+
+    vop([("tm", 0, 512)], [("tq", 0, 256)], lambda: V.tensor_scalar(T.tq[:], T.tm[:, 0:256], 1.0, 4096.0, A.min, A.mult))
+    for h in range(2):
+        op("t", [("tq", 0, 256), ("rb", 0, 2048)], [("wd%d" % h, 0, 512)],
+           *[(lambda x=x: mm(wd[h][:, 256 * x:256 * x + 256], T.rb[:, 128 * (4 * q + 2 * h + x):128 * (4 * q + 2 * h + x) + 128], T.tq[:], True, True)) for x in range(2)])
+        c = 1024 * q + 512 * h
+        vop([("wd%d" % h, 0, 512), ("ptab", c, c + 512)], [("out", 512 * h, 512 * h + 512)],
+            lambda: V.tensor_tensor(T.out[:, 512 * h:512 * h + 512], wd[h][:], T.ptab[:, c:c + 512], A.max))
+        dma("y", [("out", 512 * h, 512 * h + 512)], [], T.yp[:, 512 * h:512 * h + 512], T.out[:, 512 * h:512 * h + 512])
+    g.wait_ge(T.sem.sent, sent[0])
+    finish()

@@ -4,45 +4,39 @@ from concourse.bass import DstId, RemoteDMATransfer
 from concourse.mybir import AluOpType as A, ActivationFunctionType as F
 
 N, RO, K = 4, 6, 256
-CUT = 72
-SHARE = (5, 4)
+CUT = 240
+SHARE = 6
+SPREAD = (10, 13, 13)
 LN2 = math.log(2.0)
-ROUTE, SX, SXB, AT, CL, SLO, SELF, P2S, PKW = 0, 256, 512, 768, 864, 880, 896, 912, 928
+H0 = 33024.0
+SXL, SXH, SXB, P2S, PBW = 0, 256, 512, 768, 784
+CL, SLO = 96, 112
 
 SCRATCH = {
     "ptab": ("sbuf", [128, 4096], "int32"), "tin": ("sbuf", [128, 1024], "int32"), "ttab": ("sbuf", [128, 1024], "float32"),
     "cin": ("sbuf", [128, 16], "int32"), "rin": ("sbuf", [128, 256], "int32"),
-    "pk0": ("sbuf", [128, PKW], "float32"), "pk1": ("sbuf", [128, PKW], "float32"),
-    "pk2": ("sbuf", [128, PKW], "float32"), "pk3": ("sbuf", [128, PKW], "float32"),
-    "ls0": ("sbuf", [128, 128], "uint16"), "ls1": ("sbuf", [128, 128], "uint16"),
-    "ls2": ("sbuf", [128, 128], "uint16"), "ls3": ("sbuf", [128, 128], "uint16"),
-    "re0": ("sbuf", [128, 4096], "float32"), "re1": ("sbuf", [128, 4096], "float32"),
-    "re2": ("sbuf", [128, 4096], "float32"), "re3": ("sbuf", [128, 4096], "float32"),
-    "nn": ("sbuf", [128, 4096], "bfloat16"), "eq": ("sbuf", [128, 4096], "bfloat16"), "al": ("sbuf", [128, 4096], "bfloat16"),
+    "nn": ("sbuf", [128, 1024], "bfloat16"), "eq": ("sbuf", [128, 4096], "bfloat16"), "al": ("sbuf", [128, 4096], "bfloat16"),
     "als": ("sbuf", [128, 256], "bfloat16"), "tb": ("sbuf", [128, 256], "bfloat16"), "tq": ("sbuf", [128, 256], "bfloat16"),
     "hb": ("sbuf", [128, RO * 256], "bfloat16"), "lh": ("sbuf", [128, RO * N * 256], "bfloat16"),
-    "ones": ("sbuf", [128, 512], "bfloat16"), "onef": ("sbuf", [128, 512], "float32"), "rb": ("sbuf", [128, 2048], "bfloat16"),
-    "i16": ("sbuf", [128, 16], "bfloat16"), "rm": ("sbuf", [128, 16], "float32"),
+    "ones": ("sbuf", [128, 128], "bfloat16"), "zz": ("sbuf", [128, 512], "bfloat16"), "rb": ("sbuf", [128, 2048], "bfloat16"),
+    "cnt": ("sbuf", [128, 256], "bfloat16"), "ig": ("sbuf", [128, 128], "bfloat16"), "prow": ("sbuf", [128, 128], "bfloat16"),
+    "clo": ("sbuf", [128, 128], "bfloat16"),
     "idb": ("sbuf", [128, 128], "bfloat16"), "idf": ("sbuf", [128, 128], "float32"), "idq": ("sbuf", [128, 128], "bfloat16"),
-    "idn": ("sbuf", [128, 128], "float32"), "idp": ("sbuf", [128, 128], "float32"), "idm": ("sbuf", [128, 128], "bfloat16"),
-    "bda": ("sbuf", [128, 128], "bfloat16"), "bd": ("sbuf", [128, 128], "bfloat16"),
-    "wa": ("sbuf", [128, 144], "bfloat16"), "wb": ("sbuf", [128, 144], "bfloat16"), "wc": ("sbuf", [128, 144], "bfloat16"),
-    "mw": ("sbuf", [128, 8], "bfloat16"), "ml": ("sbuf", [128, 8], "bfloat16"), "ma": ("sbuf", [128, 512], "bfloat16"),
-    "ex": ("sbuf", [128, 256], "bfloat16"), "prm": ("sbuf", [128, 512], "float32"), "prn": ("sbuf", [128, 512], "float32"),
-    "ch": ("sbuf", [128, 224], "bfloat16"), "clo": ("sbuf", [128, 128], "bfloat16"), "zz": ("sbuf", [128, 256], "bfloat16"),
-    "cra": ("sbuf", [128, 128], "bfloat16"), "crb": ("sbuf", [128, 128], "bfloat16"), "cr": ("sbuf", [128, 128], "bfloat16"),
-    "pfa": ("sbuf", [128, 128], "float32"), "pfac": ("sbuf", [128, 144], "float32"),
-    "rwi": ("sbuf", [128, 8], "int32"), "col": ("sbuf", [128, 64], "float32"), "pwb": ("sbuf", [128, 8], "bfloat16"),
-    "ci": ("sbuf", [128, 96], "int32"), "cb": ("sbuf", [128, 96], "bfloat16"), "tr": ("sbuf", [128, 256], "float32"),
+    "idn": ("sbuf", [128, 128], "bfloat16"), "idm": ("sbuf", [128, 128], "bfloat16"),
+    "mw": ("sbuf", [128, 8], "bfloat16"), "ml": ("sbuf", [128, 8], "bfloat16"), "mo": ("sbuf", [128, 8], "bfloat16"),
+    "s8": ("sbuf", [128, 8], "bfloat16"), "ma": ("sbuf", [128, 512], "bfloat16"), "ex": ("sbuf", [128, 128], "bfloat16"),
+    "prn": ("sbuf", [128, 512], "float32"), "cr": ("sbuf", [128, 144], "bfloat16"), "wl": ("sbuf", [128, 136], "bfloat16"),
+    "r16": ("sbuf", [128, 128], "bfloat16"), "r32": ("sbuf", [128, 256], "bfloat16"),
+    "rwi": ("sbuf", [128, 8], "int32"), "col": ("sbuf", [128, 32], "float32"), "pwb": ("sbuf", [128, 8], "bfloat16"),
+    "ci": ("sbuf", [128, 48], "int32"), "cb": ("sbuf", [128, 48], "bfloat16"), "tr": ("sbuf", [128, 256], "float32"),
     "ati": ("sbuf", [128, 192], "int32"), "hf": ("sbuf", [128, 256], "float32"),
     "lf": ("sbuf", [128, 256], "uint16"), "ll": ("sbuf", [128, 256], "uint16"), "h2": ("sbuf", [128, 256], "bfloat16"),
-    "nm": ("sbuf", [128, 256], "bfloat16"), "p2": ("sbuf", [128, 272], "bfloat16"), "ab": ("sbuf", [128, 1024], "bfloat16"),
+    "lob": ("sbuf", [128, 256], "bfloat16"), "nm": ("sbuf", [128, 256], "bfloat16"), "p2": ("sbuf", [128, 272], "bfloat16"),
+    "ab": ("sbuf", [128, 1024], "bfloat16"), "df": ("sbuf", [128, 256], "bfloat16"),
     "y": ("sbuf", [128, 272], "int32"), "ya": ("sbuf", [128, 272], "int32"), "dd": ("sbuf", [128, 272], "float32"),
-    "kk": ("sbuf", [128, 272], "float32"), "m1": ("sbuf", [128, 128], "float32"), "m2": ("sbuf", [128, 64], "float32"),
-    "m3": ("sbuf", [128, 32], "float32"), "m4": ("sbuf", [128, 16], "float32"), "bi": ("sbuf", [128, 16], "int32"),
-    "hl": ("sbuf", [128, 32], "int32"), "hlf": ("sbuf", [128, 32], "float32"), "si": ("sbuf", [128, 16], "int32"),
-    "oh": ("sbuf", [128, 2048], "bfloat16"), "ol": ("sbuf", [128, 2048], "bfloat16"),
-    "cdi": ("sbuf", [128, 16], "int32"), "cdb": ("sbuf", [128, 16], "bfloat16"), "ct": ("sbuf", [128, 128], "bfloat16"),
+    "kk": ("sbuf", [128, 272], "float32"), "run": ("sbuf", [128, 256], "float32"), "bi": ("sbuf", [128, 16], "int32"),
+    "hl": ("sbuf", [128, 48], "int32"), "dg": ("sbuf", [128, 1536], "bfloat16"), "up": ("sbuf", [128, 512], "bfloat16"),
+    "oh": ("sbuf", [128, 512], "bfloat16"), "ol": ("sbuf", [128, 2048], "bfloat16"), "ct": ("sbuf", [128, 256], "bfloat16"),
     "t1": ("sbuf", [128, 256], "float32"), "t2": ("sbuf", [128, 256], "float32"),
     "val": ("sbuf", [128, 1024], "float32"), "out": ("sbuf", [128, 1024], "float32"),
     "key0": ("psum", [128, 512], "float32"), "key1": ("psum", [128, 512], "float32"),
@@ -50,9 +44,15 @@ SCRATCH = {
     "his": ("psum", [128, 512], "float32"), "tm": ("psum", [128, 512], "float32"),
     "ms": ("psum", [128, 512], "float32"), "mt": ("psum", [128, 512], "float32"),
 }
+for _r in range(N):
+    SCRATCH["pk%d" % _r] = ("sbuf", [128, 256], "float32")
+    SCRATCH["pb%d" % _r] = ("sbuf", [128, PBW], "bfloat16")
+    SCRATCH["ls%d" % _r] = ("sbuf", [128, 128], "uint16")
+    SCRATCH["re%d" % _r] = ("sbuf", [128, 4096], "float32")
 PSUM = [k for k in SCRATCH if SCRATCH[k][0] == "psum"]
-SEMAPHORES = (["cv", "cs", "ct", "cg", "sent"] + ["d%d" % i for i in range(16)] + ["k%d" % r for r in range(N)]
-              + ["p%d" % r for r in range(N)] + ["h%d_%d" % (t, r) for t in range(RO) for r in range(N)])
+SEMAPHORES = (["cv", "cs", "ct", "cg", "sent"] + ["d%d" % i for i in range(16)]
+              + ["%s%d" % (b, r) for b in ("apk", "apb", "als") for r in range(N)]
+              + ["h%d_%d" % (t, r) for t in range(RO) for r in range(N)])
 
 
 def scheduler(g, T):
@@ -83,8 +83,9 @@ def scheduler(g, T):
         for b, lo, hi in reads:
             log[b] = [e for e in log.get(b, []) if e[2] or e[3] != s or not (lo <= e[0] and e[1] <= hi)] + [(lo, hi, False, s, n)]
 
-    def op(qn, reads, writes, *fns):
+    def op(qn, reads, writes, *fns, adds=False):
         need, rd, wr = needs(reads, writes)
+        if adds: need.pop("ct", None)
         wait(qn, need)
         for f in fns: ins = f()
         s = "c" + qn
@@ -122,16 +123,18 @@ def rank_program(g, core, T, topo):
     op, dma, arrives, send, finish = scheduler(g, T)
     V, S, P = g.vector, g.scalar, g.tensor
     pk = [T["pk%d" % r] for r in range(N)]
+    pb = [T["pb%d" % r] for r in range(N)]
     ls = [T["ls%d" % r] for r in range(N)]
     rx = [T["re%d" % r] for r in range(N)]
     key, wd = [T.key0, T.key1], [T.wd0, T.wd1]
     mm = P.matmul
-    own = pk[q]
-    po = "pk%d" % q
+    ID = [(b, 0, 128) for b in ("idb", "idq", "idn", "idm", "idf")]
 
     def vop(reads, writes, f): op("v", reads, writes, f)
 
     def sop(reads, writes, f): op("s", reads, writes, f)
+
+    def bank(b): return (b, 0, 512)
 
     def ways(c):
         w, used, plan = {}, set(), []
@@ -145,6 +148,7 @@ def rank_program(g, core, T, topo):
         return plan
     plan = ways(core)
     near = {r: [len(e) for e, ds in ways(T.cores[r]) if core in ds][0] for r in range(N) if r != q}
+    order = sorted(near, key=lambda r: topo.chip(T.cores[r]) != topo.chip(core))
     sent = [0]
 
     def broadcast(src, dst, sem):
@@ -154,370 +158,397 @@ def rank_program(g, core, T, topo):
         sent[0] += sum(len(e) for e, ds in plan)
         return lambda: g.remote_dma_fused(trs, local_sem=T.sem.sent)
 
-    def tell(a, b, sem):
-        send([(po, a, b)], broadcast(own[:, a:b], own[:, a:b], "%s%d" % (sem, q)))
-        for r in near: arrives([("pk%d" % r, a, b)], "%s%d" % (sem, r), near[r])
+    def tell(b, w):
+        mine = "%s%d" % (b, q)
+        send([(mine, 0, w)], broadcast(T[mine][:], T[mine][:], "a" + mine))
+        for r in near: arrives([("%s%d" % (b, r), 0, w)], "a%s%d" % (b, r), near[r])
 
-    dma("y", [], [("cin", 0, 16)], T.cin[:], T.calls[:])
     dma("y", [], [("rin", 0, 256)], T.rin[:], T.routes[:])
+    dma("s", [], [("cin", 0, 16)], T.cin[:], T.calls[:])
     dma("y", [], [("tin", 0, 1024)], T.tin[:], T.trunk[:])
-    for c in range(4):
-        dma("y", [], [("ptab", 1024 * c, 1024 * c + 1024)], T.ptab[:, 1024 * c:1024 * c + 1024], T.paths[:, 1024 * c:1024 * c + 1024])
-
-    def select(dst, w, src, pattern, cmp, fill, base, cm, lo=0):
-        op("g", [(src, lo, lo + w)], [(dst, lo, lo + w)],
-           lambda: g.affine_select(T[dst][:, lo:lo + w], T[src][:, lo:lo + w], pattern, cmp, fill, base, cm))
+    for i in range(4):
+        c = 1024 * ((q + i) % N)
+        dma("sy"[i % 2], [], [("ptab", c, c + 1024)], T.ptab[:, c:c + 1024], T.paths[:, c:c + 1024])
 
     def iota(dst, w, pattern, base, cm):
         op("g", [], [(dst, 0, w)], lambda: g.iota(T[dst][:, 0:w], pattern, base, cm, allow_small_or_imprecise_dtypes=True))
-    COL = {15 * LN2: 8, 144 * LN2: 16, 32896.5: 32, 1.0: 40}
 
-    def cc(x): return T.col[:, COL[x]:COL[x] + 1]
+    def where(dst, w, pattern, fill):
+        op("g", [("zz", 0, w)], [(dst, 0, w)], lambda: g.affine_select(T[dst][:, 0:w], T.zz[:, 0:w], pattern, A.not_equal, fill, 0, 1))
+    PART, PP, P48, P24, P16, G16, PART16, Y0, Y1, BACK, WL, MINE, LOW, HIGH = range(14)
+    NUM = {144 * LN2: 16, H0 - 127.5: 17, 1.0: 18, H0: 19, 128.0: 20, 4096.0: 21}
 
-    def cn(x): return ("col", COL[x], COL[x] + 1)
-    vop([], [("ones", 0, 512)], lambda: V.memset(T.ones[:], 1.0))
-    vop([], [("onef", 0, 512)], lambda: V.memset(T.onef[:], 1.0))
+    def cx(i): return T.col[:, i:i + 1]
+
+    def cn(i): return ("col", i, i + 1)
+
+    def column(dst, src, s1, s2, *ops):
+        vop([cn(src)], [cn(dst)], lambda: V.tensor_scalar(cx(dst), cx(src), s1, s2, *ops))
+
+    def match(dst, a, b, src, view, c, s2, *more, reads=()):
+        vop([src, cn(c)] + list(reads), [(dst, a, b)], lambda: V.tensor_scalar(T[dst][:, a:b], view, cx(c), s2, A.is_equal, *more))
     iota("rwi", 1, [[0, 1]], 0, 1)
-    iota("i16", 16, [[1, 16]], 0, 0)
-    select("bda", 128, "ones", [[-16, 8], [0, 16]], A.is_ge, 0.0, 0, 1)
-    select("bd", 128, "bda", [[16, 8], [0, 16]], A.is_ge, 0.0, 15, -1)
-    select("idf", 128, "onef", [[-1, 128]], A.is_equal, 0.0, 0, 1)
-    select("prm", 512, "onef", [[-16, 2], [16, 2], [-1, 128]], A.is_equal, 0.0, 0, 1)
-    for b in range(4):
-        select("prn", 128, "prm", [[0, 4], [1, 2], [0, 16]], A.is_equal, 0.0, -(b % 2), 0, 128 * b)
-    iota("ch", 224, [[-1, 224]], 127, 0)
-    iota("clo", 128, [[-1, 128]], 127, 0)
-    select("idb", 128, "ones", [[-1, 128]], A.is_equal, 0.0, 0, 1)
-    vop([], [("zz", 0, 256)], lambda: V.memset(T.zz[:], 0.0))
-    for x in COL: vop([], [cn(x)], lambda: V.memset(cc(x), x))
-    vop([], [("pfac", 0, 16)], lambda: V.memset(T.pfac[:, 0:16], (8388608.0 + 16) / 32768))
+    iota("cnt", 256, [[1, 256]], 0, 0)
+    iota("ig", 128, [[16, 8], [0, 16]], 0, 0)
+    iota("prow", 128, [[0, 8], [-1, 16]], 15, 0)
+    vop([], [("zz", 0, 512)], lambda: V.memset(T.zz[:], 0.0))
+    vop([], [("ones", 0, 128)], lambda: V.memset(T.ones[:], 1.0))
+    for x, i in NUM.items(): vop([], [cn(i)], lambda: V.memset(cx(i), x))
+    vop([], [("dg", 0, 1536)], lambda: V.memset(T.dg[:], 1.0))
+    for b, w, step in (("r16", 128, 16), ("r32", 256, 32)):
+        vop([], [(b, 0, w)], lambda: V.memset(T[b][:], 1.0))
+        vop([], [(b, 0, w)], lambda: V.memset(T[b][:, 0::step], 0.0))
+    vop([], [("cr", 0, 144)], lambda: V.memset(T.cr[:], 0.0))
+    for row, a, b in ((0, -16.0, None), (32, 1179648.0, -786432.0), (64, 8192.0, 8160.0)):
+        vop([], [("cr", 0, 16)], lambda: V.memset(T.cr[row:row + 1, 0:16], a))
+        if b: vop([], [("cr", 16, 144)], lambda: V.memset(T.cr[row:row + 1, 16:144], b))
+    for i, m in ((PP, 15), (P48, 48), (P24, 24), (P16, 16), (G16, 112)):
+        vop([("rwi", 0, 1)], [("rwi", i, i + 1)], lambda: V.tensor_scalar(T.rwi[:, i:i + 1], T.rwi[:, 0:1], m, None, A.bitwise_and))
+    vop([("rwi", 0, 6)], [("col", 0, 6)], lambda: V.tensor_copy(T.col[:, 0:6], T.rwi[:, 0:6]))
+    column(PART16, PART, 16.0, None, A.add)
+    column(Y0, P16, 0.0, None, A.is_equal)
+    column(Y1, P16, 16.0, None, A.is_equal)
+    sop([cn(PP)], [("pwb", 0, 1)], lambda: S.activation(T.pwb[:, 0:1], cx(PP), F.Exp, scale=LN2))
+    CNT, IG = ("cnt", 0, 256), ("ig", 0, 128)
 
     ci, cb, ati = T.ci, T.cb, T.ati
-    vop([("rwi", 0, 1)], [("rwi", 4, 5)], lambda: V.tensor_scalar(T.rwi[:, 4:5], T.rwi[:, 0:1], 15, None, A.bitwise_and))
-    vop([("rwi", 4, 5)], [("col", 0, 1)], lambda: V.tensor_copy(T.col[:, 0:1], T.rwi[:, 4:5]))
-    sop([("col", 0, 1)], [("pwb", 0, 1)], lambda: S.activation(T.pwb[:, 0:1], T.col[:, 0:1], F.Exp, scale=LN2))
-    vop([("i16", 0, 16), ("col", 0, 1)], [("rm", 0, 16)], lambda: V.tensor_scalar(T.rm[:], T.i16[:], T.col[:, 0:1], None, A.is_equal))
-    for x in range(16):
-        vop([("bd", 0, 128), ("rm", 0, 16)], [("rb", 128 * x, 128 * x + 128)],
-            lambda: V.tensor_scalar(T.rb[:, 128 * x:128 * x + 128], T.bd[:], T.rm[:, x:x + 1], None, A.mult))
+    own, po, mine, bo, lo_ = pk[q], "pk%d" % q, pb[q], "pb%d" % q, "ls%d" % q
+    vop([("rin", 0, 256)], [(po, 0, 256)], lambda: V.tensor_copy(own[:], T.rin[:]))
+    vop([(po, 0, 256)], [("tr", 0, 256)], lambda: V.transpose(T.tr[:], own[:]))
+    tell("pk", 256)
+    for y in range(2):
+        for b in range(2):
+            s, c = 16 - 16 * (b - y), 256 * y + 128 * b
+            match("prn", c, c + 128, CNT, T.cnt[:, s:s + 128], PART16, cx(Y0 + y), A.mult, reads=[cn(Y0 + y)])
+    where("idb", 128, [[-1, 128]], 1.0)
+    where("idq", 128, [[-1, 128]], -1.0)
+    where("idn", 128, [[-1, 128]], -32.0)
+    where("idm", 128, [[-1, 128]], -2097152.0)
+    where("ex", 128, [[-1, 8], [0, 16]], 1.0)
+    where("ma", 512, [[128, 2], [-1, 2], [-2, 128]], 1.0)
+
+    def expand(qn, r, ps):
+        for p in ps:
+            if qn == "s": f = lambda: S.activation(rx[r][:, p::16], pk[r][:], F.Copy)
+            else: f = lambda: g.affine_select(rx[r][:, p::16], pk[r][:], [[0, 256]], A.is_ge, 0.0, 0, 0)
+            op(qn, [("pk%d" % r, 0, 256)], [("re%d" % r, 256 * p, 256 * p + 256)], f)
+    expand("s", q, range(8))
+
+    def opened(b, ts):
+        op("t", [("tr", 0, 256), ("prn", 0, 512)], [bank(b)],
+           *[(lambda t=t, y=y, x=x: mm(T[b][:, 16 * t + y:16 * t + 16:2], T.prn[:, 256 * y + 128 * x:256 * y + 128 * x + 128],
+                                       T.tr[:, 16 * x + t::32], x == 0, x == 1)) for t in ts for y in range(2) for x in range(2)])
+
+    def opened_lists(bn, ts):
+        a, b = 16 * ts[0], 16 * ts[-1] + 16
+        vop([bank(bn)], [("ati", a, b)], lambda: V.tensor_copy(ati[:, a:b], T[bn][:, a:b]))
+        vop([("ati", a, b)], [("ati", 96 + a, 96 + b)], lambda: V.tensor_scalar(ati[:, 96 + a:96 + b], ati[:, a:b], 1023, None, A.bitwise_and))
+        vop([("ati", 96 + a, 96 + b)], [(lo_, a, b)], lambda: V.tensor_copy(ls[q][:, a:b], ati[:, 96 + a:96 + b]))
+    opened("wd0", [0])
+    opened("tm", [1, 2, 3, 4, 5])
     for i, m in ((0, 255), (1, 3840), (2, 3072)):
         vop([("cin", 0, 16)], [("ci", 16 * i, 16 * i + 16)], lambda: V.tensor_scalar(ci[:, 16 * i:16 * i + 16], T.cin[:], m, None, A.bitwise_and))
-    vop([("ci", 0, 48)], [("cb", 0, 48)], lambda: V.tensor_copy(cb[:, 0:48], ci[:, 0:48]))
-    vop([("rin", 0, 256)], [(po, 0, 256)], lambda: V.tensor_copy(own[:, 0:256], T.rin[:]))
-    vop([(po, 0, 256)], [("tr", 0, 256)], lambda: V.transpose(T.tr[:], own[:, 0:256]))
-    tell(ROUTE, SX, "k")
-    select("wa", 144, "ones", [[0, 9], [1, 16]], A.is_equal, 0.0, -15, 0)
-    select("wb", 144, "wa", [[-16, 9], [0, 16]], A.is_ge, 0.0, 0, 1)
-    select("wc", 144, "wb", [[16, 9], [0, 16]], A.is_ge, 0.0, 15, -1)
-    iota("cra", 128, [[0, 8], [-1, 16]], -17, 0)
-    select("crb", 128, "cra", [[0, 128]], A.is_equal, 0.0, -1, 1)
-    select("cr", 128, "crb", [[0, 128]], A.not_equal, 262144.0, 0, 1)
-    iota("pfa", 128, [[0, 8], [-1, 16]], 4194304 + 15, 0)
-    select("ma", 512, "ones", [[128, 2], [-1, 2], [-2, 128]], A.is_equal, 0.0, 0, 1)
-    select("ex", 256, "ones", [[-1, 16], [0, 16]], A.is_equal, 0.0, 0, 1)
-
-    def expand(r, lo, hi):
-        for p in range(lo, hi):
-            sop([("pk%d" % r, 0, 256)], [("re%d" % r, 256 * p, 256 * p + 256)],
-                lambda: S.activation(rx[r][:, p::16], pk[r][:, 0:256], F.Copy))
-    expand(q, 0, 16)
-    op("t", [("cb", 0, 32), ("rb", 0, 2048)], [("ms", 0, 512)],
-       *[(lambda x=x, h=h: mm(T.ms[:, x:256:16], T.rb[:, 128 * x:128 * x + 128], cb[:, 16 * h:16 * h + 16], h == 0, h == 1))
-         for x in range(16) for h in range(2)])
-    vop([("ms", 0, 512)], [(po, SX, SX + 256)], lambda: V.tensor_copy(own[:, SX:SX + 256], T.ms[:, 0:256]))
-    op("t", [(po, SX, SX + 256), ("idf", 0, 128)], [("wd1", 0, 512)],
-       *[(lambda h=h: mm(T.wd1[:, 8 * h:8 * h + 8], own[:, SX + 128 * h:SX + 128 * h + 128], T.idf[:, 0::16], True, True)) for h in range(2)])
-
-    def opened(bank, bname, ts):
-        op("t", [("tr", 0, 256), ("prn", 0, 512)], [(bname, 0, 512)],
-           *[(lambda t=t, y=y, b=b: mm(bank[:, 16 * t + y:16 * t + 16:2], T.prn[:, 256 * y + 128 * b:256 * y + 128 * b + 128],
-                                       T.tr[:, 16 * b + t::32], b == 0, b == 1)) for t in ts for y in range(2) for b in range(2)])
-
-    def opened_lists(bank, bname, ts):
-        a, b = 16 * ts[0], 16 * ts[-1] + 16
-        vop([(bname, 0, 512)], [("ati", a, b)], lambda: V.tensor_copy(ati[:, a:b], bank[:, a:b]))
-        vop([("ati", a, b)], [("ati", 96 + a, 96 + b)], lambda: V.tensor_scalar(ati[:, 96 + a:96 + b], ati[:, a:b], 1023, None, A.bitwise_and))
-        vop([("ati", 96 + a, 96 + b)], [("ls%d" % q, a, b)], lambda: V.tensor_copy(ls[q][:, a:b], ati[:, 96 + a:96 + b]))
-    opened(T.wd0, "wd0", [0])
-    opened_lists(T.wd0, "wd0", [0])
-    op("t", [("cb", 32, 48), ("rb", 0, 2048)], [("mt", 0, 512)],
+    vop([("ci", 0, 16)], [("cb", 0, 16)], lambda: V.tensor_copy(cb[:, 0:16], ci[:, 0:16]))
+    vop([("ci", 16, 48)], [("cb", 16, 48)], lambda: V.tensor_scalar(cb[:, 16:48], ci[:, 16:48], H0, None, A.add))
+    for x in range(16):
+        vop([IG, cn(PART)], [("rb", 128 * x, 128 * x + 128)],
+            lambda: V.tensor_scalar(T.rb[:, 128 * x:128 * x + 128], T.ig[:], float(x), cx(PART), A.add, A.is_equal))
+    op("t", [("cb", 0, 32), ("rb", 0, 2048)], [bank("ms")],
+       *[(lambda x=x: mm(T.ms[:, x::16], T.rb[:, 128 * x:128 * x + 128], cb[:, 0:32], True, True)) for x in range(16)])
+    op("t", [("cb", 32, 48), ("rb", 0, 2048)], [bank("mt")],
        *[(lambda x=x: mm(T.mt[:, x:256:16], T.rb[:, 128 * x:128 * x + 128], cb[:, 32:48], True, True)) for x in range(16)])
-    opened(T.tm, "tm", [1, 2, 3, 4, 5])
-    vop([("mt", 0, 512)], [(po, SXB, SXB + 256)], lambda: V.tensor_copy(own[:, SXB:SXB + 256], T.mt[:, 0:256]))
-    vop([("wd1", 0, 512)], [(po, SELF, SELF + 16)], lambda: V.tensor_scalar(own[:, SELF:SELF + 16], T.wd1[:, 0:16], -32.0, 4095.0 * 32 + 16, A.mult, A.add))
-    vop([("wd1", 0, 512)], [("ci", 48, 64)], lambda: V.tensor_copy(ci[:, 48:64], T.wd1[:, 0:16]))
-    vop([("ci", 48, 64)], [("ci", 64, 80)], lambda: V.tensor_scalar(ci[:, 64:80], ci[:, 48:64], 3840, None, A.bitwise_and))
-    vop([("ci", 64, 80)], [("cb", 48, 64)], lambda: V.tensor_copy(cb[:, 48:64], ci[:, 64:80]))
-    sop([("cb", 48, 64), cn(15 * LN2)], [("cb", 64, 80)], lambda: S.activation(cb[:, 64:80], cb[:, 48:64], F.Exp, bias=cc(15 * LN2), scale=-LN2 / 256))
-    sop([("cb", 64, 80)], [(po, P2S, P2S + 16)], lambda: S.activation(own[:, P2S:P2S + 16], cb[:, 64:80], F.Copy))
-
-    def lists(r):
-        vop([("pk%d" % r, AT, SELF)], [("ls%d" % r, 0, 128)], lambda: V.tensor_copy(ls[r][:], pk[r][:, AT:SELF]))
-
-    def package():
-        opened_lists(T.tm, "tm", [1, 2, 3, 4, 5])
-        vop([("ati", 96, 192)], [(po, AT, AT + 96)], lambda: V.tensor_copy(own[:, AT:AT + 96], ati[:, 96:192]))
-        vop([("cin", 0, 16)], [(po, CL, CL + 16)], lambda: V.tensor_copy(own[:, CL:CL + 16], T.cin[:]))
-        vop([("ci", 0, 16)], [(po, SLO, SLO + 16)], lambda: V.tensor_copy(own[:, SLO:SLO + 16], ci[:, 0:16]))
-        vop([(po, CL, SELF)], [("ls%d" % q, 96, 128)], lambda: V.tensor_copy(ls[q][:, 96:128], own[:, CL:SELF]))
-        tell(SX, PKW, "p")
+    opened_lists("wd0", [0])
     vop([("tin", 0, 1024)], [("ttab", 0, 1024)], lambda: V.tensor_copy(T.ttab[:], T.tin[:]))
-    vop([("idf", 0, 128)], [("idn", 0, 128)], lambda: V.tensor_scalar(T.idn[:], T.idf[:], -32.0, None, A.mult))
-    vop([("idf", 0, 128)], [("idp", 0, 128)], lambda: V.tensor_scalar(T.idp[:], T.idf[:], -1.0, None, A.mult))
-    vop([("idb", 0, 128)], [("idq", 0, 128)], lambda: V.tensor_scalar(T.idq[:], T.idb[:], -1.0, None, A.mult))
-    vop([("idb", 0, 128)], [("idm", 0, 128)], lambda: V.tensor_scalar(T.idm[:], T.idb[:], -4194304.0, None, A.mult))
-    vop([("bd", 0, 128), ("pwb", 0, 1)], [("mw", 0, 8)], lambda: V.tensor_scalar(T.mw[:], T.bd[:, 0::16], T.pwb[:, 0:1], None, A.mult))
-    vop([("bd", 0, 128)], [("ml", 0, 8)], lambda: V.tensor_scalar(T.ml[:], T.bd[:, 0::16], 131072.0, None, A.mult))
-    vop([("pfa", 0, 128)], [("pfac", 16, 144)], lambda: V.tensor_scalar(T.pfac[:, 16:144], T.pfa[:], 1.0 / 32768, None, A.mult))
-    vop([("pfac", 0, 144)], [("mt", 0, 512)], lambda: V.tensor_copy(T.mt[:, 256:400], T.pfac[:]))
-    vop([("col", 0, 1)], [("col", 1, 2)], lambda: V.tensor_scalar(T.col[:, 1:2], T.col[:, 0:1], -1.0, 15.0, A.mult, A.add))
-    vop([("col", 0, 1)], [("col", 2, 3)], lambda: V.tensor_scalar(T.col[:, 2:3], T.col[:, 0:1], 6.0, None, A.is_lt))
-    vop([("col", 0, 1)], [("col", 3, 4)], lambda: V.tensor_scalar(T.col[:, 3:4], T.col[:, 0:1], 6.0, 4096.0, A.is_ge, A.mult))
+    sop([bank("ms")], [(bo, SXL, SXB)], lambda: S.activation(mine[:, SXL:SXB], T.ms[:], F.Copy))
+    sop([bank("mt")], [(bo, SXB, P2S)], lambda: S.activation(mine[:, SXB:P2S], T.mt[:, 0:256], F.Copy))
+    op("t", [(bo, SXH, SXB), ID[0]], [bank("wd1")],
+       *[(lambda h=h: mm(T.wd1[:, 8 * h:8 * h + 8], mine[:, SXH + 128 * h:SXH + 128 * h + 128], T.idb[:, 0::16], True, True)) for h in range(2)])
+    sop([bank("wd1"), cn(NUM[144 * LN2])], [(bo, P2S, PBW)],
+        lambda: S.activation(mine[:, P2S:PBW], T.wd1[:, 0:16], F.Exp, bias=cx(NUM[144 * LN2]), scale=-LN2 / 256))
+    expand("s", q, range(8, 16))
+    opened_lists("tm", [1, 2, 3, 4, 5])
+    vop([("cin", 0, 16)], [(lo_, CL, CL + 16)], lambda: V.tensor_copy(ls[q][:, CL:CL + 16], T.cin[:]))
+    vop([("ci", 0, 16)], [(lo_, SLO, SLO + 16)], lambda: V.tensor_copy(ls[q][:, SLO:SLO + 16], ci[:, 0:16]))
+    tell("pb", PBW)
+    tell("ls", 128)
+    expand("g", (q - 1) % N, range(SPREAD[0]))
+    match("idf", 0, 128, CNT, T.cnt[:, 0:128], PART, None)
+    match("s8", 0, 8, IG, T.ig[:, 0::16], PART, -32.0, A.mult)
+    match("mo", 0, 8, IG, T.ig[:, 0::16], G16, None)
+    match("ml", 0, 8, IG, T.ig[:, 0::16], G16, 131072.0, A.mult)
+    vop([("mo", 0, 8), ("pwb", 0, 1)], [("mw", 0, 8)], lambda: V.tensor_scalar(T.mw[:], T.mo[:], T.pwb[:, 0:1], None, A.mult))
+    vop([CNT], [("clo", 0, 128)], lambda: V.tensor_scalar(T.clo[:], T.cnt[:, 0:128], -1.0, 127.0, A.mult, A.add))
+    vop([("prow", 0, 128)], [("cr", 16, 144)], lambda: V.tensor_copy(T.cr[0:1, 16:144], T.prow[0:1, :]))
+    column(BACK, PP, -1.0, 15.0, A.mult, A.add)
+    column(WL, P48, 2.0, 8.0 * q + 7, A.mult, A.add)
+    column(MINE, P24, 8.0 * q, None, A.is_equal)
+    column(LOW, PP, float(RO), None, A.is_lt)
+    column(HIGH, PP, float(RO), 4096.0, A.is_ge, A.mult)
+    match("wl", 0, 136, CNT, T.cnt[:, 0:136], WL, None)
+    vop([], [bank("mt")], lambda: V.memset(T.mt[:, 256:272], (8388608.0 + 16) / 32768))
+    vop([("prow", 0, 128)], [bank("mt")], lambda: V.tensor_scalar(T.mt[:, 272:400], T.prow[:], 1.0 / 32768, 128.0, A.mult, A.add))
 
     def clear_hist():
-        op("t", [("ones", 0, 128), ("zz", 0, 256)], [("his", 0, 512)], lambda: mm(T.his[:, 0:256], T.ones[:, 0:128], T.zz[:], True, False))
+        op("t", [("ones", 0, 128), ("zz", 0, 256)], [bank("his")], lambda: mm(T.his[:, 0:256], T.ones[:], T.zz[:, 0:256], True, False))
 
-    def histogram(half, bname, buf, sign, last, share):
-        o = 16 * half
-        vop([(bname, 8 * half, 8 * half + 8)], [("hl", o, o + 8)],
-            lambda: V.tensor_scalar(T.hl[:, o:o + 8], buf[:, 8 * half:8 * half + 8], 12, 0xC1F, A.logical_shift_right, A.bitwise_and))
-        vop([(bname, 8 * half, 8 * half + 8)], [("hl", o + 8, o + 16)],
-            lambda: V.tensor_scalar(T.hl[:, o + 8:o + 16], buf[:, 8 * half:8 * half + 8], 5, 127, A.logical_shift_right, A.bitwise_and))
-        vop([("hl", o, o + 16)], [("hlf", o, o + 16)], lambda: V.tensor_copy(T.hlf[:, o:o + 16], T.hl[:, o:o + 16]))
-        a = 512 * half
+    def digits(h, codes):
+        o, d, n = 24 * h, 768 * h, 24 if codes else 16
+        src, sn = T.bi[:, 8 * h:8 * h + 8], ("bi", 8 * h, 8 * h + 8)
+        vop([sn], [("hl", o, o + 8)], lambda: V.tensor_scalar(T.hl[:, o:o + 8], src, 12, 0xC1F, A.logical_shift_right, A.bitwise_and))
+        vop([sn], [("hl", o + 8, o + 16)], lambda: V.tensor_scalar(T.hl[:, o + 8:o + 16], src, 5, 127, A.logical_shift_right, A.bitwise_and))
+        if codes: vop([sn], [("hl", o + 16, o + 24)], lambda: V.tensor_scalar(T.hl[:, o + 16:o + 24], src, 31, None, A.bitwise_and))
+        vop([("hl", o, o + n)], [("dg", d, d + 32 * n)], lambda: V.tensor_copy(T.dg[:, d:d + 32 * n:32], T.hl[:, o:o + n]))
+
+    def one_hots(h, sign, share):
+        d, c = 768 * h, 256 * h
+        low = [T.dg[:, d + 256 + 32 * n:d + 257 + 32 * n] for n in range(8)]
         for n in range(share, 8):
-            d = a + 128 * (n - share)
-            sop([("clo", 0, 128), ("hlf", o, o + 16)], [("ab", d, d + 128)],
-                lambda: S.activation(T.ab[:, d:d + 128], T.clo[:], F.Abs, bias=T.hlf[:, o + 8 + n:o + 9 + n], scale=-1.0))
+            a = 128 * (n - share)
+            sop([("clo", 0, 128), ("dg", d + 256, d + 512)], [("ab", a, a + 128)],
+                lambda: S.activation(T.ab[:, a:a + 128], T.clo[:], F.Abs, bias=low[n], scale=-1.0))
         if share < 8:
-            d, w = 1024 * half + 1024, 128 * (8 - share)
-            sop([("ab", a, a + w), cn(1.0)], [("ol", d - w, d)],
-                lambda: S.activation(T.ol[:, d - w:d], T.ab[:, a:a + w], F.Relu, bias=cc(1.0), scale=-1.0))
-        for n in range(8):
-            c = 128 * (8 * half + n)
-            k = 96 - 32 * (n % 4)
-            if sign > 0:
-                vop([("ch", 0, 224), ("hlf", o, o + 16)], [("oh", c, c + 128)],
-                    lambda: V.tensor_scalar(T.oh[:, c:c + 128], T.ch[:, k:k + 128], T.hlf[:, o + n:o + n + 1], None, A.is_equal))
-            else:
-                vop([("ch", 0, 224), ("hlf", o, o + 16)], [("oh", c, c + 128)],
-                    lambda: V.tensor_scalar(T.oh[:, c:c + 128], T.ch[:, k:k + 128], T.hlf[:, o + n:o + n + 1], -1.0, A.is_equal, A.mult))
-            if n < share:
-                vop([("clo", 0, 128), ("hlf", o, o + 16)], [("ol", c, c + 128)],
-                    lambda: V.tensor_scalar(T.ol[:, c:c + 128], T.clo[:], T.hlf[:, o + 8 + n:o + 9 + n], None, A.is_equal))
-        for n in range(8):
-            c, j = 128 * (8 * half + n), 128 * (n // 4)
-            op("t", [("oh", c, c + 128), ("ol", c, c + 128)], [("his", 0, 512)],
-               lambda: mm(T.his[:, j:j + 128], T.oh[:, c:c + 128], T.ol[:, c:c + 128], False, last and n == 7))
+            e, w = 1024 * h + 1024, 128 * (8 - share)
+            sop([("ab", 0, w), cn(NUM[1.0])], [("ol", e - w, e)],
+                lambda: S.activation(T.ol[:, e - w:e], T.ab[:, 0:w], F.Relu, bias=cx(NUM[1.0]), scale=-1.0))
+        vop([("r32", 0, 256), ("dg", d, d + 256)], [("up", c, c + 256)],
+            lambda: V.tensor_tensor_scan(T.up[:, c:c + 256], T.r32[:], T.dg[:, d:d + 256], 0.0, A.mult, A.add))
+        vop([("up", c, c + 256)], [("oh", c, c + 256)],
+            lambda: V.tensor_scalar(T.oh[:, c:c + 256], T.up[:, c:c + 256], 31.0, sign, A.is_equal, A.mult))
+        for n in range(share):
+            a = 128 * (8 * h + n)
+            vop([("clo", 0, 128), ("dg", d + 256, d + 512)], [("ol", a, a + 128)],
+                lambda: V.tensor_scalar(T.ol[:, a:a + 128], T.clo[:], low[n], None, A.is_equal))
+
+    def counts(h, ns, last):
+        for n in ns:
+            c, a, j, r = 256 * h + 32 * n, 128 * (8 * h + n), 128 * (n // 4), 32 * (n % 4)
+            op("t", [("oh", c, c + 32), ("ol", a, a + 128)], [bank("his")],
+               lambda: mm(T.his[r:r + 32, j:j + 128], T.oh[:, c:c + 32], T.ol[:, a:a + 128], False, last and n >= 4), adds=True)
 
     def fetch(t):
         r = (q - t) % N
         at = ls[r][:, 16 * t:16 * t + 16]
-        lsn = ("ls%d" % r, 0, 128)
+        lsn = ("ls%d" % r, 16 * t, 16 * t + 16)
         vop([("ttab", 0, 1024), lsn], [("lf", 0, 256)], lambda: V.tensor_copy(T.lf[:], T.ttab[:].indirect(at)))
         sop([("ttab", 0, 1024), lsn], [("hf", 0, 256)], lambda: S.activation(T.hf[:], T.ttab[:].indirect(at), F.Copy))
-
-    def parts(t):
-        pr = "pk%d" % ((q - t) % N)
-        ps = pk[(q - t) % N][:, P2S:P2S + 16]
-        sop([("hf", 0, 256), cn(32896.5)], [("h2", 0, 256)], lambda: S.activation(T.h2[:], T.hf[:], F.Identity, bias=cc(32896.5)))
-        op("t", [("h2", 0, 256), ("idb", 0, 128)], [("ms", 0, 512)],
-           *[(lambda h=h: mm(T.ms[:, 128 * h:128 * h + 128], T.h2[:, 128 * h:128 * h + 128], T.idb[:], True, True)) for h in range(2)])
-        op("t", [("hf", 0, 256), ("h2", 0, 256), ("idf", 0, 128), ("idq", 0, 128)], [("ms", 0, 512)],
+        sop([("hf", 0, 256), cn(NUM[H0 - 127.5])], [("h2", 0, 256)], lambda: S.activation(T.h2[:], T.hf[:], F.Identity, bias=cx(NUM[H0 - 127.5])))
+        op("t", [("hf", 0, 256), ("h2", 0, 256)] + ID, [bank("ms")],
            lambda: mm(T.ms[:, 256:512], T.idf[:], T.hf[:], True, False),
-           lambda: mm(T.ms[:, 256:512], T.idq[:], T.h2[:], False, True))
-        sop([("ms", 0, 512), cn(144 * LN2)], [("p2", 16, 272)], lambda: S.activation(T.p2[:, 16:272], T.ms[:, 0:256], F.Exp, bias=cc(144 * LN2), scale=-LN2 / 256))
-        if t > 0: sop([(pr, P2S, P2S + 16)], [("p2", 0, 16)], lambda: S.activation(T.p2[:, 0:16], ps, F.Copy))
+           lambda: mm(T.ms[:, 256:512], T.idq[:], T.h2[:], False, True),
+           *[(lambda h=h: mm(T.ms[:, 128 * h:128 * h + 128], T.h2[:, 128 * h:128 * h + 128], T.idb[:], True, True)) for h in range(2 if t else 0)])
+        op("t", [("h2", 0, 256), ("pb%d" % r, SXB, P2S)] + ID, [bank("wd1")],
+           lambda: mm(T.wd1[:, 0:256], T.idb[:], T.h2[:], True, False),
+           lambda: mm(T.wd1[:, 0:256], T.idq[:], pb[r][:, SXB:P2S], False, True))
 
     def low_list():
-        vop([("ms", 0, 512)], [("ll", 0, 256)], lambda: V.tensor_scalar(T.ll[:], T.ms[:, 256:512], 33024.0, None, A.add))
+        vop([bank("ms")], [("ll", 0, 256)], lambda: V.tensor_scalar(T.ll[:], T.ms[:, 256:512], H0, None, A.add))
 
-    def classes(t):
-        pr = "pk%d" % ((q - t) % N)
-        sb = pk[(q - t) % N][:, SXB:SXB + 256]
-        vop([("hf", 0, 256), (pr, SXB, SXB + 256)], [("nm", 0, 256)], lambda: V.tensor_tensor(T.nm[:], T.hf[:], sb, A.is_ge))
+    def parts(t):
+        r = (q - t) % N
+        sop([bank("wd1"), cn(NUM[128.0])], [("nm", 0, 256)], lambda: S.activation(T.nm[:], T.wd1[:, 0:256], F.Sign, bias=cx(NUM[128.0])))
+        sop([bank("ms"), cn(NUM[H0])], [("lob", 0, 256)], lambda: S.activation(T.lob[:], T.ms[:, 256:512], F.Identity, bias=cx(NUM[H0])))
+        if t > 0:
+            sop([bank("ms"), cn(NUM[144 * LN2])], [("p2", 16, 272)],
+                lambda: S.activation(T.p2[:, 16:272], T.ms[:, 0:256], F.Exp, bias=cx(NUM[144 * LN2]), scale=-LN2 / 256))
+            sop([("pb%d" % r, P2S, PBW)], [("p2", 0, 16)], lambda: S.activation(T.p2[:, 0:16], pb[r][:, P2S:PBW], F.Copy))
+
+    def own_keys(b, r, w, stop):
+        return [lambda: mm(b[:, 0:w], T.ones[:], T.cr[:, 0:w], True, False)] + [
+            (lambda h=h, c=c: mm(b[:, 8 * h:8 * h + 8], pb[r][:, c + 128 * h:c + 128 * h + 128], T.s8[:], False, stop and h == 1 and c == SXH))
+            for h in range(2) for c in (SXL, SXH)]
 
     def key_base(t, h):
-        pr = "pk%d" % ((q - t) % N)
-        se = pk[(q - t) % N][:, SELF:SELF + 16]
-        if t > 0 and h == 0: op("t", [(pr, SELF, SELF + 16), ("idf", 0, 128)], [("key0", 0, 512)], lambda: mm(T.key0[:, 0:16], T.idf[:], se, True, True))
-        c = 128 * h
+        r, c = (q - t) % N, 128 * h
         k = key[h][:, 16 - 16 * h:144 - 16 * h]
-        op("t", [("ones", 0, 128), ("cr", 0, 128), ("hf", c, c + 128), ("idn", 0, 128), ("nm", c, c + 128), ("idm", 0, 128)], [("key%d" % h, 0, 512)],
-           lambda: mm(k, T.ones[:, 0:128], T.cr[:], True, False),
-           lambda: mm(k, T.hf[:, c:c + 128], T.idn[:], False, False),
+        first = own_keys(T.key0, r, 144, False) if h == 0 else [lambda: mm(k, T.ones[:], T.cr[:, 16:144], True, False)]
+        op("t", [("ones", 0, 128), ("cr", 0, 144), ("s8", 0, 8), ("pb%d" % r, SXL, SXB), ("h2", c, c + 128), ("lob", c, c + 128), ("nm", c, c + 128)] + ID,
+           [bank("key%d" % h)], *first,
+           lambda: mm(k, T.h2[:, c:c + 128], T.idn[:], False, False),
+           lambda: mm(k, T.lob[:, c:c + 128], T.idn[:], False, False),
            lambda: mm(k, T.nm[:, c:c + 128], T.idm[:], False, False))
 
     def difference(t):
-        pr = "pk%d" % ((q - t) % N)
-        sx = pk[(q - t) % N][:, SX:SX + 256]
-        op("t", [("idf", 0, 128), (pr, SX, SX + 256), ("idp", 0, 128), ("hf", 0, 256)], [("ms", 0, 512)],
-           lambda: mm(T.ms[:, 256:512], T.idf[:], sx, True, False),
-           lambda: mm(T.ms[:, 256:512], T.idp[:], T.hf[:], False, True))
-
-    def like(t, h):
         r = (q - t) % N
-        c = 2048 * h
-        vop([("ptab", 0, 4096), ("lf", 0, 256), ("re%d" % r, 0, 4096)], [("eq", c, c + 2048)],
-            lambda: V.tensor_tensor(T.eq[:, c:c + 2048], T.ptab[:].indirect(T.lf[:, 128 * h:128 * h + 128]), rx[r][:, c:c + 2048], A.is_equal))
+        op("t", [("pb%d" % r, SXL, SXB), ("h2", 0, 256), ("lob", 0, 256)] + ID, [bank("ms")],
+           lambda: mm(T.ms[:, 256:512], T.idb[:], pb[r][:, SXH:SXB], True, False),
+           lambda: mm(T.ms[:, 256:512], T.idq[:], T.h2[:], False, False),
+           lambda: mm(T.ms[:, 256:512], T.idb[:], pb[r][:, SXL:SXH], False, False),
+           lambda: mm(T.ms[:, 256:512], T.idq[:], T.lob[:], False, True))
+
+    def like(t, a, b):
+        r = (q - t) % N
+        vop([("ptab", 0, 4096), ("lf", a, b), ("re%d" % r, 0, 4096)], [("eq", 16 * a, 16 * b)],
+            lambda: V.tensor_tensor(T.eq[:, 16 * a:16 * b], T.ptab[:].indirect(T.lf[:, a:b]), rx[r][:, 16 * a:16 * b], A.is_equal))
 
     def like_sum(h):
         c = 2048 * h
-        op("t", [("eq", c, c + 2048), ("ml", 0, 8)], [("key%d" % h, 0, 512)],
-           *[(lambda p=p: mm(key[h][:, 16 - 16 * h + p:144 - 16 * h:16], T.eq[:, c + p:c + 2048:16], T.ml[:], False, p == 15)) for p in range(16)])
+        op("t", [("eq", c, c + 2048), ("ml", 0, 8)], [bank("key%d" % h)],
+           *[(lambda p=p: mm(key[h][:, 16 - 16 * h + p:144 - 16 * h:16], T.eq[:, c + p:c + 2048:16], T.ml[:], False, p == 15)) for p in range(16)], adds=True)
 
-    def dead(a, b):
-        sop([("tb", 0, 256), ("ll", 0, 256)], [("al", 16 * a, 16 * b)],
-            lambda: S.activation(T.al[:, 16 * a:16 * b], T.tb[:].indirect(T.ll[:, a:b]), F.Sign))
+    def dead(t, a, b):
+        if t == 0:
+            sop([("ptab", 0, 4096), ("lf", a, b), cn(NUM[4096.0])], [("al", 16 * a, 16 * b)],
+                lambda: S.activation(T.al[:, 16 * a:16 * b], T.ptab[:].indirect(T.lf[:, a:b]), F.Sign, bias=cx(NUM[4096.0]), scale=-1.0))
+        else:
+            sop([("tb", 0, 256), ("ll", a, b)], [("al", 16 * a, 16 * b)],
+                lambda: S.activation(T.al[:, 16 * a:16 * b], T.tb[:].indirect(T.ll[:, a:b]), F.Sign))
 
     def dead_too(a, b):
-        vop([("tb", 0, 256), ("ll", 0, 256)], [("al", 16 * a, 16 * b)],
+        vop([("tb", 0, 256), ("ll", a, b)], [("al", 16 * a, 16 * b)],
             lambda: V.tensor_scalar(T.al[:, 16 * a:16 * b], T.tb[:].indirect(T.ll[:, a:b]), 0.0, None, A.is_gt))
-
-    def words(h):
-        c = 2048 * h
-        op("t", [("al", c, c + 2048), ("mw", 0, 8)], [("wd%d" % h, 0, 512)],
-           *[(lambda p=p: mm(wd[h][:, 16 - 16 * h + p:144 - 16 * h:16], T.al[:, c + p:c + 2048:16], T.mw[:], True, True)) for p in range(16)])
 
     def dead_seekers(t):
         r = (q - t) % N
-        vop([("tb", 0, 256), ("ls%d" % r, 0, 128)], [("als", 0, 256)],
-            lambda: V.tensor_scalar(T.als[:], T.tb[:].indirect(ls[r][:, SLO - AT:SLO - AT + 16]), 0.0, None, A.is_gt))
+        sop([("tb", 0, 256), ("ls%d" % r, SLO, SLO + 16)], [("als", 0, 256)],
+            lambda: S.activation(T.als[:], T.tb[:].indirect(ls[r][:, SLO:SLO + 16]), F.Sign))
 
     def seeker_words():
-        op("t", [("als", 0, 256), ("mw", 0, 8)], [("wd0", 0, 512)],
+        op("t", [("als", 0, 256), ("mw", 0, 8)], [bank("wd0")],
            *[(lambda h=h: mm(T.wd0[:, 8 * h:8 * h + 8], T.als[:, 128 * h:128 * h + 128], T.mw[:], True, True)) for h in range(2)])
+
+    def words(t, h):
+        c, w = 2048 * h, "mw" if t else "mo"
+        op("t", [("al", c, c + 2048), (w, 0, 8)], [bank("wd%d" % h)],
+           *[(lambda p=p: mm(wd[h][:, 16 - 16 * h + p:144 - 16 * h:16], T.al[:, c + p:c + 2048:16], T[w][:], True, True)) for p in range(16)])
 
     def decide(t, h):
         a = 0 if h == 0 and t > 0 else 16
         e0, e1 = (a, 144) if h == 0 else (144, 272)
         f0, f1 = (a, 144) if h == 0 else (0, 128)
-        pf = T.mt[:, 256 + a:400] if h == 0 else T.mt[:, 272:400]
-        if h == 0 and t == 0: vop([(po, SELF, SELF + 16)], [("kk", 0, 16)], lambda: V.tensor_copy(T.kk[:, 0:16], own[:, SELF:SELF + 16]))
-        vop([("wd%d" % h, 0, 512), ("p2", e0, e1)], [("y", e0, e1)], lambda: V.tensor_tensor(T.y[:, e0:e1], wd[h][:, f0:f1], T.p2[:, e0:e1], A.mult))
-        vop([("y", e0, e1)], [("ya", e0, e1)], lambda: V.tensor_scalar(T.ya[:, e0:e1], T.y[:, e0:e1], 32768, None, A.bitwise_and))
-        vop([("ya", e0, e1), ("mt", 0, 512)], [("dd", e0, e1)], lambda: V.tensor_tensor(T.dd[:, e0:e1], pf, T.ya[:, e0:e1], A.mult))
-        vop([("key%d" % h, 0, 512), ("dd", e0, e1)], [("kk", e0, e1)], lambda: V.tensor_tensor(T.kk[:, e0:e1], key[h][:, f0:f1], T.dd[:, e0:e1], A.max))
-        src, w, off = "kk", 128, 16
-        for dst in ("m1", "m2", "m3", "m4"):
-            a, b, d = off + h * w, off + h * w + w, h * w // 2
-            vop([(src, a, b)], [(dst, d, d + w // 2)],
-                lambda: V.tensor_tensor(T[dst][:, d:d + w // 2], T[src][:, a:b:2], T[src][:, a + 1:b:2], A.max))
-            src, w, off = dst, w // 2, 0
+        pf = T.mt[:, 256 + a:400]
+        wn = bank("wd%d" % h)
+        if t == 0:
+            vop([wn], [("ya", e0, e1)], lambda: V.tensor_scalar(T.ya[:, e0:e1], wd[h][:, f0:f1], 0.0, 32768.0, A.is_equal, A.mult))
+        else:
+            vop([wn, ("p2", e0, e1)], [("y", e0, e1)], lambda: V.tensor_tensor(T.y[:, e0:e1], wd[h][:, f0:f1], T.p2[:, e0:e1], A.mult))
+            vop([("y", e0, e1)], [("ya", e0, e1)], lambda: V.tensor_scalar(T.ya[:, e0:e1], T.y[:, e0:e1], 32768, None, A.bitwise_and))
+        vop([("ya", e0, e1), bank("mt")], [("dd", e0, e1)], lambda: V.tensor_tensor(T.dd[:, e0:e1], pf, T.ya[:, e0:e1], A.mult))
+        vop([bank("key%d" % h), ("dd", e0, e1)], [("kk", e0, e1)], lambda: V.tensor_tensor(T.kk[:, e0:e1], key[h][:, f0:f1], T.dd[:, e0:e1], A.max))
+        c = 128 * h
+        vop([("r16", 0, 128), ("kk", 16 + c, 144 + c)], [("run", c, c + 128)],
+            lambda: V.tensor_tensor_scan(T.run[:, c:c + 128], T.r16[:], T.kk[:, 16 + c:144 + c], 0.0, A.mult, A.max))
         a = 8 * h
-        vop([("m4", a, a + 8), ("kk", a, a + 8)], [("bi", a, a + 8)], lambda: V.tensor_tensor(T.bi[:, a:a + 8], T.m4[:, a:a + 8], T.kk[:, a:a + 8], A.max))
+        self_key, sn = (T.kk, ("kk", a, a + 8)) if t else (T.key0, bank("key0"))
+        vop([("run", c, c + 128), sn], [("bi", a, a + 8)],
+            lambda: V.tensor_tensor(T.bi[:, a:a + 8], self_key[:, a:a + 8], T.run[:, c + 15:c + 128:16], A.max))
+        digits(h, True)
 
     def codes():
-        vop([("bi", 0, 16)], [("cdi", 0, 16)], lambda: V.tensor_scalar(T.cdi[:], T.bi[:], 31, None, A.bitwise_and))
-        vop([("cdi", 0, 16)], [("cdb", 0, 16)], lambda: V.tensor_copy(T.cdb[:], T.cdi[:]))
-        op("t", [("cdb", 0, 16), ("idb", 0, 128)], [("ms", 0, 512)], lambda: mm(T.ms[0:16, 0:128], T.cdb[:], T.idb[:], True, True))
-        sop([("ms", 0, 512)], [("ct", 0, 128)], lambda: S.activation(T.ct[0:16, :], T.ms[0:16, 0:128], F.Copy))
-        op("t", [("ct", 0, 128), ("ex", 0, 256)], [("mt", 0, 512)],
-           *[(lambda h=h: mm(T.mt[:, 128 * h:128 * h + 128], T.ex[0:16, 128 * h:128 * h + 128], T.ct[0:16, :], True, True)) for h in range(2)])
+        op("t", [("dg", 0, 1536), ID[0]], [bank("ms")],
+           *[(lambda h=h: mm(T.ms[0:8, 128 * h:128 * h + 128], T.dg[:, 768 * h + 512:768 * h + 768:32], T.idb[:], True, True)) for h in range(2)])
+        sop([bank("ms")], [("ct", 0, 256)], lambda: S.activation(T.ct[0:8, :], T.ms[0:8, 0:256], F.Copy))
+
+    def spread_codes():
+        op("t", [("ct", 0, 256), ("ex", 0, 128)], [bank("mt")], lambda: mm(T.mt[:, 0:256], T.ex[0:8, :], T.ct[0:8, :], True, True))
 
     def update(t):
         r = (q - t) % N
-        vop([("mt", 0, 512), ("col", 1, 2)], [("t1", 0, 256)], lambda: V.tensor_scalar(T.t1[:], T.mt[:, 0:256], T.col[:, 1:2], None, A.is_equal))
-        vop([("t1", 0, 256), ("ms", 0, 512)], [("t2", 0, 256)], lambda: V.tensor_tensor(T.t2[:], T.ms[:, 256:512], T.t1[:], A.mult))
-        vop([("t2", 0, 256), ("hf", 0, 256), ("ls%d" % r, 0, 128)], [("ttab", 0, 1024)],
+        vop([bank("mt"), cn(BACK)], [("t1", 0, 256)], lambda: V.tensor_scalar(T.t1[:], T.mt[:, 0:256], cx(BACK), None, A.is_equal))
+        vop([("t1", 0, 256), bank("ms")], [("t2", 0, 256)], lambda: V.tensor_tensor(T.t2[:], T.ms[:, 256:512], T.t1[:], A.mult))
+        vop([("t2", 0, 256), ("hf", 0, 256), ("ls%d" % r, 16 * t, 16 * t + 16)], [("ttab", 0, 1024)],
             lambda: V.tensor_tensor(T.ttab[:].indirect(ls[r][:, 16 * t:16 * t + 16]), T.t2[:], T.hf[:], A.add))
 
     def exchange(t):
         c = 256 * t
-        sop([("his", 0, 512)], [("hb", c, c + 256)], lambda: S.activation(T.hb[:, c:c + 256], T.his[:, 0:256], F.Copy))
+        sop([bank("his")], [("hb", c, c + 256)], lambda: S.activation(T.hb[:, c:c + 256], T.his[:, 0:256], F.Copy))
         o = 256 * (N * t + q)
         send([("hb", c, c + 256)], broadcast(T.hb[:, c:c + 256], T.lh[:, o:o + 256], "h%d_%d" % (t, q)))
         for r in near: arrives([("lh", 256 * (N * t + r), 256 * (N * t + r) + 256)], "h%d_%d" % (t, r), near[r])
 
+    def part(buf, c, first, last):
+        return [(lambda b=b, s=s: mm(T.tm[:, 128 * b:128 * b + 128], T.ma[:, 256 * s + 128 * b:256 * s + 128 * b + 128],
+                                     buf[:, c + 128 * s:c + 128 * s + 128], False, last and b == 1 and s == 1)) for b in range(2) for s in range(2)]
+
+    def merge_own(t):
+        old, on = (T.tb, "tb") if t else (T.zz, "zz")
+        op("t", [(on, 0, 256), ID[0], ("hb", 256 * t, 256 * t + 256), ("ma", 0, 512)], [bank("tm")],
+           lambda: mm(T.tm[:, 0:256], T.idb[:], old[:, 0:256], True, False), *part(T.hb, 256 * t, False, False))
+
     def merge(t):
-        def part(buf, c, last):
-            return [(lambda b=b, s=s: mm(T.tm[:, 128 * b:128 * b + 128], T.ma[:, 256 * s + 128 * b:256 * s + 128 * b + 128],
-                                         buf[:, c + 128 * s:c + 128 * s + 128], False, last and b == 1 and s == 1)) for b in range(2) for s in range(2)]
-        op("t", [("tb", 0, 256), ("idb", 0, 128), ("hb", 256 * t, 256 * t + 256), ("ma", 0, 512)], [("tm", 0, 512)],
-           lambda: mm(T.tm[:, 0:256], T.idb[:], T.tb[:], True, False), *part(T.hb, 256 * t, False))
-        order = sorted(near, key=lambda r: topo.chip(T.cores[r]) != topo.chip(core))
         for r in order:
             c = 256 * (N * t + r)
-            op("t", [("lh", c, c + 256), ("ma", 0, 512)], [("tm", 0, 512)], *part(T.lh, c, r == order[-1]))
+            op("t", [("lh", c, c + 256), ("ma", 0, 512)], [bank("tm")], *part(T.lh, c, False, r == order[-1]), adds=True)
 
-    todo = [((q - d) % N, p) for d in (1, 2, 3) for p in range(16)]
+    def living():
+        c = 1024 * q
+        vop([("ptab", c, c + 1024)], [("nn", 0, 1024)], lambda: V.tensor_scalar(T.nn[:], T.ptab[:, c:c + 1024], 4096.0, None, A.not_equal))
+        for s in range(2):
+            op("t", [("nn", 0, 1024), ("wl", 0, 136)], [bank("key1")],
+               *[(lambda x=x: mm(T.key1[:, 128 * s:128 * s + 128], T.wl[64 * s:64 * s + 64, 7 - x:135 - x],
+                                 T.nn[64 * s:64 * s + 64, 128 * x:128 * x + 128], x == 0, x == 7)) for x in range(8)])
+        vop([bank("key1"), cn(MINE)], [("df", 0, 256)], lambda: V.tensor_scalar(T.df[:], T.key1[:, 0:256], 0.0, cx(MINE), A.is_equal, A.mult))
+        op("t", [("df", 0, 256), ID[0]], [bank("his")], lambda: mm(T.his[:, 0:256], T.idb[:], T.df[:], False, False), adds=True)
 
-    def expand_some(n):
-        for i in range(min(n, len(todo))):
-            r, p = todo.pop(0)
-            expand(r, p, p + 1)
+    def value(r):
+        sop([("pk%d" % r, 0, 256), cn(LOW), cn(HIGH)], [("val", 256 * r, 256 * r + 256)],
+            lambda: S.activation(T.val[:, 256 * r:256 * r + 256], pk[r][:], F.Identity, bias=cx(HIGH), scale=cx(LOW)))
 
-    def living(c):
-        vop([("ptab", 1024 * c, 1024 * c + 1024)], [("nn", 1024 * c, 1024 * c + 1024)],
-            lambda: V.tensor_scalar(T.nn[:, 1024 * c:1024 * c + 1024], T.ptab[:, 1024 * c:1024 * c + 1024], 4096.0, None, A.not_equal))
-        op("t", [("nn", 1024 * c, 1024 * c + 1024), ("wc", 0, 144)], [("tm", 0, 512)],
-           *[(lambda x=x: mm(T.tm[:, 0:256], T.wc[:, 15 - x:143 - x], T.nn[:, 256 * x:256 * x + 256], x == 0, x == 15)) for x in range(4 * c, 4 * c + 4)])
-
-    clear_hist()
-    vop([(po, SELF, SELF + 16)], [("si", 0, 16)], lambda: V.tensor_copy(T.si[:], own[:, SELF:SELF + 16]))
-    for h in range(2): histogram(h, "si", T.si, -1, False, 4)
-    package()
-    for c in range(3): living(c)
     fetch(0)
-    parts(0)
-    living(3)
-    low_list()
-    vop([("tm", 0, 512)], [("tb", 0, 256)], lambda: V.tensor_scalar(T.tb[:], T.tm[:, 0:256], 0.0, None, A.is_equal))
+    op("t", [("ones", 0, 128), ("cr", 0, 144), ("s8", 0, 8), (bo, SXL, SXB)], [bank("wd0")], *own_keys(T.wd0, q, 16, True))
+    clear_hist()
+    vop([bank("wd0")], [("bi", 0, 16)], lambda: V.tensor_copy(T.bi[:], T.wd0[:, 0:16]))
+    for h in range(2):
+        digits(h, False)
+        one_hots(h, -1.0, 8)
+        counts(h, range(8), False)
+    living()
 
     for t in range(RO):
-        cut = 128 if t == 0 else CUT
-        dead(0, cut)
-        dead(128, 256)
-        if t == 0:
-            like(t, 0)
-            classes(t)
-        key_base(t, 0)
-        like_sum(0)
-        key_base(t, 1)
-        like(t, 1)
-        like_sum(1)
         if t > 0:
+            like(t, 0, 64)
+            low_list()
+        parts(t)
+        if t > 0:
+            if t < 3: expand("s", (q - t - 1) % N, range(SPREAD[t], 16))
+            else:
+                for r in ([0, 1], [2], [3])[t - 3]: value(r)
+            merge(t - 1)
+            sop([bank("tm")], [("tb", 0, 256)], lambda: S.activation(T.tb[:], T.tm[:, 0:256], F.Copy))
             dead_seekers(t)
-            dead_too(cut, 128)
-            seeker_words()
-        words(0)
-        words(1)
+        key_base(t, 0)
+        key_base(t, 1)
         difference(t)
-        expand_some(16 if t == 0 else 6)
-        if t > 0: clear_hist()
+        dead(t, 0, 128)
+        like(t, 64 if t else 0, 128)
+        like_sum(0)
+        if t > 0:
+            clear_hist()
+            seeker_words()
+        words(t, 0)
+        like(t, 128, 256)
+        like_sum(1)
+        dead(t, 128, CUT if t else 256)
+        if t > 0: dead_too(CUT, 256)
+        else: expand("s", (q - 1) % N, range(SPREAD[0], 16))
         decide(t, 0)
-        histogram(0, "bi", T.bi, 1, False, 8 if t == 0 else SHARE[0])
+        if t == 0: words(t, 1)
+        one_hots(0, 1.0, 8)
+        counts(0, range(8), False)
+        if t > 0: words(t, 1)
         decide(t, 1)
         codes()
-        histogram(1, "bi", T.bi, 1, True, 8 if t == 0 else SHARE[1])
+        one_hots(1, 1.0, SHARE)
+        counts(1, range(3), False)
+        spread_codes()
+        counts(1, range(3, 8), True)
         exchange(t)
+        if t < 2: expand("g", (q - t - 2) % N, range(SPREAD[t + 1]))
         update(t)
-        if t < 3: lists((q - t - 1) % N)
-        if t + 1 < RO:
-            fetch(t + 1)
-            parts(t + 1)
-            like(t + 1, 0)
-            low_list()
-            classes(t + 1)
-            expand_some(11)
-        else:
-            dma("y", [("ttab", 0, 1024)], [], T.yt[:], T.ttab[:])
-            for r in range(N):
-                pr = "pk%d" % r
-                vop([(pr, 0, 256), ("col", 2, 4)], [("val", 256 * r, 256 * r + 256)],
-                    lambda: V.tensor_scalar(T.val[:, 256 * r:256 * r + 256], pk[r][:, 0:256], T.col[:, 2:3], T.col[:, 3:4], A.mult, A.add))
-                vop([("val", 256 * r, 256 * r + 256), ("ls%d" % r, 0, 128)], [("ptab", 0, 4096)],
-                    lambda: V.tensor_copy(T.ptab[:].indirect(ls[r][:, CL - AT:CL - AT + 16]), T.val[:, 256 * r:256 * r + 256]))
-        merge(t)
-        if t + 1 < RO: sop([("tm", 0, 512)], [("tb", 0, 256)], lambda: S.activation(T.tb[:], T.tm[:, 0:256], F.Copy))
+        merge_own(t)
+        if t + 1 < RO: fetch(t + 1)
 
-    vop([("tm", 0, 512)], [("tq", 0, 256)], lambda: V.tensor_scalar(T.tq[:], T.tm[:, 0:256], 1.0, 4096.0, A.min, A.mult))
+    dma("y", [("ttab", 0, 1024)], [], T.yt[:], T.ttab[:])
+    for r in range(N):
+        vop([("val", 256 * r, 256 * r + 256), ("ls%d" % r, CL, CL + 16)], [("ptab", 0, 4096)],
+            lambda: V.tensor_copy(T.ptab[:].indirect(ls[r][:, CL:CL + 16]), T.val[:, 256 * r:256 * r + 256]))
+    merge(RO - 1)
+    vop([bank("tm")], [("tq", 0, 256)], lambda: V.tensor_scalar(T.tq[:], T.tm[:, 0:256], 1.0, 4096.0, A.min, A.mult))
     for h in range(2):
-        op("t", [("tq", 0, 256), ("rb", 0, 2048)], [("wd%d" % h, 0, 512)],
+        op("t", [("tq", 0, 256), ("rb", 0, 2048)], [bank("wd%d" % h)],
            *[(lambda x=x: mm(wd[h][:, 256 * x:256 * x + 256], T.rb[:, 128 * (4 * q + 2 * h + x):128 * (4 * q + 2 * h + x) + 128], T.tq[:], True, True)) for x in range(2)])
         c = 1024 * q + 512 * h
-        vop([("wd%d" % h, 0, 512), ("ptab", c, c + 512)], [("out", 512 * h, 512 * h + 512)],
+        vop([bank("wd%d" % h), ("ptab", c, c + 512)], [("out", 512 * h, 512 * h + 512)],
             lambda: V.tensor_tensor(T.out[:, 512 * h:512 * h + 512], wd[h][:], T.ptab[:, c:c + 512], A.max))
-        dma("y", [("out", 512 * h, 512 * h + 512)], [], T.yp[:, 512 * h:512 * h + 512], T.out[:, 512 * h:512 * h + 512])
+        dma("ys"[h], [("out", 512 * h, 512 * h + 512)], [], T.yp[:, 512 * h:512 * h + 512], T.out[:, 512 * h:512 * h + 512])
     g.wait_ge(T.sem.sent, sent[0])
     finish()

@@ -4,9 +4,10 @@ from concourse.bass import DstId, RemoteDMATransfer
 from concourse.mybir import AluOpType as A, ActivationFunctionType as F
 
 N, RO, K = 4, 6, 256
-CUT = 240
-SHARE = 6
-SPREAD = (10, 13, 13)
+LEAD = 2
+CUT = 192
+SHARE = 13
+SPREAD = (8, 11, 11)
 LN2 = math.log(2.0)
 H0 = 33024.0
 SXL, SXH, SXB, P2S, PBW = 0, 256, 512, 768, 784
@@ -18,14 +19,14 @@ SCRATCH = {
     "nn": ("sbuf", [128, 1024], "bfloat16"), "eq": ("sbuf", [128, 4096], "bfloat16"), "al": ("sbuf", [128, 4096], "bfloat16"),
     "als": ("sbuf", [128, 256], "bfloat16"), "tb": ("sbuf", [128, 256], "bfloat16"), "tq": ("sbuf", [128, 256], "bfloat16"),
     "hb": ("sbuf", [128, RO * 256], "bfloat16"), "lh": ("sbuf", [128, RO * N * 256], "bfloat16"),
-    "ones": ("sbuf", [128, 128], "bfloat16"), "zz": ("sbuf", [128, 512], "bfloat16"), "rb": ("sbuf", [128, 2048], "bfloat16"),
+    "ones": ("sbuf", [128, 128], "bfloat16"), "zz": ("sbuf", [128, 256], "bfloat16"), "rb": ("sbuf", [128, 2048], "bfloat16"),
     "cnt": ("sbuf", [128, 256], "bfloat16"), "ig": ("sbuf", [128, 128], "bfloat16"), "prow": ("sbuf", [128, 128], "bfloat16"),
     "clo": ("sbuf", [128, 128], "bfloat16"),
     "idb": ("sbuf", [128, 128], "bfloat16"), "idf": ("sbuf", [128, 128], "float32"), "idq": ("sbuf", [128, 128], "bfloat16"),
     "idn": ("sbuf", [128, 128], "bfloat16"), "idm": ("sbuf", [128, 128], "bfloat16"),
     "mw": ("sbuf", [128, 8], "bfloat16"), "ml": ("sbuf", [128, 8], "bfloat16"), "mo": ("sbuf", [128, 8], "bfloat16"),
-    "s8": ("sbuf", [128, 8], "bfloat16"), "ma": ("sbuf", [128, 512], "bfloat16"), "ex": ("sbuf", [128, 128], "bfloat16"),
-    "prn": ("sbuf", [128, 512], "float32"), "cr": ("sbuf", [128, 144], "bfloat16"), "wl": ("sbuf", [128, 136], "bfloat16"),
+    "s8": ("sbuf", [128, 8], "bfloat16"), "ex": ("sbuf", [128, 128], "bfloat16"),
+    "prn": ("sbuf", [128, 512], "float32"), "cr": ("sbuf", [128, 144], "bfloat16"),
     "r16": ("sbuf", [128, 128], "bfloat16"), "r32": ("sbuf", [128, 256], "bfloat16"),
     "rwi": ("sbuf", [128, 8], "int32"), "col": ("sbuf", [128, 32], "float32"), "pwb": ("sbuf", [128, 8], "bfloat16"),
     "ci": ("sbuf", [128, 48], "int32"), "cb": ("sbuf", [128, 48], "bfloat16"), "tr": ("sbuf", [128, 256], "float32"),
@@ -67,15 +68,12 @@ def scheduler(g, T):
             for a, b in known.items():
                 if seen[qn].get(a, 0) < b: seen[qn][a] = b
 
-    def needs(reads, writes):
+    def needs(reads, writes, me=None):
         need = {}
-        reads, writes = list(reads), list(writes)
-        writes += [r for r in reads if r[0] in PSUM]
-        span = [(w[0], 0, 512) if w[0] in PSUM else w for w in writes]
-        for acc, wr in [(r, False) for r in reads if r[0] not in PSUM] + [(w, True) for w in span]:
+        for acc, wr in [(r, False) for r in reads] + [(w, True) for w in writes]:
             for lo, hi, w, s, n in log.get(acc[0], []):
-                if lo < acc[2] and acc[1] < hi and (w or wr): need[s] = max(need.get(s, 0), n)
-        return need, [r for r in reads if r[0] not in PSUM], span
+                if lo < acc[2] and acc[1] < hi and (w or wr or (acc[0] in PSUM and s != me)): need[s] = max(need.get(s, 0), n)
+        return need, list(reads), list(writes)
 
     def record(reads, writes, s, n):
         for b, lo, hi in writes:
@@ -84,7 +82,7 @@ def scheduler(g, T):
             log[b] = [e for e in log.get(b, []) if e[2] or e[3] != s or not (lo <= e[0] and e[1] <= hi)] + [(lo, hi, False, s, n)]
 
     def op(qn, reads, writes, *fns, adds=False):
-        need, rd, wr = needs(reads, writes)
+        need, rd, wr = needs(reads, writes, "c" + qn)
         if adds: need.pop("ct", None)
         wait(qn, need)
         for f in fns: ins = f()
@@ -175,7 +173,7 @@ def rank_program(g, core, T, topo):
 
     def where(dst, w, pattern, fill):
         op("g", [("zz", 0, w)], [(dst, 0, w)], lambda: g.affine_select(T[dst][:, 0:w], T.zz[:, 0:w], pattern, A.not_equal, fill, 0, 1))
-    PART, PP, P48, P24, P16, G16, PART16, Y0, Y1, BACK, WL, MINE, LOW, HIGH = range(14)
+    PART, PP, P16, G16, PART16, Y0, Y1, BACK, LOW, HIGH = range(10)
     NUM = {144 * LN2: 16, H0 - 127.5: 17, 1.0: 18, H0: 19, 128.0: 20, 4096.0: 21}
 
     def cx(i): return T.col[:, i:i + 1]
@@ -191,41 +189,38 @@ def rank_program(g, core, T, topo):
     iota("cnt", 256, [[1, 256]], 0, 0)
     iota("ig", 128, [[16, 8], [0, 16]], 0, 0)
     iota("prow", 128, [[0, 8], [-1, 16]], 15, 0)
-    vop([], [("zz", 0, 512)], lambda: V.memset(T.zz[:], 0.0))
-    vop([], [("ones", 0, 128)], lambda: V.memset(T.ones[:], 1.0))
-    for x, i in NUM.items(): vop([], [cn(i)], lambda: V.memset(cx(i), x))
-    vop([], [("dg", 0, 1536)], lambda: V.memset(T.dg[:], 1.0))
-    for b, w, step in (("r16", 128, 16), ("r32", 256, 32)):
-        vop([], [(b, 0, w)], lambda: V.memset(T[b][:], 1.0))
-        vop([], [(b, 0, w)], lambda: V.memset(T[b][:, 0::step], 0.0))
-    vop([], [("cr", 0, 144)], lambda: V.memset(T.cr[:], 0.0))
-    for row, a, b in ((0, -16.0, None), (32, 1179648.0, -786432.0), (64, 8192.0, 8160.0)):
-        vop([], [("cr", 0, 16)], lambda: V.memset(T.cr[row:row + 1, 0:16], a))
-        if b: vop([], [("cr", 16, 144)], lambda: V.memset(T.cr[row:row + 1, 16:144], b))
-    for i, m in ((PP, 15), (P48, 48), (P24, 24), (P16, 16), (G16, 112)):
+    vop([], [("zz", 0, 256)], lambda: V.memset(T.zz[:], 0.0))
+    for i, m in ((PP, 15), (P16, 16), (G16, 112)):
         vop([("rwi", 0, 1)], [("rwi", i, i + 1)], lambda: V.tensor_scalar(T.rwi[:, i:i + 1], T.rwi[:, 0:1], m, None, A.bitwise_and))
-    vop([("rwi", 0, 6)], [("col", 0, 6)], lambda: V.tensor_copy(T.col[:, 0:6], T.rwi[:, 0:6]))
+    vop([], [("cr", 0, 144)], lambda: V.memset(T.cr[:], 0.0))
+    vop([("rwi", 0, 4)], [("col", 0, 4)], lambda: V.tensor_copy(T.col[:, 0:4], T.rwi[:, 0:4]))
+    sop([cn(PP)], [("pwb", 0, 1)], lambda: S.activation(T.pwb[:, 0:1], cx(PP), F.Exp, scale=LN2))
+    scans = (("r16", 128, 16), ("r32", 256, 32))
+    for b, w, step in scans: vop([], [(b, 0, w)], lambda: V.memset(T[b][:], 1.0))
     column(PART16, PART, 16.0, None, A.add)
     column(Y0, P16, 0.0, None, A.is_equal)
     column(Y1, P16, 16.0, None, A.is_equal)
-    sop([cn(PP)], [("pwb", 0, 1)], lambda: S.activation(T.pwb[:, 0:1], cx(PP), F.Exp, scale=LN2))
+    for b, w, step in scans: vop([], [(b, 0, w)], lambda: V.memset(T[b][:, 0::step], 0.0))
+    for row, a, b in ((0, -16.0, None), (32, 1179648.0, -786432.0), (64, 8192.0, 8160.0)):
+        vop([("cr", 0, 144)], [("cr", 200 + row, 201 + row)], lambda: V.memset(T.cr[row:row + 1, 0:16], a))
+        if b: vop([("cr", 0, 144)], [("cr", 201 + row, 202 + row)], lambda: V.memset(T.cr[row:row + 1, 16:144], b))
+    CR = ("cr", 0, 300)
     CNT, IG = ("cnt", 0, 256), ("ig", 0, 128)
+    for y in range(2):
+        for b in range(2):
+            s, c = 16 - 16 * (b - y), 256 * y + 128 * b
+            match("prn", c, c + 128, CNT, T.cnt[:, s:s + 128], PART16, cx(Y0 + y), A.mult, reads=[cn(Y0 + y)])
 
     ci, cb, ati = T.ci, T.cb, T.ati
     own, po, mine, bo, lo_ = pk[q], "pk%d" % q, pb[q], "pb%d" % q, "ls%d" % q
     vop([("rin", 0, 256)], [(po, 0, 256)], lambda: V.tensor_copy(own[:], T.rin[:]))
     vop([(po, 0, 256)], [("tr", 0, 256)], lambda: V.transpose(T.tr[:], own[:]))
     tell("pk", 256)
-    for y in range(2):
-        for b in range(2):
-            s, c = 16 - 16 * (b - y), 256 * y + 128 * b
-            match("prn", c, c + 128, CNT, T.cnt[:, s:s + 128], PART16, cx(Y0 + y), A.mult, reads=[cn(Y0 + y)])
     where("idb", 128, [[-1, 128]], 1.0)
     where("idq", 128, [[-1, 128]], -1.0)
     where("idn", 128, [[-1, 128]], -32.0)
     where("idm", 128, [[-1, 128]], -2097152.0)
     where("ex", 128, [[-1, 8], [0, 16]], 1.0)
-    where("ma", 512, [[128, 2], [-1, 2], [-2, 128]], 1.0)
 
     def expand(qn, r, ps):
         for p in ps:
@@ -245,7 +240,8 @@ def rank_program(g, core, T, topo):
         vop([("ati", a, b)], [("ati", 96 + a, 96 + b)], lambda: V.tensor_scalar(ati[:, 96 + a:96 + b], ati[:, a:b], 1023, None, A.bitwise_and))
         vop([("ati", 96 + a, 96 + b)], [(lo_, a, b)], lambda: V.tensor_copy(ls[q][:, a:b], ati[:, 96 + a:96 + b]))
     opened("wd0", [0])
-    opened("tm", [1, 2, 3, 4, 5])
+    vop([], [("ones", 0, 128)], lambda: V.memset(T.ones[:], 1.0))
+    for x, i in NUM.items(): vop([], [cn(i)], lambda: V.memset(cx(i), x))
     for i, m in ((0, 255), (1, 3840), (2, 3072)):
         vop([("cin", 0, 16)], [("ci", 16 * i, 16 * i + 16)], lambda: V.tensor_scalar(ci[:, 16 * i:16 * i + 16], T.cin[:], m, None, A.bitwise_and))
     vop([("ci", 0, 16)], [("cb", 0, 16)], lambda: V.tensor_copy(cb[:, 0:16], ci[:, 0:16]))
@@ -258,6 +254,8 @@ def rank_program(g, core, T, topo):
     op("t", [("cb", 32, 48), ("rb", 0, 2048)], [bank("mt")],
        *[(lambda x=x: mm(T.mt[:, x:256:16], T.rb[:, 128 * x:128 * x + 128], cb[:, 32:48], True, True)) for x in range(16)])
     opened_lists("wd0", [0])
+    match("s8", 0, 8, IG, T.ig[:, 0::16], PART, -32.0, A.mult)
+    vop([("prow", 0, 128), ("cr", 0, 144)], [("cr", 201, 202)], lambda: V.tensor_copy(T.cr[0:1, 16:144], T.prow[0:1, :]))
     vop([("tin", 0, 1024)], [("ttab", 0, 1024)], lambda: V.tensor_copy(T.ttab[:], T.tin[:]))
     sop([bank("ms")], [(bo, SXL, SXB)], lambda: S.activation(mine[:, SXL:SXB], T.ms[:], F.Copy))
     sop([bank("mt")], [(bo, SXB, P2S)], lambda: S.activation(mine[:, SXB:P2S], T.mt[:, 0:256], F.Copy))
@@ -266,64 +264,66 @@ def rank_program(g, core, T, topo):
     sop([bank("wd1"), cn(NUM[144 * LN2])], [(bo, P2S, PBW)],
         lambda: S.activation(mine[:, P2S:PBW], T.wd1[:, 0:16], F.Exp, bias=cx(NUM[144 * LN2]), scale=-LN2 / 256))
     expand("s", q, range(8, 16))
-    opened_lists("tm", [1, 2, 3, 4, 5])
+
+    def own_keys(b, r, w, stop):
+        return [lambda: mm(b[:, 0:w], T.ones[:], T.cr[:, 0:w], True, False)] + [
+            (lambda h=h, c=c: mm(b[:, 8 * h:8 * h + 8], pb[r][:, c + 128 * h:c + 128 * h + 128], T.s8[:], False, stop and h == 1 and c == SXH))
+            for h in range(2) for c in (SXL, SXH)]
+    op("t", [("ones", 0, 128), CR, ("s8", 0, 8), (bo, SXL, SXB)], [bank("key0")], *own_keys(T.key0, q, 16, True))
+    opened("tm", [1, 2, 3, 4, 5])
     vop([("cin", 0, 16)], [(lo_, CL, CL + 16)], lambda: V.tensor_copy(ls[q][:, CL:CL + 16], T.cin[:]))
     vop([("ci", 0, 16)], [(lo_, SLO, SLO + 16)], lambda: V.tensor_copy(ls[q][:, SLO:SLO + 16], ci[:, 0:16]))
     tell("pb", PBW)
-    tell("ls", 128)
-    expand("g", (q - 1) % N, range(SPREAD[0]))
+    vop([], [("dg", 0, 512)], lambda: V.memset(T.dg[:, 0:512], 1.0))
     match("idf", 0, 128, CNT, T.cnt[:, 0:128], PART, None)
-    match("s8", 0, 8, IG, T.ig[:, 0::16], PART, -32.0, A.mult)
     match("mo", 0, 8, IG, T.ig[:, 0::16], G16, None)
     match("ml", 0, 8, IG, T.ig[:, 0::16], G16, 131072.0, A.mult)
     vop([("mo", 0, 8), ("pwb", 0, 1)], [("mw", 0, 8)], lambda: V.tensor_scalar(T.mw[:], T.mo[:], T.pwb[:, 0:1], None, A.mult))
     vop([CNT], [("clo", 0, 128)], lambda: V.tensor_scalar(T.clo[:], T.cnt[:, 0:128], -1.0, 127.0, A.mult, A.add))
-    vop([("prow", 0, 128)], [("cr", 16, 144)], lambda: V.tensor_copy(T.cr[0:1, 16:144], T.prow[0:1, :]))
     column(BACK, PP, -1.0, 15.0, A.mult, A.add)
-    column(WL, P48, 2.0, 8.0 * q + 7, A.mult, A.add)
-    column(MINE, P24, 8.0 * q, None, A.is_equal)
     column(LOW, PP, float(RO), None, A.is_lt)
     column(HIGH, PP, float(RO), 4096.0, A.is_ge, A.mult)
-    match("wl", 0, 136, CNT, T.cnt[:, 0:136], WL, None)
     vop([], [bank("mt")], lambda: V.memset(T.mt[:, 256:272], (8388608.0 + 16) / 32768))
     vop([("prow", 0, 128)], [bank("mt")], lambda: V.tensor_scalar(T.mt[:, 272:400], T.prow[:], 1.0 / 32768, 128.0, A.mult, A.add))
 
     def clear_hist():
         op("t", [("ones", 0, 128), ("zz", 0, 256)], [bank("his")], lambda: mm(T.his[:, 0:256], T.ones[:], T.zz[:, 0:256], True, False))
 
-    def digits(h, codes):
-        o, d, n = 24 * h, 768 * h, 24 if codes else 16
-        src, sn = T.bi[:, 8 * h:8 * h + 8], ("bi", 8 * h, 8 * h + 8)
-        vop([sn], [("hl", o, o + 8)], lambda: V.tensor_scalar(T.hl[:, o:o + 8], src, 12, 0xC1F, A.logical_shift_right, A.bitwise_and))
-        vop([sn], [("hl", o + 8, o + 16)], lambda: V.tensor_scalar(T.hl[:, o + 8:o + 16], src, 5, 127, A.logical_shift_right, A.bitwise_and))
-        if codes: vop([sn], [("hl", o + 16, o + 24)], lambda: V.tensor_scalar(T.hl[:, o + 16:o + 24], src, 31, None, A.bitwise_and))
-        vop([("hl", o, o + n)], [("dg", d, d + 32 * n)], lambda: V.tensor_copy(T.dg[:, d:d + 32 * n:32], T.hl[:, o:o + n]))
+    def digits(codes):
+        n, sn = 48 if codes else 32, ("bi", 0, 16)
+        vop([sn], [("hl", 0, 16)], lambda: V.tensor_scalar(T.hl[:, 0:16], T.bi[:], 12, 0xC1F, A.logical_shift_right, A.bitwise_and))
+        vop([sn], [("hl", 16, 32)], lambda: V.tensor_scalar(T.hl[:, 16:32], T.bi[:], 5, 127, A.logical_shift_right, A.bitwise_and))
+        if codes: vop([sn], [("hl", 32, 48)], lambda: V.tensor_scalar(T.hl[:, 32:48], T.bi[:], 31, None, A.bitwise_and))
+        vop([("hl", 0, n)], [("dg", 0, 32 * n)], lambda: V.tensor_copy(T.dg[:, 0:32 * n:32], T.hl[:, 0:n]))
 
-    def one_hots(h, sign, share):
-        d, c = 768 * h, 256 * h
-        low = [T.dg[:, d + 256 + 32 * n:d + 257 + 32 * n] for n in range(8)]
-        for n in range(share, 8):
+    def one_hots(sign, share, between=None):
+        low = [T.dg[:, 512 + 32 * n:513 + 32 * n] for n in range(16)]
+        for n in range(share, 16):
             a = 128 * (n - share)
-            sop([("clo", 0, 128), ("dg", d + 256, d + 512)], [("ab", a, a + 128)],
+            sop([("clo", 0, 128), ("dg", 512, 1024)], [("ab", a, a + 128)],
                 lambda: S.activation(T.ab[:, a:a + 128], T.clo[:], F.Abs, bias=low[n], scale=-1.0))
-        if share < 8:
-            e, w = 1024 * h + 1024, 128 * (8 - share)
-            sop([("ab", 0, w), cn(NUM[1.0])], [("ol", e - w, e)],
-                lambda: S.activation(T.ol[:, e - w:e], T.ab[:, 0:w], F.Relu, bias=cx(NUM[1.0]), scale=-1.0))
-        vop([("r32", 0, 256), ("dg", d, d + 256)], [("up", c, c + 256)],
-            lambda: V.tensor_tensor_scan(T.up[:, c:c + 256], T.r32[:], T.dg[:, d:d + 256], 0.0, A.mult, A.add))
-        vop([("up", c, c + 256)], [("oh", c, c + 256)],
-            lambda: V.tensor_scalar(T.oh[:, c:c + 256], T.up[:, c:c + 256], 31.0, sign, A.is_equal, A.mult))
+        if between: between()
+        if share < 16:
+            w = 128 * (16 - share)
+            sop([("ab", 0, w), cn(NUM[1.0])], [("ol", 2048 - w, 2048)],
+                lambda: S.activation(T.ol[:, 2048 - w:2048], T.ab[:, 0:w], F.Relu, bias=cx(NUM[1.0]), scale=-1.0))
+        for c in (0, 256):
+            vop([("r32", 0, 256), ("dg", c, c + 256)], [("up", c, c + 256)],
+                lambda: V.tensor_tensor_scan(T.up[:, c:c + 256], T.r32[:], T.dg[:, c:c + 256], 0.0, A.mult, A.add))
         for n in range(share):
-            a = 128 * (8 * h + n)
-            vop([("clo", 0, 128), ("dg", d + 256, d + 512)], [("ol", a, a + 128)],
+            a = 128 * n
+            vop([("clo", 0, 128), ("dg", 512, 1024)], [("ol", a, a + 128)],
                 lambda: V.tensor_scalar(T.ol[:, a:a + 128], T.clo[:], low[n], None, A.is_equal))
+            if n < 2:
+                c = 256 * n
+                vop([("up", c, c + 256)], [("oh", c, c + 256)],
+                    lambda: V.tensor_scalar(T.oh[:, c:c + 256], T.up[:, c:c + 256], 31.0, sign, A.is_equal, A.mult))
 
-    def counts(h, ns, last):
+    def counts(ns, last):
         for n in ns:
-            c, a, j, r = 256 * h + 32 * n, 128 * (8 * h + n), 128 * (n // 4), 32 * (n % 4)
+            c, a, j = 32 * n, 128 * n, 32 * (n % 8)
             op("t", [("oh", c, c + 32), ("ol", a, a + 128)], [bank("his")],
-               lambda: mm(T.his[r:r + 32, j:j + 128], T.oh[:, c:c + 32], T.ol[:, a:a + 128], False, last and n >= 4), adds=True)
+               lambda: mm(T.his[:, j:j + 32], T.ol[:, a:a + 128], T.oh[:, c:c + 32], False, last and n == 15), adds=True)
 
     def fetch(t):
         r = (q - t) % N
@@ -352,16 +352,11 @@ def rank_program(g, core, T, topo):
                 lambda: S.activation(T.p2[:, 16:272], T.ms[:, 0:256], F.Exp, bias=cx(NUM[144 * LN2]), scale=-LN2 / 256))
             sop([("pb%d" % r, P2S, PBW)], [("p2", 0, 16)], lambda: S.activation(T.p2[:, 0:16], pb[r][:, P2S:PBW], F.Copy))
 
-    def own_keys(b, r, w, stop):
-        return [lambda: mm(b[:, 0:w], T.ones[:], T.cr[:, 0:w], True, False)] + [
-            (lambda h=h, c=c: mm(b[:, 8 * h:8 * h + 8], pb[r][:, c + 128 * h:c + 128 * h + 128], T.s8[:], False, stop and h == 1 and c == SXH))
-            for h in range(2) for c in (SXL, SXH)]
-
     def key_base(t, h):
         r, c = (q - t) % N, 128 * h
         k = key[h][:, 16 - 16 * h:144 - 16 * h]
         first = own_keys(T.key0, r, 144, False) if h == 0 else [lambda: mm(k, T.ones[:], T.cr[:, 16:144], True, False)]
-        op("t", [("ones", 0, 128), ("cr", 0, 144), ("s8", 0, 8), ("pb%d" % r, SXL, SXB), ("h2", c, c + 128), ("lob", c, c + 128), ("nm", c, c + 128)] + ID,
+        op("t", [("ones", 0, 128), CR, ("s8", 0, 8), ("pb%d" % r, SXL, SXB), ("h2", c, c + 128), ("lob", c, c + 128), ("nm", c, c + 128)] + ID,
            [bank("key%d" % h)], *first,
            lambda: mm(k, T.h2[:, c:c + 128], T.idn[:], False, False),
            lambda: mm(k, T.lob[:, c:c + 128], T.idn[:], False, False),
@@ -416,26 +411,31 @@ def rank_program(g, core, T, topo):
         e0, e1 = (a, 144) if h == 0 else (144, 272)
         f0, f1 = (a, 144) if h == 0 else (0, 128)
         pf = T.mt[:, 256 + a:400]
-        wn = bank("wd%d" % h)
+        wn, c = bank("wd%d" % h), 128 * h
         if t == 0:
-            vop([wn], [("ya", e0, e1)], lambda: V.tensor_scalar(T.ya[:, e0:e1], wd[h][:, f0:f1], 0.0, 32768.0, A.is_equal, A.mult))
+            steps = [lambda: vop([wn], [("ya", e0, e1)], lambda: V.tensor_scalar(T.ya[:, e0:e1], wd[h][:, f0:f1], 0.0, 32768.0, A.is_equal, A.mult))]
         else:
-            vop([wn, ("p2", e0, e1)], [("y", e0, e1)], lambda: V.tensor_tensor(T.y[:, e0:e1], wd[h][:, f0:f1], T.p2[:, e0:e1], A.mult))
-            vop([("y", e0, e1)], [("ya", e0, e1)], lambda: V.tensor_scalar(T.ya[:, e0:e1], T.y[:, e0:e1], 32768, None, A.bitwise_and))
-        vop([("ya", e0, e1), bank("mt")], [("dd", e0, e1)], lambda: V.tensor_tensor(T.dd[:, e0:e1], pf, T.ya[:, e0:e1], A.mult))
-        vop([bank("key%d" % h), ("dd", e0, e1)], [("kk", e0, e1)], lambda: V.tensor_tensor(T.kk[:, e0:e1], key[h][:, f0:f1], T.dd[:, e0:e1], A.max))
-        c = 128 * h
-        vop([("r16", 0, 128), ("kk", 16 + c, 144 + c)], [("run", c, c + 128)],
-            lambda: V.tensor_tensor_scan(T.run[:, c:c + 128], T.r16[:], T.kk[:, 16 + c:144 + c], 0.0, A.mult, A.max))
-        a = 8 * h
-        self_key, sn = (T.kk, ("kk", a, a + 8)) if t else (T.key0, bank("key0"))
-        vop([("run", c, c + 128), sn], [("bi", a, a + 8)],
-            lambda: V.tensor_tensor(T.bi[:, a:a + 8], self_key[:, a:a + 8], T.run[:, c + 15:c + 128:16], A.max))
-        digits(h, True)
+            steps = [lambda: vop([wn, ("p2", e0, e1)], [("y", e0, e1)], lambda: V.tensor_tensor(T.y[:, e0:e1], wd[h][:, f0:f1], T.p2[:, e0:e1], A.mult)),
+                     lambda: vop([("y", e0, e1)], [("ya", e0, e1)], lambda: V.tensor_scalar(T.ya[:, e0:e1], T.y[:, e0:e1], 32768, None, A.bitwise_and))]
+        return steps + [
+            lambda: vop([("ya", e0, e1), bank("mt")], [("dd", e0, e1)], lambda: V.tensor_tensor(T.dd[:, e0:e1], pf, T.ya[:, e0:e1], A.mult)),
+            lambda: vop([bank("key%d" % h), ("dd", e0, e1)], [("kk", e0, e1)], lambda: V.tensor_tensor(T.kk[:, e0:e1], key[h][:, f0:f1], T.dd[:, e0:e1], A.max)),
+            lambda: vop([("r16", 0, 128), ("kk", 16 + c, 144 + c)], [("run", c, c + 128)],
+                        lambda: V.tensor_tensor_scan(T.run[:, c:c + 128], T.r16[:], T.kk[:, 16 + c:144 + c], 0.0, A.mult, A.max))]
+
+    def best(t):
+        a, b = decide(t, 0), decide(t, 1)
+        for i in range(LEAD): a.pop(0)()
+        for x, y in zip(a + [None] * LEAD, b):
+            if x: x()
+            y()
+        self_key, sn = (T.kk, ("kk", 0, 16)) if t else (T.key0, bank("key0"))
+        vop([("run", 0, 256), sn], [("bi", 0, 16)], lambda: V.tensor_tensor(T.bi[:], self_key[:, 0:16], T.run[:, 15::16], A.max))
+        digits(True)
 
     def codes():
-        op("t", [("dg", 0, 1536), ID[0]], [bank("ms")],
-           *[(lambda h=h: mm(T.ms[0:8, 128 * h:128 * h + 128], T.dg[:, 768 * h + 512:768 * h + 768:32], T.idb[:], True, True)) for h in range(2)])
+        op("t", [("dg", 1024, 1536), ID[0]], [bank("ms")],
+           *[(lambda h=h: mm(T.ms[0:8, 128 * h:128 * h + 128], T.dg[:, 1024 + 256 * h:1280 + 256 * h:32], T.idb[:], True, True)) for h in range(2)])
         sop([bank("ms")], [("ct", 0, 256)], lambda: S.activation(T.ct[0:8, :], T.ms[0:8, 0:256], F.Copy))
 
     def spread_codes():
@@ -455,53 +455,51 @@ def rank_program(g, core, T, topo):
         send([("hb", c, c + 256)], broadcast(T.hb[:, c:c + 256], T.lh[:, o:o + 256], "h%d_%d" % (t, q)))
         for r in near: arrives([("lh", 256 * (N * t + r), 256 * (N * t + r) + 256)], "h%d_%d" % (t, r), near[r])
 
-    def part(buf, c, first, last):
-        return [(lambda b=b, s=s: mm(T.tm[:, 128 * b:128 * b + 128], T.ma[:, 256 * s + 128 * b:256 * s + 128 * b + 128],
-                                     buf[:, c + 128 * s:c + 128 * s + 128], False, last and b == 1 and s == 1)) for b in range(2) for s in range(2)]
+    def part(buf, c, last):
+        return [(lambda e=e: mm(T.tm[:, 128 * e:128 * e + 128], buf[:, c + e:c + 256:2], T.idb[:], False, last and e == 1)) for e in range(2)]
 
     def merge_own(t):
         old, on = (T.tb, "tb") if t else (T.zz, "zz")
-        op("t", [(on, 0, 256), ID[0], ("hb", 256 * t, 256 * t + 256), ("ma", 0, 512)], [bank("tm")],
-           lambda: mm(T.tm[:, 0:256], T.idb[:], old[:, 0:256], True, False), *part(T.hb, 256 * t, False, False))
+        op("t", [(on, 0, 256), ID[0], ("hb", 256 * t, 256 * t + 256)], [bank("tm")],
+           lambda: mm(T.tm[:, 0:256], T.idb[:], old[:, 0:256], True, False), *part(T.hb, 256 * t, False))
 
     def merge(t):
         for r in order:
             c = 256 * (N * t + r)
-            op("t", [("lh", c, c + 256), ("ma", 0, 512)], [bank("tm")], *part(T.lh, c, False, r == order[-1]), adds=True)
+            op("t", [("lh", c, c + 256), ID[0]], [bank("tm")], *part(T.lh, c, r == order[-1]), adds=True)
 
     def living():
         c = 1024 * q
         vop([("ptab", c, c + 1024)], [("nn", 0, 1024)], lambda: V.tensor_scalar(T.nn[:], T.ptab[:, c:c + 1024], 4096.0, None, A.not_equal))
-        for s in range(2):
-            op("t", [("nn", 0, 1024), ("wl", 0, 136)], [bank("key1")],
-               *[(lambda x=x: mm(T.key1[:, 128 * s:128 * s + 128], T.wl[64 * s:64 * s + 64, 7 - x:135 - x],
-                                 T.nn[64 * s:64 * s + 64, 128 * x:128 * x + 128], x == 0, x == 7)) for x in range(8)])
-        vop([bank("key1"), cn(MINE)], [("df", 0, 256)], lambda: V.tensor_scalar(T.df[:], T.key1[:, 0:256], 0.0, cx(MINE), A.is_equal, A.mult))
-        op("t", [("df", 0, 256), ID[0]], [bank("his")], lambda: mm(T.his[:, 0:256], T.idb[:], T.df[:], False, False), adds=True)
+        op("t", [("nn", 0, 1024), ("mo", 0, 8)], [bank("tm")],
+           *[(lambda x=x: mm(T.tm[:, x:64:8], T.nn[:, 128 * x:128 * x + 128], T.mo[:], True, True)) for x in range(8)])
+
+    def born_dead():
+        sop([bank("tm"), cn(NUM[1.0])], [("df", 0, 64)], lambda: S.activation(T.df[:, 0:64], T.tm[:, 0:64], F.Relu, bias=cx(NUM[1.0]), scale=-1.0))
+        op("t", [("df", 0, 64), ID[0]], [bank("his")],
+           *[(lambda n=n: mm(T.his[:, 32 * n + 8 * q:32 * n + 8 * q + 8], T.idb[:], T.df[:, 8 * n:8 * n + 8], False, False)) for n in range(8)], adds=True)
 
     def value(r):
         sop([("pk%d" % r, 0, 256), cn(LOW), cn(HIGH)], [("val", 256 * r, 256 * r + 256)],
             lambda: S.activation(T.val[:, 256 * r:256 * r + 256], pk[r][:], F.Identity, bias=cx(HIGH), scale=cx(LOW)))
 
     fetch(0)
-    op("t", [("ones", 0, 128), ("cr", 0, 144), ("s8", 0, 8), (bo, SXL, SXB)], [bank("wd0")], *own_keys(T.wd0, q, 16, True))
     clear_hist()
-    vop([bank("wd0")], [("bi", 0, 16)], lambda: V.tensor_copy(T.bi[:], T.wd0[:, 0:16]))
-    for h in range(2):
-        digits(h, False)
-        one_hots(h, -1.0, 8)
-        counts(h, range(8), False)
+    vop([bank("key0")], [("bi", 0, 16)], lambda: V.tensor_copy(T.bi[:], T.key0[:, 0:16]))
+    digits(False)
+    parts(0)
+    one_hots(-1.0, 12)
+    counts(range(16), False)
+    opened_lists("tm", [1, 2, 3, 4, 5])
+    tell("ls", 128)
+    expand("g", (q - 1) % N, range(SPREAD[0]))
     living()
 
     for t in range(RO):
         if t > 0:
             like(t, 0, 64)
             low_list()
-        parts(t)
-        if t > 0:
-            if t < 3: expand("s", (q - t - 1) % N, range(SPREAD[t], 16))
-            else:
-                for r in ([0, 1], [2], [3])[t - 3]: value(r)
+            parts(t)
             merge(t - 1)
             sop([bank("tm")], [("tb", 0, 256)], lambda: S.activation(T.tb[:], T.tm[:, 0:256], F.Copy))
             dead_seekers(t)
@@ -516,21 +514,23 @@ def rank_program(g, core, T, topo):
             seeker_words()
         words(t, 0)
         like(t, 128, 256)
-        like_sum(1)
         dead(t, 128, CUT if t else 256)
-        if t > 0: dead_too(CUT, 256)
-        else: expand("s", (q - 1) % N, range(SPREAD[0], 16))
-        decide(t, 0)
-        if t == 0: words(t, 1)
-        one_hots(0, 1.0, 8)
-        counts(0, range(8), False)
-        if t > 0: words(t, 1)
-        decide(t, 1)
-        codes()
-        one_hots(1, 1.0, SHARE)
-        counts(1, range(3), False)
+        if t > 0:
+            like_sum(1)
+            dead_too(CUT, 256)
+            words(t, 1)
+        else:
+            words(t, 1)
+            like_sum(1)
+            born_dead()
+        if t < 3: expand("s", (q - t - 1) % N, range(SPREAD[t], 16))
+        else:
+            for r in ([0, 1], [2], [3])[t - 3]: value(r)
+        best(t)
+        one_hots(1.0, SHARE, codes)
+        counts(range(6), False)
         spread_codes()
-        counts(1, range(3, 8), True)
+        counts(range(6, 16), True)
         exchange(t)
         if t < 2: expand("g", (q - t - 2) % N, range(SPREAD[t + 1]))
         update(t)

@@ -4,10 +4,11 @@ from concourse.bass import DstId, RemoteDMATransfer
 from concourse.mybir import AluOpType as A, ActivationFunctionType as F
 
 N, RO, K = 4, 6, 256
-LEAD = 2
-CUT = 192
-SHARE = 13
-SPREAD = (8, 11, 11)
+FIRST = 40
+CUT0, CUT = 246, 200
+SOON, MORE = (), 20
+SHARE = 12
+SPREAD = (10, 10, 10)
 LN2 = math.log(2.0)
 H0 = 33024.0
 SXL, SXH, SXB, P2S, PBW = 0, 256, 512, 768, 784
@@ -23,16 +24,16 @@ SCRATCH = {
     "cnt": ("sbuf", [128, 256], "bfloat16"), "ig": ("sbuf", [128, 128], "bfloat16"), "prow": ("sbuf", [128, 128], "bfloat16"),
     "clo": ("sbuf", [128, 128], "bfloat16"),
     "idb": ("sbuf", [128, 128], "bfloat16"), "idf": ("sbuf", [128, 128], "float32"), "idq": ("sbuf", [128, 128], "bfloat16"),
-    "idn": ("sbuf", [128, 128], "bfloat16"), "idm": ("sbuf", [128, 128], "bfloat16"),
+    "idn": ("sbuf", [128, 128], "bfloat16"), "lob": ("sbuf", [128, 256], "bfloat16"), "idm": ("sbuf", [128, 128], "bfloat16"),
     "mw": ("sbuf", [128, 8], "bfloat16"), "ml": ("sbuf", [128, 8], "bfloat16"), "mo": ("sbuf", [128, 8], "bfloat16"),
-    "s8": ("sbuf", [128, 8], "bfloat16"), "ex": ("sbuf", [128, 128], "bfloat16"),
+    "all": ("sbuf", [128, 64], "uint16"), "rq": ("sbuf", [128, 512], "bfloat16"), "s8": ("sbuf", [128, 8], "bfloat16"), "ex": ("sbuf", [128, 128], "bfloat16"),
     "prn": ("sbuf", [128, 512], "float32"), "cr": ("sbuf", [128, 144], "bfloat16"),
     "r16": ("sbuf", [128, 128], "bfloat16"), "r32": ("sbuf", [128, 256], "bfloat16"),
     "rwi": ("sbuf", [128, 8], "int32"), "col": ("sbuf", [128, 32], "float32"), "pwb": ("sbuf", [128, 8], "bfloat16"),
     "ci": ("sbuf", [128, 48], "int32"), "cb": ("sbuf", [128, 48], "bfloat16"), "tr": ("sbuf", [128, 256], "float32"),
     "ati": ("sbuf", [128, 192], "int32"), "hf": ("sbuf", [128, 256], "float32"),
     "lf": ("sbuf", [128, 256], "uint16"), "ll": ("sbuf", [128, 256], "uint16"), "h2": ("sbuf", [128, 256], "bfloat16"),
-    "lob": ("sbuf", [128, 256], "bfloat16"), "nm": ("sbuf", [128, 256], "bfloat16"), "p2": ("sbuf", [128, 272], "bfloat16"),
+    "nm": ("sbuf", [128, 256], "bfloat16"), "p2": ("sbuf", [128, 272], "bfloat16"),
     "ab": ("sbuf", [128, 1024], "bfloat16"), "df": ("sbuf", [128, 256], "bfloat16"),
     "y": ("sbuf", [128, 272], "int32"), "ya": ("sbuf", [128, 272], "int32"), "dd": ("sbuf", [128, 272], "float32"),
     "kk": ("sbuf", [128, 272], "float32"), "run": ("sbuf", [128, 256], "float32"), "bi": ("sbuf", [128, 16], "int32"),
@@ -46,7 +47,7 @@ SCRATCH = {
     "ms": ("psum", [128, 512], "float32"), "mt": ("psum", [128, 512], "float32"),
 }
 for _r in range(N):
-    SCRATCH["pk%d" % _r] = ("sbuf", [128, 256], "float32")
+    SCRATCH["pk%d" % _r] = ("sbuf", [128, PBW // 2], "float32")
     SCRATCH["pb%d" % _r] = ("sbuf", [128, PBW], "bfloat16")
     SCRATCH["ls%d" % _r] = ("sbuf", [128, 128], "uint16")
     SCRATCH["re%d" % _r] = ("sbuf", [128, 4096], "float32")
@@ -149,24 +150,31 @@ def rank_program(g, core, T, topo):
     order = sorted(near, key=lambda r: topo.chip(T.cores[r]) != topo.chip(core))
     sent = [0]
 
-    def broadcast(src, dst, sem):
-        trs = [RemoteDMATransfer(dst_ids=[DstId(rid=topo.addr(d)[0], pnc=topo.addr(d)[1]) for d in ds],
-                                 dma_engine_mask=sum(1 << x for x in e), remote_sem=T.sem[sem],
-                                 srcs=[src], dsts=[dst] * len(ds)) for e, ds in plan]
-        sent[0] += sum(len(e) for e, ds in plan)
-        return lambda: g.remote_dma_fused(trs, local_sem=T.sem.sent)
+    def transfers(src, dst, sem, steps):
+        to = [T.cores[(q + s) % N] for s in steps]
+        some = [(e, [d for d in ds if d in to]) for e, ds in plan if set(ds) & set(to)]
+        sent[0] += sum(len(e) for e, ds in some)
+        return [RemoteDMATransfer(dst_ids=[DstId(rid=topo.addr(d)[0], pnc=topo.addr(d)[1]) for d in ds],
+                                  dma_engine_mask=sum(1 << x for x in e), remote_sem=T.sem[sem],
+                                  srcs=[src], dsts=[dst] * len(ds)) for e, ds in some], [x for e, ds in some for x in e]
 
-    def tell(b, w):
-        mine = "%s%d" % (b, q)
-        send([(mine, 0, w)], broadcast(T[mine][:], T[mine][:], "a" + mine))
-        for r in near: arrives([("%s%d" % (b, r), 0, w)], "a%s%d" % (b, r), near[r])
+    def tell(*items):
+        calls = []
+        for b, w, steps in items:
+            mine = "%s%d" % (b, q)
+            trs, used = transfers(T[mine][:, 0:w], T[mine][:, 0:w], "a" + mine, steps)
+            if calls and not set(used) & set(calls[-1][2]): calls[-1] = (calls[-1][0] + [(mine, 0, w)], calls[-1][1] + trs, calls[-1][2] + used)
+            else: calls.append(([(mine, 0, w)], trs, used))
+            for s in steps:
+                r = (q - s) % N
+                arrives([("%s%d" % (b, r), 0, w)], "a%s%d" % (b, r), near[r])
+        for reads, trs, used in calls: send(reads, lambda: g.remote_dma_fused(trs, local_sem=T.sem.sent))
 
     dma("y", [], [("rin", 0, 256)], T.rin[:], T.routes[:])
     dma("s", [], [("cin", 0, 16)], T.cin[:], T.calls[:])
     dma("y", [], [("tin", 0, 1024)], T.tin[:], T.trunk[:])
-    for i in range(4):
-        c = 1024 * ((q + i) % N)
-        dma("sy"[i % 2], [], [("ptab", c, c + 1024)], T.ptab[:, c:c + 1024], T.paths[:, c:c + 1024])
+    for qn, a, b in (("s", 0, 2560), ("y", 2560, 4096)):
+        dma(qn, [], [("ptab", a, b)], T.ptab[:, a:b], T.paths[:, a:b])
 
     def iota(dst, w, pattern, base, cm):
         op("g", [], [(dst, 0, w)], lambda: g.iota(T[dst][:, 0:w], pattern, base, cm, allow_small_or_imprecise_dtypes=True))
@@ -213,21 +221,26 @@ def rank_program(g, core, T, topo):
 
     ci, cb, ati = T.ci, T.cb, T.ati
     own, po, mine, bo, lo_ = pk[q], "pk%d" % q, pb[q], "pb%d" % q, "ls%d" % q
-    vop([("rin", 0, 256)], [(po, 0, 256)], lambda: V.tensor_copy(own[:], T.rin[:]))
-    vop([(po, 0, 256)], [("tr", 0, 256)], lambda: V.transpose(T.tr[:], own[:]))
-    tell("pk", 256)
+    vop([("rin", 0, 256)], [(po, 0, 256)], lambda: V.tensor_copy(own[:, 0:256], T.rin[:]))
+    vop([(po, 0, 256)], [("tr", 0, 256)], lambda: V.transpose(T.tr[:], own[:, 0:256]))
     where("idb", 128, [[-1, 128]], 1.0)
     where("idq", 128, [[-1, 128]], -1.0)
-    where("idn", 128, [[-1, 128]], -32.0)
-    where("idm", 128, [[-1, 128]], -2097152.0)
-    where("ex", 128, [[-1, 8], [0, 16]], 1.0)
+    iota("clo", 128, [[-1, 128]], 127, 0)
 
     def expand(qn, r, ps):
         for p in ps:
-            if qn == "s": f = lambda: S.activation(rx[r][:, p::16], pk[r][:], F.Copy)
-            else: f = lambda: g.affine_select(rx[r][:, p::16], pk[r][:], [[0, 256]], A.is_ge, 0.0, 0, 0)
+            if qn == "s": f = lambda: S.activation(rx[r][:, p::16], pk[r][:, 0:256], F.Copy)
+            else: f = lambda: g.affine_select(rx[r][:, p::16], pk[r][:, 0:256], [[0, 256]], A.is_ge, 0.0, 0, 0)
             op(qn, [("pk%d" % r, 0, 256)], [("re%d" % r, 256 * p, 256 * p + 256)], f)
-    expand("s", q, range(8))
+    expand("s", q, range(11))
+    expand("g", q, range(13, 16))
+    iota("dg", 512, [[0, 512]], 1, 0)
+    where("idn", 128, [[-1, 128]], -32.0)
+    where("idm", 128, [[-1, 128]], -2097152.0)
+    tell(("pk", 256, [1]))
+    where("ex", 128, [[-1, 8], [0, 16]], 1.0)
+    op("g", [], [(po, 256, PBW // 2)], lambda: g.iota(own[:, 256:PBW // 2], [[0, PBW // 2 - 256]], 0, 0, allow_small_or_imprecise_dtypes=True))
+    op("g", [("tin", 0, 1024)], [("ttab", 0, 1024)], lambda: g.affine_select(T.ttab[:], T.tin[:], [[0, 1024]], A.is_ge, 0.0, 0, 0))
 
     def opened(b, ts):
         op("t", [("tr", 0, 256), ("prn", 0, 512)], [bank(b)],
@@ -256,30 +269,26 @@ def rank_program(g, core, T, topo):
     opened_lists("wd0", [0])
     match("s8", 0, 8, IG, T.ig[:, 0::16], PART, -32.0, A.mult)
     vop([("prow", 0, 128), ("cr", 0, 144)], [("cr", 201, 202)], lambda: V.tensor_copy(T.cr[0:1, 16:144], T.prow[0:1, :]))
-    vop([("tin", 0, 1024)], [("ttab", 0, 1024)], lambda: V.tensor_copy(T.ttab[:], T.tin[:]))
     sop([bank("ms")], [(bo, SXL, SXB)], lambda: S.activation(mine[:, SXL:SXB], T.ms[:], F.Copy))
     sop([bank("mt")], [(bo, SXB, P2S)], lambda: S.activation(mine[:, SXB:P2S], T.mt[:, 0:256], F.Copy))
     op("t", [(bo, SXH, SXB), ID[0]], [bank("wd1")],
        *[(lambda h=h: mm(T.wd1[:, 8 * h:8 * h + 8], mine[:, SXH + 128 * h:SXH + 128 * h + 128], T.idb[:, 0::16], True, True)) for h in range(2)])
     sop([bank("wd1"), cn(NUM[144 * LN2])], [(bo, P2S, PBW)],
         lambda: S.activation(mine[:, P2S:PBW], T.wd1[:, 0:16], F.Exp, bias=cx(NUM[144 * LN2]), scale=-LN2 / 256))
-    expand("s", q, range(8, 16))
+    expand("s", q, range(11, 13))
 
     def own_keys(b, r, w, stop):
         return [lambda: mm(b[:, 0:w], T.ones[:], T.cr[:, 0:w], True, False)] + [
             (lambda h=h, c=c: mm(b[:, 8 * h:8 * h + 8], pb[r][:, c + 128 * h:c + 128 * h + 128], T.s8[:], False, stop and h == 1 and c == SXH))
             for h in range(2) for c in (SXL, SXH)]
     op("t", [("ones", 0, 128), CR, ("s8", 0, 8), (bo, SXL, SXB)], [bank("key0")], *own_keys(T.key0, q, 16, True))
-    opened("tm", [1, 2, 3, 4, 5])
     vop([("cin", 0, 16)], [(lo_, CL, CL + 16)], lambda: V.tensor_copy(ls[q][:, CL:CL + 16], T.cin[:]))
     vop([("ci", 0, 16)], [(lo_, SLO, SLO + 16)], lambda: V.tensor_copy(ls[q][:, SLO:SLO + 16], ci[:, 0:16]))
-    tell("pb", PBW)
-    vop([], [("dg", 0, 512)], lambda: V.memset(T.dg[:, 0:512], 1.0))
     match("idf", 0, 128, CNT, T.cnt[:, 0:128], PART, None)
+    vop([CNT, cn(PP)], [("all", 0, 64)], lambda: V.tensor_scalar(T.all[:], T.cnt[:, 0:64], 16.0, cx(PP), A.mult, A.add))
     match("mo", 0, 8, IG, T.ig[:, 0::16], G16, None)
     match("ml", 0, 8, IG, T.ig[:, 0::16], G16, 131072.0, A.mult)
     vop([("mo", 0, 8), ("pwb", 0, 1)], [("mw", 0, 8)], lambda: V.tensor_scalar(T.mw[:], T.mo[:], T.pwb[:, 0:1], None, A.mult))
-    vop([CNT], [("clo", 0, 128)], lambda: V.tensor_scalar(T.clo[:], T.cnt[:, 0:128], -1.0, 127.0, A.mult, A.add))
     column(BACK, PP, -1.0, 15.0, A.mult, A.add)
     column(LOW, PP, float(RO), None, A.is_lt)
     column(HIGH, PP, float(RO), 4096.0, A.is_ge, A.mult)
@@ -303,21 +312,19 @@ def rank_program(g, core, T, topo):
             sop([("clo", 0, 128), ("dg", 512, 1024)], [("ab", a, a + 128)],
                 lambda: S.activation(T.ab[:, a:a + 128], T.clo[:], F.Abs, bias=low[n], scale=-1.0))
         if between: between()
-        if share < 16:
-            w = 128 * (16 - share)
-            sop([("ab", 0, w), cn(NUM[1.0])], [("ol", 2048 - w, 2048)],
-                lambda: S.activation(T.ol[:, 2048 - w:2048], T.ab[:, 0:w], F.Relu, bias=cx(NUM[1.0]), scale=-1.0))
+        w = 128 * (16 - share)
+        sop([("ab", 0, w), cn(NUM[1.0])], [("ol", 2048 - w, 2048)],
+            lambda: S.activation(T.ol[:, 2048 - w:2048], T.ab[:, 0:w], F.Relu, bias=cx(NUM[1.0]), scale=-1.0))
         for c in (0, 256):
             vop([("r32", 0, 256), ("dg", c, c + 256)], [("up", c, c + 256)],
                 lambda: V.tensor_tensor_scan(T.up[:, c:c + 256], T.r32[:], T.dg[:, c:c + 256], 0.0, A.mult, A.add))
+        for c in (0, 256):
+            vop([("up", c, c + 256)], [("oh", c, c + 256)],
+                lambda: V.tensor_scalar(T.oh[:, c:c + 256], T.up[:, c:c + 256], 31.0, sign, A.is_equal, A.mult))
         for n in range(share):
             a = 128 * n
             vop([("clo", 0, 128), ("dg", 512, 1024)], [("ol", a, a + 128)],
                 lambda: V.tensor_scalar(T.ol[:, a:a + 128], T.clo[:], low[n], None, A.is_equal))
-            if n < 2:
-                c = 256 * n
-                vop([("up", c, c + 256)], [("oh", c, c + 256)],
-                    lambda: V.tensor_scalar(T.oh[:, c:c + 256], T.up[:, c:c + 256], 31.0, sign, A.is_equal, A.mult))
 
     def counts(ns, last):
         for n in ns:
@@ -329,16 +336,17 @@ def rank_program(g, core, T, topo):
         r = (q - t) % N
         at = ls[r][:, 16 * t:16 * t + 16]
         lsn = ("ls%d" % r, 16 * t, 16 * t + 16)
-        vop([("ttab", 0, 1024), lsn], [("lf", 0, 256)], lambda: V.tensor_copy(T.lf[:], T.ttab[:].indirect(at)))
-        sop([("ttab", 0, 1024), lsn], [("hf", 0, 256)], lambda: S.activation(T.hf[:], T.ttab[:].indirect(at), F.Copy))
+        tab = "ttab" if t else "tin"
+        vop([(tab, 0, 1024), lsn], [("lf", 0, 256)], lambda: V.tensor_copy(T.lf[:], T[tab][:].indirect(at)))
+        sop([(tab, 0, 1024), lsn], [("hf", 0, 256)], lambda: S.activation(T.hf[:], T[tab][:].indirect(at), F.Copy))
         sop([("hf", 0, 256), cn(NUM[H0 - 127.5])], [("h2", 0, 256)], lambda: S.activation(T.h2[:], T.hf[:], F.Identity, bias=cx(NUM[H0 - 127.5])))
-        op("t", [("hf", 0, 256), ("h2", 0, 256)] + ID, [bank("ms")],
-           lambda: mm(T.ms[:, 256:512], T.idf[:], T.hf[:], True, False),
-           lambda: mm(T.ms[:, 256:512], T.idq[:], T.h2[:], False, True),
-           *[(lambda h=h: mm(T.ms[:, 128 * h:128 * h + 128], T.h2[:, 128 * h:128 * h + 128], T.idb[:], True, True)) for h in range(2 if t else 0)])
-        op("t", [("h2", 0, 256), ("pb%d" % r, SXB, P2S)] + ID, [bank("wd1")],
-           lambda: mm(T.wd1[:, 0:256], T.idb[:], T.h2[:], True, False),
-           lambda: mm(T.wd1[:, 0:256], T.idq[:], pb[r][:, SXB:P2S], False, True))
+        op("t", [("pb%d" % r, SXB, P2S)] + ID, [bank("wd1")], lambda: mm(T.wd1[:, 0:256], T.idq[:], pb[r][:, SXB:P2S], True, False))
+        op("t", [("hf", 0, 256)] + ID, [bank("ms")], lambda: mm(T.ms[:, 256:512], T.idf[:], T.hf[:], True, False))
+        op("t", [("h2", 0, 256)], [bank("ms")], lambda: mm(T.ms[:, 256:512], T.idq[:], T.h2[:], False, True), adds=True)
+        op("t", [("h2", 0, 256)], [bank("wd1")], lambda: mm(T.wd1[:, 0:256], T.idb[:], T.h2[:], False, True), adds=True)
+        if t > 0:
+            op("t", [("h2", 0, 256)], [bank("wd0")],
+               *[(lambda h=h: mm(T.wd0[:, 128 * h:128 * h + 128], T.h2[:, 128 * h:128 * h + 128], T.idb[:], True, True)) for h in range(2)])
 
     def low_list():
         vop([bank("ms")], [("ll", 0, 256)], lambda: V.tensor_scalar(T.ll[:], T.ms[:, 256:512], H0, None, A.add))
@@ -346,11 +354,14 @@ def rank_program(g, core, T, topo):
     def parts(t):
         r = (q - t) % N
         sop([bank("wd1"), cn(NUM[128.0])], [("nm", 0, 256)], lambda: S.activation(T.nm[:], T.wd1[:, 0:256], F.Sign, bias=cx(NUM[128.0])))
-        sop([bank("ms"), cn(NUM[H0])], [("lob", 0, 256)], lambda: S.activation(T.lob[:], T.ms[:, 256:512], F.Identity, bias=cx(NUM[H0])))
         if t > 0:
-            sop([bank("ms"), cn(NUM[144 * LN2])], [("p2", 16, 272)],
-                lambda: S.activation(T.p2[:, 16:272], T.ms[:, 0:256], F.Exp, bias=cx(NUM[144 * LN2]), scale=-LN2 / 256))
-            sop([("pb%d" % r, P2S, PBW)], [("p2", 0, 16)], lambda: S.activation(T.p2[:, 0:16], pb[r][:, P2S:PBW], F.Copy))
+            sop([bank("wd0"), cn(NUM[144 * LN2])], [("p2", 16, 272)],
+                lambda: S.activation(T.p2[:, 16:272], T.wd0[:, 0:256], F.Exp, bias=cx(NUM[144 * LN2]), scale=-LN2 / 256))
+        sop([bank("ms"), cn(NUM[H0])], [("lob", 0, 256)], lambda: S.activation(T.lob[:], T.ms[:, 256:512], F.Identity, bias=cx(NUM[H0])))
+
+    def own_powers(t):
+        r = (q - t) % N
+        sop([("pb%d" % r, P2S, PBW)], [("p2", 0, 16)], lambda: S.activation(T.p2[:, 0:16], pb[r][:, P2S:PBW], F.Copy))
 
     def key_base(t, h):
         r, c = (q - t) % N, 128 * h
@@ -388,9 +399,13 @@ def rank_program(g, core, T, topo):
             sop([("tb", 0, 256), ("ll", a, b)], [("al", 16 * a, 16 * b)],
                 lambda: S.activation(T.al[:, 16 * a:16 * b], T.tb[:].indirect(T.ll[:, a:b]), F.Sign))
 
-    def dead_too(a, b):
-        vop([("tb", 0, 256), ("ll", a, b)], [("al", 16 * a, 16 * b)],
-            lambda: V.tensor_scalar(T.al[:, 16 * a:16 * b], T.tb[:].indirect(T.ll[:, a:b]), 0.0, None, A.is_gt))
+    def dead_too(t, a, b):
+        if t == 0:
+            vop([("ptab", 0, 4096), ("lf", a, b)], [("al", 16 * a, 16 * b)],
+                lambda: V.tensor_scalar(T.al[:, 16 * a:16 * b], T.ptab[:].indirect(T.lf[:, a:b]), 4096.0, None, A.not_equal))
+        else:
+            vop([("tb", 0, 256), ("ll", a, b)], [("al", 16 * a, 16 * b)],
+                lambda: V.tensor_scalar(T.al[:, 16 * a:16 * b], T.tb[:].indirect(T.ll[:, a:b]), 0.0, None, A.is_gt))
 
     def dead_seekers(t):
         r = (q - t) % N
@@ -424,27 +439,28 @@ def rank_program(g, core, T, topo):
                         lambda: V.tensor_tensor_scan(T.run[:, c:c + 128], T.r16[:], T.kk[:, 16 + c:144 + c], 0.0, A.mult, A.max))]
 
     def best(t):
-        a, b = decide(t, 0), decide(t, 1)
-        for i in range(LEAD): a.pop(0)()
-        for x, y in zip(a + [None] * LEAD, b):
-            if x: x()
+        for x, y in zip(decide(t, 0), decide(t, 1)):
+            x()
             y()
         self_key, sn = (T.kk, ("kk", 0, 16)) if t else (T.key0, bank("key0"))
         vop([("run", 0, 256), sn], [("bi", 0, 16)], lambda: V.tensor_tensor(T.bi[:], self_key[:, 0:16], T.run[:, 15::16], A.max))
         digits(True)
 
     def codes():
-        op("t", [("dg", 1024, 1536), ID[0]], [bank("ms")],
-           *[(lambda h=h: mm(T.ms[0:8, 128 * h:128 * h + 128], T.dg[:, 1024 + 256 * h:1280 + 256 * h:32], T.idb[:], True, True)) for h in range(2)])
-        sop([bank("ms")], [("ct", 0, 256)], lambda: S.activation(T.ct[0:8, :], T.ms[0:8, 0:256], F.Copy))
+        op("t", [("dg", 1024, 1536), ID[0]], [bank("wd1")],
+           *[(lambda h=h: mm(T.wd1[0:8, 128 * h:128 * h + 128], T.dg[:, 1024 + 256 * h:1280 + 256 * h:32], T.idb[:], True, True)) for h in range(2)])
+        sop([bank("wd1")], [("ct", 0, 256)], lambda: S.activation(T.ct[0:8, :], T.wd1[0:8, 0:256], F.Copy))
 
     def spread_codes():
-        op("t", [("ct", 0, 256), ("ex", 0, 128)], [bank("mt")], lambda: mm(T.mt[:, 0:256], T.ex[0:8, :], T.ct[0:8, :], True, True))
+        op("t", [("ct", 0, 256), ("ex", 0, 128)], [bank("wd0")], lambda: mm(T.wd0[:, 0:256], T.ex[0:8, :], T.ct[0:8, :], True, True))
 
     def update(t):
         r = (q - t) % N
-        vop([bank("mt"), cn(BACK)], [("t1", 0, 256)], lambda: V.tensor_scalar(T.t1[:], T.mt[:, 0:256], cx(BACK), None, A.is_equal))
-        vop([("t1", 0, 256), bank("ms")], [("t2", 0, 256)], lambda: V.tensor_tensor(T.t2[:], T.ms[:, 256:512], T.t1[:], A.mult))
+        for c in (0, 128):
+            vop([bank("wd0"), cn(BACK)], [("t1", c, c + 128)], lambda: V.tensor_scalar(T.t1[:, c:c + 128], T.wd0[:, c:c + 128], cx(BACK), None, A.is_equal))
+        for c in (0, 128):
+            vop([("t1", c, c + 128), bank("ms")], [("t2", c, c + 128)],
+                lambda: V.tensor_tensor(T.t2[:, c:c + 128], T.ms[:, 256 + c:384 + c], T.t1[:, c:c + 128], A.mult))
         vop([("t2", 0, 256), ("hf", 0, 256), ("ls%d" % r, 16 * t, 16 * t + 16)], [("ttab", 0, 1024)],
             lambda: V.tensor_tensor(T.ttab[:].indirect(ls[r][:, 16 * t:16 * t + 16]), T.t2[:], T.hf[:], A.add))
 
@@ -452,7 +468,8 @@ def rank_program(g, core, T, topo):
         c = 256 * t
         sop([bank("his")], [("hb", c, c + 256)], lambda: S.activation(T.hb[:, c:c + 256], T.his[:, 0:256], F.Copy))
         o = 256 * (N * t + q)
-        send([("hb", c, c + 256)], broadcast(T.hb[:, c:c + 256], T.lh[:, o:o + 256], "h%d_%d" % (t, q)))
+        trs = transfers(T.hb[:, c:c + 256], T.lh[:, o:o + 256], "h%d_%d" % (t, q), range(1, N))[0]
+        send([("hb", c, c + 256)], lambda: g.remote_dma_fused(trs, local_sem=T.sem.sent))
         for r in near: arrives([("lh", 256 * (N * t + r), 256 * (N * t + r) + 256)], "h%d_%d" % (t, r), near[r])
 
     def part(buf, c, last):
@@ -470,7 +487,8 @@ def rank_program(g, core, T, topo):
 
     def living():
         c = 1024 * q
-        vop([("ptab", c, c + 1024)], [("nn", 0, 1024)], lambda: V.tensor_scalar(T.nn[:], T.ptab[:, c:c + 1024], 4096.0, None, A.not_equal))
+        sop([("ptab", c, c + 1024), ("all", 0, 64), cn(NUM[4096.0])], [("nn", 0, 1024)],
+            lambda: S.activation(T.nn[:], T.ptab[:, c:c + 1024].indirect(T.all[:]), F.Sign, bias=cx(NUM[4096.0]), scale=-1.0))
         op("t", [("nn", 0, 1024), ("mo", 0, 8)], [bank("tm")],
            *[(lambda x=x: mm(T.tm[:, x:64:8], T.nn[:, 128 * x:128 * x + 128], T.mo[:], True, True)) for x in range(8)])
 
@@ -481,23 +499,39 @@ def rank_program(g, core, T, topo):
 
     def value(r):
         sop([("pk%d" % r, 0, 256), cn(LOW), cn(HIGH)], [("val", 256 * r, 256 * r + 256)],
-            lambda: S.activation(T.val[:, 256 * r:256 * r + 256], pk[r][:], F.Identity, bias=cx(HIGH), scale=cx(LOW)))
+            lambda: S.activation(T.val[:, 256 * r:256 * r + 256], pk[r][:, 0:256], F.Identity, bias=cx(HIGH), scale=cx(LOW)))
 
+    def aside(t):
+        if t < 3: expand("s", (q - t - 1) % N, range(SPREAD[t], 16 if t else 13))
+        if t == 3: sop([("rb", 512 * q, 512 * q + 512)], [("rq", 0, 512)], lambda: S.activation(T.rq[:], T.rb[:, 512 * q:512 * q + 512], F.Copy, scale=4096.0))
+        if t > 1: value((q + t - 2) % N)
+        if t + 1 < RO: own_powers(t + 1)
+
+    def routes_in(r):
+        vop([("val", 256 * r, 256 * r + 256), ("ls%d" % r, CL, CL + 16)], [("ptab", 0, 4096)],
+            lambda: V.tensor_copy(T.ptab[:].indirect(ls[r][:, CL:CL + 16]), T.val[:, 256 * r:256 * r + 256]))
+
+    def packages(step):
+        tell(("pb", PBW, [step]), *[("pk", PBW // 2, [step + 1])][:N - 1 - step])
+        if step == 1: tell(("ls", 128, range(1, N)))
+    opened("tm", [1, 2, 3])
     fetch(0)
+    opened("tm", [4, 5])
     clear_hist()
     vop([bank("key0")], [("bi", 0, 16)], lambda: V.tensor_copy(T.bi[:], T.key0[:, 0:16]))
     digits(False)
+    dead(0, 0, 64)
     parts(0)
     one_hots(-1.0, 12)
-    counts(range(16), False)
+    like(0, 0, FIRST)
     opened_lists("tm", [1, 2, 3, 4, 5])
-    tell("ls", 128)
+    packages(1)
     expand("g", (q - 1) % N, range(SPREAD[0]))
-    living()
+    counts(range(16), False)
 
     for t in range(RO):
         if t > 0:
-            like(t, 0, 64)
+            like(t, 0, FIRST)
             low_list()
             parts(t)
             merge(t - 1)
@@ -506,49 +540,50 @@ def rank_program(g, core, T, topo):
         key_base(t, 0)
         key_base(t, 1)
         difference(t)
-        dead(t, 0, 128)
-        like(t, 64 if t else 0, 128)
+        dead(t, 0 if t else 64, 128)
+        like(t, FIRST, 128)
         like_sum(0)
         if t > 0:
             clear_hist()
             seeker_words()
         words(t, 0)
-        like(t, 128, 256)
-        dead(t, 128, CUT if t else 256)
-        if t > 0:
-            like_sum(1)
-            dead_too(CUT, 256)
-            words(t, 1)
-        else:
-            words(t, 1)
-            like_sum(1)
+        cut = CUT0 if t == 0 else CUT + MORE * (t in SOON)
+        like(t, 128, 192)
+        dead_too(t, cut, 256)
+        if t in SOON: routes_in((q + SOON.index(t)) % N)
+        like(t, 192, 256)
+        dead(t, 128, cut)
+        words(t, 1)
+        like_sum(1)
+        if t == 0:
+            living()
+            expand("s", (q - 1) % N, range(13, 16))
             born_dead()
-        if t < 3: expand("s", (q - t - 1) % N, range(SPREAD[t], 16))
-        else:
-            for r in ([0, 1], [2], [3])[t - 3]: value(r)
         best(t)
+        if t > 0: aside(t)
         one_hots(1.0, SHARE, codes)
         counts(range(6), False)
         spread_codes()
         counts(range(6, 16), True)
         exchange(t)
-        if t < 2: expand("g", (q - t - 2) % N, range(SPREAD[t + 1]))
+        if t == 0: aside(t)
+        if t < 2:
+            packages(t + 2)
+            expand("g", (q - t - 2) % N, range(SPREAD[t + 1]))
         update(t)
         merge_own(t)
         if t + 1 < RO: fetch(t + 1)
 
     dma("y", [("ttab", 0, 1024)], [], T.yt[:], T.ttab[:])
-    for r in range(N):
-        vop([("val", 256 * r, 256 * r + 256), ("ls%d" % r, CL, CL + 16)], [("ptab", 0, 4096)],
-            lambda: V.tensor_copy(T.ptab[:].indirect(ls[r][:, CL:CL + 16]), T.val[:, 256 * r:256 * r + 256]))
+    for i in range(len(SOON), N): routes_in((q + i) % N)
     merge(RO - 1)
-    vop([bank("tm")], [("tq", 0, 256)], lambda: V.tensor_scalar(T.tq[:], T.tm[:, 0:256], 1.0, 4096.0, A.min, A.mult))
+    sop([bank("tm")], [("tq", 0, 256)], lambda: S.activation(T.tq[:], T.tm[:, 0:256], F.Sign))
     for h in range(2):
-        op("t", [("tq", 0, 256), ("rb", 0, 2048)], [bank("wd%d" % h)],
-           *[(lambda x=x: mm(wd[h][:, 256 * x:256 * x + 256], T.rb[:, 128 * (4 * q + 2 * h + x):128 * (4 * q + 2 * h + x) + 128], T.tq[:], True, True)) for x in range(2)])
-        c = 1024 * q + 512 * h
-        vop([bank("wd%d" % h), ("ptab", c, c + 512)], [("out", 512 * h, 512 * h + 512)],
-            lambda: V.tensor_tensor(T.out[:, 512 * h:512 * h + 512], wd[h][:], T.ptab[:, c:c + 512], A.max))
-        dma("ys"[h], [("out", 512 * h, 512 * h + 512)], [], T.yp[:, 512 * h:512 * h + 512], T.out[:, 512 * h:512 * h + 512])
+        a, c = 512 * h, 1024 * q + 512 * h
+        op("t", [("tq", 0, 256), ("rq", 0, 512)], [bank("wd%d" % h)],
+           *[(lambda x=x: mm(wd[h][:, 256 * x:256 * x + 256], T.rq[:, 256 * h + 128 * x:256 * h + 128 * x + 128], T.tq[:], True, True)) for x in range(2)])
+        vop([bank("wd%d" % h), ("ptab", c, c + 512)], [("out", a, a + 512)],
+            lambda: V.tensor_tensor(T.out[:, a:a + 512], wd[h][:], T.ptab[:, c:c + 512], A.max))
+        dma("ys"[h], [("out", a, a + 512)], [], T.yp[:, a:a + 512], T.out[:, a:a + 512])
     g.wait_ge(T.sem.sent, sent[0])
     finish()

import math
import numpy as np
from concourse.bass import DstId, RemoteDMATransfer
from concourse.mybir import AluOpType as A, ActivationFunctionType as F

N, RO, K = 4, 6, 256
FIRST = 40
CUT0, CUT = 246, 200
SOON, MORE = (), 20
SHARE = 12
SPREAD = (10, 10, 10)
LN2 = math.log(2.0)
H0 = 33024.0
SXL, SXH, SXB, P2S, PBW = 0, 256, 512, 768, 784
CL, SLO = 96, 112

SCRATCH = {
    "ptab": ("sbuf", [128, 4096], "int32"), "tin": ("sbuf", [128, 1024], "int32"), "ttab": ("sbuf", [128, 1024], "float32"),
    "cin": ("sbuf", [128, 16], "int32"), "rin": ("sbuf", [128, 256], "int32"),
    "nn": ("sbuf", [128, 1024], "bfloat16"), "eq": ("sbuf", [128, 4096], "bfloat16"), "al": ("sbuf", [128, 4096], "bfloat16"),
    "als": ("sbuf", [128, 256], "bfloat16"), "tb": ("sbuf", [128, 256], "bfloat16"), "tq": ("sbuf", [128, 256], "bfloat16"),
    "hb": ("sbuf", [128, RO * 256], "bfloat16"), "lh": ("sbuf", [128, RO * N * 256], "bfloat16"),
    "ones": ("sbuf", [128, 128], "bfloat16"), "zz": ("sbuf", [128, 256], "bfloat16"), "rb": ("sbuf", [128, 2048], "bfloat16"),
    "cnt": ("sbuf", [128, 256], "bfloat16"), "ig": ("sbuf", [128, 128], "bfloat16"), "prow": ("sbuf", [128, 128], "bfloat16"),
    "clo": ("sbuf", [128, 128], "bfloat16"),
    "idb": ("sbuf", [128, 128], "bfloat16"), "idf": ("sbuf", [128, 128], "float32"), "idq": ("sbuf", [128, 128], "bfloat16"),
    "idn": ("sbuf", [128, 128], "bfloat16"), "lob": ("sbuf", [128, 256], "bfloat16"), "idm": ("sbuf", [128, 128], "bfloat16"),
    "mw": ("sbuf", [128, 8], "bfloat16"), "ml": ("sbuf", [128, 8], "bfloat16"), "mo": ("sbuf", [128, 8], "bfloat16"),
    "all": ("sbuf", [128, 64], "uint16"), "rq": ("sbuf", [128, 512], "bfloat16"), "s8": ("sbuf", [128, 8], "bfloat16"), "ex": ("sbuf", [128, 128], "bfloat16"),
    "prn": ("sbuf", [128, 512], "float32"), "cr": ("sbuf", [128, 144], "bfloat16"),
    "r16": ("sbuf", [128, 128], "bfloat16"), "r32": ("sbuf", [128, 256], "bfloat16"),
    "rwi": ("sbuf", [128, 8], "int32"), "col": ("sbuf", [128, 32], "float32"), "pwb": ("sbuf", [128, 8], "bfloat16"),
    "ci": ("sbuf", [128, 48], "int32"), "cb": ("sbuf", [128, 48], "bfloat16"), "tr": ("sbuf", [128, 256], "float32"),
    "ati": ("sbuf", [128, 192], "int32"), "hf": ("sbuf", [128, 256], "float32"),
    "lf": ("sbuf", [128, 256], "uint16"), "ll": ("sbuf", [128, 256], "uint16"), "h2": ("sbuf", [128, 256], "bfloat16"),
    "nm": ("sbuf", [128, 256], "bfloat16"), "p2": ("sbuf", [128, 272], "bfloat16"),
    "ab": ("sbuf", [128, 1024], "bfloat16"), "df": ("sbuf", [128, 256], "bfloat16"),
    "y": ("sbuf", [128, 272], "int32"), "ya": ("sbuf", [128, 272], "int32"), "dd": ("sbuf", [128, 272], "float32"),
    "kk": ("sbuf", [128, 272], "float32"), "run": ("sbuf", [128, 256], "float32"), "bi": ("sbuf", [128, 16], "int32"),
    "hl": ("sbuf", [128, 48], "int32"), "dg": ("sbuf", [128, 1536], "bfloat16"), "up": ("sbuf", [128, 512], "bfloat16"),
    "oh": ("sbuf", [128, 512], "bfloat16"), "ol": ("sbuf", [128, 2048], "bfloat16"), "ct": ("sbuf", [128, 256], "bfloat16"),
    "t1": ("sbuf", [128, 256], "float32"), "t2": ("sbuf", [128, 256], "float32"),
    "val": ("sbuf", [128, 1024], "float32"), "out": ("sbuf", [128, 1024], "float32"),
    "key0": ("psum", [128, 512], "float32"), "key1": ("psum", [128, 512], "float32"),
    "wd0": ("psum", [128, 512], "float32"), "wd1": ("psum", [128, 512], "float32"),
    "his": ("psum", [128, 512], "float32"), "tm": ("psum", [128, 512], "float32"),
    "ms": ("psum", [128, 512], "float32"), "mt": ("psum", [128, 512], "float32"),
}
for _r in range(N):
    SCRATCH["pk%d" % _r] = ("sbuf", [128, PBW // 2], "float32")
    SCRATCH["pb%d" % _r] = ("sbuf", [128, PBW], "bfloat16")
    SCRATCH["ls%d" % _r] = ("sbuf", [128, 128], "uint16")
    SCRATCH["re%d" % _r] = ("sbuf", [128, 4096], "float32")
PSUM = [k for k in SCRATCH if SCRATCH[k][0] == "psum"]
SEMAPHORES = (["cv", "cs", "ct", "cg", "sent"] + ["d%d" % i for i in range(16)]
              + ["%s%d" % (b, r) for b in ("apk", "apb", "als") for r in range(N)]
              + ["h%d_%d" % (t, r) for t in range(RO) for r in range(N)])


def scheduler(g, T):
    queues = {"v": g.vector, "s": g.scalar, "t": g.tensor, "g": g, "y": g.sync}
    count, seen, snap, log, dmas = {}, {k: {} for k in queues}, {}, {}, [0]

    def wait(qn, need):
        for s, n in need.items():
            if seen[qn].get(s, 0) >= n: continue
            queues[qn].wait_ge(T.sem[s], n)
            known = dict(snap.get((s, n), {})); known[s] = n
            for a, b in known.items():
                if seen[qn].get(a, 0) < b: seen[qn][a] = b

    def needs(reads, writes, me=None):
        need = {}
        for acc, wr in [(r, False) for r in reads] + [(w, True) for w in writes]:
            for lo, hi, w, s, n in log.get(acc[0], []):
                if lo < acc[2] and acc[1] < hi and (w or wr or (acc[0] in PSUM and s != me)): need[s] = max(need.get(s, 0), n)
        return need, list(reads), list(writes)

    def record(reads, writes, s, n):
        for b, lo, hi in writes:
            log[b] = [e for e in log.get(b, []) if not (lo <= e[0] and e[1] <= hi)] + [(lo, hi, True, s, n)]
        for b, lo, hi in reads:
            log[b] = [e for e in log.get(b, []) if e[2] or e[3] != s or not (lo <= e[0] and e[1] <= hi)] + [(lo, hi, False, s, n)]

    def op(qn, reads, writes, *fns, adds=False):
        need, rd, wr = needs(reads, writes, "c" + qn)
        if adds: need.pop("ct", None)
        wait(qn, need)
        for f in fns: ins = f()
        s = "c" + qn
        count[s] = count.get(s, 0) + 1
        ins.then_inc(T.sem[s], 1)
        snap[(s, count[s])] = dict(seen[qn])
        record(rd, wr, s, count[s])

    def dma(qn, reads, writes, out, in_):
        need, rd, wr = needs(reads, writes)
        wait(qn, need)
        s = "d%d" % dmas[0]
        dmas[0] += 1
        queues[qn].dma_start(out, in_).then_inc(T.sem[s], 16)
        count[s] = 16
        snap[(s, 16)] = dict(seen[qn])
        record(rd, wr, s, 16)

    def arrives(writes, s, n):
        count[s] = n
        record([], writes, s, n)

    def send(reads, f):
        wait("g", needs(reads, [])[0])
        f()

    def finish():
        wait("g", count)
    return op, dma, arrives, send, finish


def rank_program(g, core, T, topo):
    q = T.rank_of(core)
    if q is None: return
    op, dma, arrives, send, finish = scheduler(g, T)
    V, S, P = g.vector, g.scalar, g.tensor
    pk = [T["pk%d" % r] for r in range(N)]
    pb = [T["pb%d" % r] for r in range(N)]
    ls = [T["ls%d" % r] for r in range(N)]
    rx = [T["re%d" % r] for r in range(N)]
    key, wd = [T.key0, T.key1], [T.wd0, T.wd1]
    mm = P.matmul
    ID = [(b, 0, 128) for b in ("idb", "idq", "idn", "idm", "idf")]

    def vop(reads, writes, f): op("v", reads, writes, f)

    def sop(reads, writes, f): op("s", reads, writes, f)

    def bank(b): return (b, 0, 512)

    def ways(c):
        w, used, plan = {}, set(), []
        for d in T.cores:
            if d != c: w.setdefault(tuple(topo.engines(c, d)), []).append(d)
        for es in sorted(w, key=len):
            e = [x for x in es if x not in used]
            e = e[:1 << (len(e).bit_length() - 1)]
            used |= set(e)
            plan.append((e, w[es]))
        return plan
    plan = ways(core)
    near = {r: [len(e) for e, ds in ways(T.cores[r]) if core in ds][0] for r in range(N) if r != q}
    order = sorted(near, key=lambda r: topo.chip(T.cores[r]) != topo.chip(core))
    sent = [0]

    def transfers(src, dst, sem, steps):
        to = [T.cores[(q + s) % N] for s in steps]
        some = [(e, [d for d in ds if d in to]) for e, ds in plan if set(ds) & set(to)]
        sent[0] += sum(len(e) for e, ds in some)
        return [RemoteDMATransfer(dst_ids=[DstId(rid=topo.addr(d)[0], pnc=topo.addr(d)[1]) for d in ds],
                                  dma_engine_mask=sum(1 << x for x in e), remote_sem=T.sem[sem],
                                  srcs=[src], dsts=[dst] * len(ds)) for e, ds in some], [x for e, ds in some for x in e]

    def tell(*items):
        calls = []
        for b, w, steps in items:
            mine = "%s%d" % (b, q)
            trs, used = transfers(T[mine][:, 0:w], T[mine][:, 0:w], "a" + mine, steps)
            if calls and not set(used) & set(calls[-1][2]): calls[-1] = (calls[-1][0] + [(mine, 0, w)], calls[-1][1] + trs, calls[-1][2] + used)
            else: calls.append(([(mine, 0, w)], trs, used))
            for s in steps:
                r = (q - s) % N
                arrives([("%s%d" % (b, r), 0, w)], "a%s%d" % (b, r), near[r])
        for reads, trs, used in calls: send(reads, lambda: g.remote_dma_fused(trs, local_sem=T.sem.sent))

    dma("y", [], [("rin", 0, 256)], T.rin[:], T.routes[:])
    dma("s", [], [("cin", 0, 16)], T.cin[:], T.calls[:])
    dma("y", [], [("tin", 0, 1024)], T.tin[:], T.trunk[:])
    for qn, a, b in (("s", 0, 2560), ("y", 2560, 4096)):
        dma(qn, [], [("ptab", a, b)], T.ptab[:, a:b], T.paths[:, a:b])

    def iota(dst, w, pattern, base, cm):
        op("g", [], [(dst, 0, w)], lambda: g.iota(T[dst][:, 0:w], pattern, base, cm, allow_small_or_imprecise_dtypes=True))

    def where(dst, w, pattern, fill):
        op("g", [("zz", 0, w)], [(dst, 0, w)], lambda: g.affine_select(T[dst][:, 0:w], T.zz[:, 0:w], pattern, A.not_equal, fill, 0, 1))
    PART, PP, P16, G16, PART16, Y0, Y1, BACK, LOW, HIGH = range(10)
    NUM = {144 * LN2: 16, H0 - 127.5: 17, 1.0: 18, H0: 19, 128.0: 20, 4096.0: 21}

    def cx(i): return T.col[:, i:i + 1]

    def cn(i): return ("col", i, i + 1)

    def column(dst, src, s1, s2, *ops):
        vop([cn(src)], [cn(dst)], lambda: V.tensor_scalar(cx(dst), cx(src), s1, s2, *ops))

    def match(dst, a, b, src, view, c, s2, *more, reads=()):
        vop([src, cn(c)] + list(reads), [(dst, a, b)], lambda: V.tensor_scalar(T[dst][:, a:b], view, cx(c), s2, A.is_equal, *more))
    iota("rwi", 1, [[0, 1]], 0, 1)
    iota("cnt", 256, [[1, 256]], 0, 0)
    iota("ig", 128, [[16, 8], [0, 16]], 0, 0)
    iota("prow", 128, [[0, 8], [-1, 16]], 15, 0)
    vop([], [("zz", 0, 256)], lambda: V.memset(T.zz[:], 0.0))
    for i, m in ((PP, 15), (P16, 16), (G16, 112)):
        vop([("rwi", 0, 1)], [("rwi", i, i + 1)], lambda: V.tensor_scalar(T.rwi[:, i:i + 1], T.rwi[:, 0:1], m, None, A.bitwise_and))
    vop([], [("cr", 0, 144)], lambda: V.memset(T.cr[:], 0.0))
    vop([("rwi", 0, 4)], [("col", 0, 4)], lambda: V.tensor_copy(T.col[:, 0:4], T.rwi[:, 0:4]))
    sop([cn(PP)], [("pwb", 0, 1)], lambda: S.activation(T.pwb[:, 0:1], cx(PP), F.Exp, scale=LN2))
    scans = (("r16", 128, 16), ("r32", 256, 32))
    for b, w, step in scans: vop([], [(b, 0, w)], lambda: V.memset(T[b][:], 1.0))
    column(PART16, PART, 16.0, None, A.add)
    column(Y0, P16, 0.0, None, A.is_equal)
    column(Y1, P16, 16.0, None, A.is_equal)
    for b, w, step in scans: vop([], [(b, 0, w)], lambda: V.memset(T[b][:, 0::step], 0.0))
    for row, a, b in ((0, -16.0, None), (32, 1179648.0, -786432.0), (64, 8192.0, 8160.0)):
        vop([("cr", 0, 144)], [("cr", 200 + row, 201 + row)], lambda: V.memset(T.cr[row:row + 1, 0:16], a))
        if b: vop([("cr", 0, 144)], [("cr", 201 + row, 202 + row)], lambda: V.memset(T.cr[row:row + 1, 16:144], b))
    CR = ("cr", 0, 300)
    CNT, IG = ("cnt", 0, 256), ("ig", 0, 128)
    for y in range(2):
        for b in range(2):
            s, c = 16 - 16 * (b - y), 256 * y + 128 * b
            match("prn", c, c + 128, CNT, T.cnt[:, s:s + 128], PART16, cx(Y0 + y), A.mult, reads=[cn(Y0 + y)])

    ci, cb, ati = T.ci, T.cb, T.ati
    own, po, mine, bo, lo_ = pk[q], "pk%d" % q, pb[q], "pb%d" % q, "ls%d" % q
    vop([("rin", 0, 256)], [(po, 0, 256)], lambda: V.tensor_copy(own[:, 0:256], T.rin[:]))
    vop([(po, 0, 256)], [("tr", 0, 256)], lambda: V.transpose(T.tr[:], own[:, 0:256]))
    where("idb", 128, [[-1, 128]], 1.0)
    where("idq", 128, [[-1, 128]], -1.0)
    iota("clo", 128, [[-1, 128]], 127, 0)

    def expand(qn, r, ps):
        for p in ps:
            if qn == "s": f = lambda: S.activation(rx[r][:, p::16], pk[r][:, 0:256], F.Copy)
            else: f = lambda: g.affine_select(rx[r][:, p::16], pk[r][:, 0:256], [[0, 256]], A.is_ge, 0.0, 0, 0)
            op(qn, [("pk%d" % r, 0, 256)], [("re%d" % r, 256 * p, 256 * p + 256)], f)
    expand("s", q, range(11))
    expand("g", q, range(13, 16))
    iota("dg", 512, [[0, 512]], 1, 0)
    where("idn", 128, [[-1, 128]], -32.0)
    where("idm", 128, [[-1, 128]], -2097152.0)
    tell(("pk", 256, [1]))
    where("ex", 128, [[-1, 8], [0, 16]], 1.0)
    op("g", [], [(po, 256, PBW // 2)], lambda: g.iota(own[:, 256:PBW // 2], [[0, PBW // 2 - 256]], 0, 0, allow_small_or_imprecise_dtypes=True))
    op("g", [("tin", 0, 1024)], [("ttab", 0, 1024)], lambda: g.affine_select(T.ttab[:], T.tin[:], [[0, 1024]], A.is_ge, 0.0, 0, 0))

    def opened(b, ts):
        op("t", [("tr", 0, 256), ("prn", 0, 512)], [bank(b)],
           *[(lambda t=t, y=y, x=x: mm(T[b][:, 16 * t + y:16 * t + 16:2], T.prn[:, 256 * y + 128 * x:256 * y + 128 * x + 128],
                                       T.tr[:, 16 * x + t::32], x == 0, x == 1)) for t in ts for y in range(2) for x in range(2)])

    def opened_lists(bn, ts):
        a, b = 16 * ts[0], 16 * ts[-1] + 16
        vop([bank(bn)], [("ati", a, b)], lambda: V.tensor_copy(ati[:, a:b], T[bn][:, a:b]))
        vop([("ati", a, b)], [("ati", 96 + a, 96 + b)], lambda: V.tensor_scalar(ati[:, 96 + a:96 + b], ati[:, a:b], 1023, None, A.bitwise_and))
        vop([("ati", 96 + a, 96 + b)], [(lo_, a, b)], lambda: V.tensor_copy(ls[q][:, a:b], ati[:, 96 + a:96 + b]))
    opened("wd0", [0])
    vop([], [("ones", 0, 128)], lambda: V.memset(T.ones[:], 1.0))
    for x, i in NUM.items(): vop([], [cn(i)], lambda: V.memset(cx(i), x))
    for i, m in ((0, 255), (1, 3840), (2, 3072)):
        vop([("cin", 0, 16)], [("ci", 16 * i, 16 * i + 16)], lambda: V.tensor_scalar(ci[:, 16 * i:16 * i + 16], T.cin[:], m, None, A.bitwise_and))
    vop([("ci", 0, 16)], [("cb", 0, 16)], lambda: V.tensor_copy(cb[:, 0:16], ci[:, 0:16]))
    vop([("ci", 16, 48)], [("cb", 16, 48)], lambda: V.tensor_scalar(cb[:, 16:48], ci[:, 16:48], H0, None, A.add))
    for x in range(16):
        vop([IG, cn(PART)], [("rb", 128 * x, 128 * x + 128)],
            lambda: V.tensor_scalar(T.rb[:, 128 * x:128 * x + 128], T.ig[:], float(x), cx(PART), A.add, A.is_equal))
    op("t", [("cb", 0, 32), ("rb", 0, 2048)], [bank("ms")],
       *[(lambda x=x: mm(T.ms[:, x::16], T.rb[:, 128 * x:128 * x + 128], cb[:, 0:32], True, True)) for x in range(16)])
    op("t", [("cb", 32, 48), ("rb", 0, 2048)], [bank("mt")],
       *[(lambda x=x: mm(T.mt[:, x:256:16], T.rb[:, 128 * x:128 * x + 128], cb[:, 32:48], True, True)) for x in range(16)])
    opened_lists("wd0", [0])
    match("s8", 0, 8, IG, T.ig[:, 0::16], PART, -32.0, A.mult)
    vop([("prow", 0, 128), ("cr", 0, 144)], [("cr", 201, 202)], lambda: V.tensor_copy(T.cr[0:1, 16:144], T.prow[0:1, :]))
    sop([bank("ms")], [(bo, SXL, SXB)], lambda: S.activation(mine[:, SXL:SXB], T.ms[:], F.Copy))
    sop([bank("mt")], [(bo, SXB, P2S)], lambda: S.activation(mine[:, SXB:P2S], T.mt[:, 0:256], F.Copy))
    op("t", [(bo, SXH, SXB), ID[0]], [bank("wd1")],
       *[(lambda h=h: mm(T.wd1[:, 8 * h:8 * h + 8], mine[:, SXH + 128 * h:SXH + 128 * h + 128], T.idb[:, 0::16], True, True)) for h in range(2)])
    sop([bank("wd1"), cn(NUM[144 * LN2])], [(bo, P2S, PBW)],
        lambda: S.activation(mine[:, P2S:PBW], T.wd1[:, 0:16], F.Exp, bias=cx(NUM[144 * LN2]), scale=-LN2 / 256))
    expand("s", q, range(11, 13))

    def own_keys(b, r, w, stop):
        return [lambda: mm(b[:, 0:w], T.ones[:], T.cr[:, 0:w], True, False)] + [
            (lambda h=h, c=c: mm(b[:, 8 * h:8 * h + 8], pb[r][:, c + 128 * h:c + 128 * h + 128], T.s8[:], False, stop and h == 1 and c == SXH))
            for h in range(2) for c in (SXL, SXH)]
    op("t", [("ones", 0, 128), CR, ("s8", 0, 8), (bo, SXL, SXB)], [bank("key0")], *own_keys(T.key0, q, 16, True))
    vop([("cin", 0, 16)], [(lo_, CL, CL + 16)], lambda: V.tensor_copy(ls[q][:, CL:CL + 16], T.cin[:]))
    vop([("ci", 0, 16)], [(lo_, SLO, SLO + 16)], lambda: V.tensor_copy(ls[q][:, SLO:SLO + 16], ci[:, 0:16]))
    match("idf", 0, 128, CNT, T.cnt[:, 0:128], PART, None)
    vop([CNT, cn(PP)], [("all", 0, 64)], lambda: V.tensor_scalar(T.all[:], T.cnt[:, 0:64], 16.0, cx(PP), A.mult, A.add))
    match("mo", 0, 8, IG, T.ig[:, 0::16], G16, None)
    match("ml", 0, 8, IG, T.ig[:, 0::16], G16, 131072.0, A.mult)
    vop([("mo", 0, 8), ("pwb", 0, 1)], [("mw", 0, 8)], lambda: V.tensor_scalar(T.mw[:], T.mo[:], T.pwb[:, 0:1], None, A.mult))
    column(BACK, PP, -1.0, 15.0, A.mult, A.add)
    column(LOW, PP, float(RO), None, A.is_lt)
    column(HIGH, PP, float(RO), 4096.0, A.is_ge, A.mult)
    vop([], [bank("mt")], lambda: V.memset(T.mt[:, 256:272], (8388608.0 + 16) / 32768))
    vop([("prow", 0, 128)], [bank("mt")], lambda: V.tensor_scalar(T.mt[:, 272:400], T.prow[:], 1.0 / 32768, 128.0, A.mult, A.add))

    def clear_hist():
        op("t", [("ones", 0, 128), ("zz", 0, 256)], [bank("his")], lambda: mm(T.his[:, 0:256], T.ones[:], T.zz[:, 0:256], True, False))

    def digits(codes):
        n, sn = 48 if codes else 32, ("bi", 0, 16)
        vop([sn], [("hl", 0, 16)], lambda: V.tensor_scalar(T.hl[:, 0:16], T.bi[:], 12, 0xC1F, A.logical_shift_right, A.bitwise_and))
        vop([sn], [("hl", 16, 32)], lambda: V.tensor_scalar(T.hl[:, 16:32], T.bi[:], 5, 127, A.logical_shift_right, A.bitwise_and))
        if codes: vop([sn], [("hl", 32, 48)], lambda: V.tensor_scalar(T.hl[:, 32:48], T.bi[:], 31, None, A.bitwise_and))
        vop([("hl", 0, n)], [("dg", 0, 32 * n)], lambda: V.tensor_copy(T.dg[:, 0:32 * n:32], T.hl[:, 0:n]))

    def one_hots(sign, share, between=None):
        low = [T.dg[:, 512 + 32 * n:513 + 32 * n] for n in range(16)]
        for n in range(share, 16):
            a = 128 * (n - share)
            sop([("clo", 0, 128), ("dg", 512, 1024)], [("ab", a, a + 128)],
                lambda: S.activation(T.ab[:, a:a + 128], T.clo[:], F.Abs, bias=low[n], scale=-1.0))
        if between: between()
        w = 128 * (16 - share)
        sop([("ab", 0, w), cn(NUM[1.0])], [("ol", 2048 - w, 2048)],
            lambda: S.activation(T.ol[:, 2048 - w:2048], T.ab[:, 0:w], F.Relu, bias=cx(NUM[1.0]), scale=-1.0))
        for c in (0, 256):
            vop([("r32", 0, 256), ("dg", c, c + 256)], [("up", c, c + 256)],
                lambda: V.tensor_tensor_scan(T.up[:, c:c + 256], T.r32[:], T.dg[:, c:c + 256], 0.0, A.mult, A.add))
        for c in (0, 256):
            vop([("up", c, c + 256)], [("oh", c, c + 256)],
                lambda: V.tensor_scalar(T.oh[:, c:c + 256], T.up[:, c:c + 256], 31.0, sign, A.is_equal, A.mult))
        for n in range(share):
            a = 128 * n
            vop([("clo", 0, 128), ("dg", 512, 1024)], [("ol", a, a + 128)],
                lambda: V.tensor_scalar(T.ol[:, a:a + 128], T.clo[:], low[n], None, A.is_equal))

    def counts(ns, last):
        for n in ns:
            c, a, j = 32 * n, 128 * n, 32 * (n % 8)
            op("t", [("oh", c, c + 32), ("ol", a, a + 128)], [bank("his")],
               lambda: mm(T.his[:, j:j + 32], T.ol[:, a:a + 128], T.oh[:, c:c + 32], False, last and n == 15), adds=True)

    def fetch(t):
        r = (q - t) % N
        at = ls[r][:, 16 * t:16 * t + 16]
        lsn = ("ls%d" % r, 16 * t, 16 * t + 16)
        tab = "ttab" if t else "tin"
        vop([(tab, 0, 1024), lsn], [("lf", 0, 256)], lambda: V.tensor_copy(T.lf[:], T[tab][:].indirect(at)))
        sop([(tab, 0, 1024), lsn], [("hf", 0, 256)], lambda: S.activation(T.hf[:], T[tab][:].indirect(at), F.Copy))
        sop([("hf", 0, 256), cn(NUM[H0 - 127.5])], [("h2", 0, 256)], lambda: S.activation(T.h2[:], T.hf[:], F.Identity, bias=cx(NUM[H0 - 127.5])))
        op("t", [("pb%d" % r, SXB, P2S)] + ID, [bank("wd1")], lambda: mm(T.wd1[:, 0:256], T.idq[:], pb[r][:, SXB:P2S], True, False))
        op("t", [("hf", 0, 256)] + ID, [bank("ms")], lambda: mm(T.ms[:, 256:512], T.idf[:], T.hf[:], True, False))
        op("t", [("h2", 0, 256)], [bank("ms")], lambda: mm(T.ms[:, 256:512], T.idq[:], T.h2[:], False, True), adds=True)
        op("t", [("h2", 0, 256)], [bank("wd1")], lambda: mm(T.wd1[:, 0:256], T.idb[:], T.h2[:], False, True), adds=True)
        if t > 0:
            op("t", [("h2", 0, 256)], [bank("wd0")],
               *[(lambda h=h: mm(T.wd0[:, 128 * h:128 * h + 128], T.h2[:, 128 * h:128 * h + 128], T.idb[:], True, True)) for h in range(2)])

    def low_list():
        vop([bank("ms")], [("ll", 0, 256)], lambda: V.tensor_scalar(T.ll[:], T.ms[:, 256:512], H0, None, A.add))

    def parts(t):
        r = (q - t) % N
        sop([bank("wd1"), cn(NUM[128.0])], [("nm", 0, 256)], lambda: S.activation(T.nm[:], T.wd1[:, 0:256], F.Sign, bias=cx(NUM[128.0])))
        if t > 0:
            sop([bank("wd0"), cn(NUM[144 * LN2])], [("p2", 16, 272)],
                lambda: S.activation(T.p2[:, 16:272], T.wd0[:, 0:256], F.Exp, bias=cx(NUM[144 * LN2]), scale=-LN2 / 256))
        sop([bank("ms"), cn(NUM[H0])], [("lob", 0, 256)], lambda: S.activation(T.lob[:], T.ms[:, 256:512], F.Identity, bias=cx(NUM[H0])))

    def own_powers(t):
        r = (q - t) % N
        sop([("pb%d" % r, P2S, PBW)], [("p2", 0, 16)], lambda: S.activation(T.p2[:, 0:16], pb[r][:, P2S:PBW], F.Copy))

    def key_base(t, h):
        r, c = (q - t) % N, 128 * h
        k = key[h][:, 16 - 16 * h:144 - 16 * h]
        first = own_keys(T.key0, r, 144, False) if h == 0 else [lambda: mm(k, T.ones[:], T.cr[:, 16:144], True, False)]
        op("t", [("ones", 0, 128), CR, ("s8", 0, 8), ("pb%d" % r, SXL, SXB), ("h2", c, c + 128), ("lob", c, c + 128), ("nm", c, c + 128)] + ID,
           [bank("key%d" % h)], *first,
           lambda: mm(k, T.h2[:, c:c + 128], T.idn[:], False, False),
           lambda: mm(k, T.lob[:, c:c + 128], T.idn[:], False, False),
           lambda: mm(k, T.nm[:, c:c + 128], T.idm[:], False, False))

    def difference(t):
        r = (q - t) % N
        op("t", [("pb%d" % r, SXL, SXB), ("h2", 0, 256), ("lob", 0, 256)] + ID, [bank("ms")],
           lambda: mm(T.ms[:, 256:512], T.idb[:], pb[r][:, SXH:SXB], True, False),
           lambda: mm(T.ms[:, 256:512], T.idq[:], T.h2[:], False, False),
           lambda: mm(T.ms[:, 256:512], T.idb[:], pb[r][:, SXL:SXH], False, False),
           lambda: mm(T.ms[:, 256:512], T.idq[:], T.lob[:], False, True))

    def like(t, a, b):
        r = (q - t) % N
        vop([("ptab", 0, 4096), ("lf", a, b), ("re%d" % r, 0, 4096)], [("eq", 16 * a, 16 * b)],
            lambda: V.tensor_tensor(T.eq[:, 16 * a:16 * b], T.ptab[:].indirect(T.lf[:, a:b]), rx[r][:, 16 * a:16 * b], A.is_equal))

    def like_sum(h):
        c = 2048 * h
        op("t", [("eq", c, c + 2048), ("ml", 0, 8)], [bank("key%d" % h)],
           *[(lambda p=p: mm(key[h][:, 16 - 16 * h + p:144 - 16 * h:16], T.eq[:, c + p:c + 2048:16], T.ml[:], False, p == 15)) for p in range(16)], adds=True)

    def dead(t, a, b):
        if t == 0:
            sop([("ptab", 0, 4096), ("lf", a, b), cn(NUM[4096.0])], [("al", 16 * a, 16 * b)],
                lambda: S.activation(T.al[:, 16 * a:16 * b], T.ptab[:].indirect(T.lf[:, a:b]), F.Sign, bias=cx(NUM[4096.0]), scale=-1.0))
        else:
            sop([("tb", 0, 256), ("ll", a, b)], [("al", 16 * a, 16 * b)],
                lambda: S.activation(T.al[:, 16 * a:16 * b], T.tb[:].indirect(T.ll[:, a:b]), F.Sign))

    def dead_too(t, a, b):
        if t == 0:
            vop([("ptab", 0, 4096), ("lf", a, b)], [("al", 16 * a, 16 * b)],
                lambda: V.tensor_scalar(T.al[:, 16 * a:16 * b], T.ptab[:].indirect(T.lf[:, a:b]), 4096.0, None, A.not_equal))
        else:
            vop([("tb", 0, 256), ("ll", a, b)], [("al", 16 * a, 16 * b)],
                lambda: V.tensor_scalar(T.al[:, 16 * a:16 * b], T.tb[:].indirect(T.ll[:, a:b]), 0.0, None, A.is_gt))

    def dead_seekers(t):
        r = (q - t) % N
        sop([("tb", 0, 256), ("ls%d" % r, SLO, SLO + 16)], [("als", 0, 256)],
            lambda: S.activation(T.als[:], T.tb[:].indirect(ls[r][:, SLO:SLO + 16]), F.Sign))

    def seeker_words():
        op("t", [("als", 0, 256), ("mw", 0, 8)], [bank("wd0")],
           *[(lambda h=h: mm(T.wd0[:, 8 * h:8 * h + 8], T.als[:, 128 * h:128 * h + 128], T.mw[:], True, True)) for h in range(2)])

    def words(t, h):
        c, w = 2048 * h, "mw" if t else "mo"
        op("t", [("al", c, c + 2048), (w, 0, 8)], [bank("wd%d" % h)],
           *[(lambda p=p: mm(wd[h][:, 16 - 16 * h + p:144 - 16 * h:16], T.al[:, c + p:c + 2048:16], T[w][:], True, True)) for p in range(16)])

    def decide(t, h):
        a = 0 if h == 0 and t > 0 else 16
        e0, e1 = (a, 144) if h == 0 else (144, 272)
        f0, f1 = (a, 144) if h == 0 else (0, 128)
        pf = T.mt[:, 256 + a:400]
        wn, c = bank("wd%d" % h), 128 * h
        if t == 0:
            steps = [lambda: vop([wn], [("ya", e0, e1)], lambda: V.tensor_scalar(T.ya[:, e0:e1], wd[h][:, f0:f1], 0.0, 32768.0, A.is_equal, A.mult))]
        else:
            steps = [lambda: vop([wn, ("p2", e0, e1)], [("y", e0, e1)], lambda: V.tensor_tensor(T.y[:, e0:e1], wd[h][:, f0:f1], T.p2[:, e0:e1], A.mult)),
                     lambda: vop([("y", e0, e1)], [("ya", e0, e1)], lambda: V.tensor_scalar(T.ya[:, e0:e1], T.y[:, e0:e1], 32768, None, A.bitwise_and))]
        return steps + [
            lambda: vop([("ya", e0, e1), bank("mt")], [("dd", e0, e1)], lambda: V.tensor_tensor(T.dd[:, e0:e1], pf, T.ya[:, e0:e1], A.mult)),
            lambda: vop([bank("key%d" % h), ("dd", e0, e1)], [("kk", e0, e1)], lambda: V.tensor_tensor(T.kk[:, e0:e1], key[h][:, f0:f1], T.dd[:, e0:e1], A.max)),
            lambda: vop([("r16", 0, 128), ("kk", 16 + c, 144 + c)], [("run", c, c + 128)],
                        lambda: V.tensor_tensor_scan(T.run[:, c:c + 128], T.r16[:], T.kk[:, 16 + c:144 + c], 0.0, A.mult, A.max))]

    def best(t):
        for x, y in zip(decide(t, 0), decide(t, 1)):
            x()
            y()
        self_key, sn = (T.kk, ("kk", 0, 16)) if t else (T.key0, bank("key0"))
        vop([("run", 0, 256), sn], [("bi", 0, 16)], lambda: V.tensor_tensor(T.bi[:], self_key[:, 0:16], T.run[:, 15::16], A.max))
        digits(True)

    def codes():
        op("t", [("dg", 1024, 1536), ID[0]], [bank("wd1")],
           *[(lambda h=h: mm(T.wd1[0:8, 128 * h:128 * h + 128], T.dg[:, 1024 + 256 * h:1280 + 256 * h:32], T.idb[:], True, True)) for h in range(2)])
        sop([bank("wd1")], [("ct", 0, 256)], lambda: S.activation(T.ct[0:8, :], T.wd1[0:8, 0:256], F.Copy))

    def spread_codes():
        op("t", [("ct", 0, 256), ("ex", 0, 128)], [bank("wd0")], lambda: mm(T.wd0[:, 0:256], T.ex[0:8, :], T.ct[0:8, :], True, True))

    def update(t):
        r = (q - t) % N
        for c in (0, 128):
            vop([bank("wd0"), cn(BACK)], [("t1", c, c + 128)], lambda: V.tensor_scalar(T.t1[:, c:c + 128], T.wd0[:, c:c + 128], cx(BACK), None, A.is_equal))
        for c in (0, 128):
            vop([("t1", c, c + 128), bank("ms")], [("t2", c, c + 128)],
                lambda: V.tensor_tensor(T.t2[:, c:c + 128], T.ms[:, 256 + c:384 + c], T.t1[:, c:c + 128], A.mult))
        vop([("t2", 0, 256), ("hf", 0, 256), ("ls%d" % r, 16 * t, 16 * t + 16)], [("ttab", 0, 1024)],
            lambda: V.tensor_tensor(T.ttab[:].indirect(ls[r][:, 16 * t:16 * t + 16]), T.t2[:], T.hf[:], A.add))

    def exchange(t):
        c = 256 * t
        sop([bank("his")], [("hb", c, c + 256)], lambda: S.activation(T.hb[:, c:c + 256], T.his[:, 0:256], F.Copy))
        o = 256 * (N * t + q)
        trs = transfers(T.hb[:, c:c + 256], T.lh[:, o:o + 256], "h%d_%d" % (t, q), range(1, N))[0]
        send([("hb", c, c + 256)], lambda: g.remote_dma_fused(trs, local_sem=T.sem.sent))
        for r in near: arrives([("lh", 256 * (N * t + r), 256 * (N * t + r) + 256)], "h%d_%d" % (t, r), near[r])

    def part(buf, c, last):
        return [(lambda e=e: mm(T.tm[:, 128 * e:128 * e + 128], buf[:, c + e:c + 256:2], T.idb[:], False, last and e == 1)) for e in range(2)]

    def merge_own(t):
        old, on = (T.tb, "tb") if t else (T.zz, "zz")
        op("t", [(on, 0, 256), ID[0], ("hb", 256 * t, 256 * t + 256)], [bank("tm")],
           lambda: mm(T.tm[:, 0:256], T.idb[:], old[:, 0:256], True, False), *part(T.hb, 256 * t, False))

    def merge(t):
        for r in order:
            c = 256 * (N * t + r)
            op("t", [("lh", c, c + 256), ID[0]], [bank("tm")], *part(T.lh, c, r == order[-1]), adds=True)

    def living():
        c = 1024 * q
        sop([("ptab", c, c + 1024), ("all", 0, 64), cn(NUM[4096.0])], [("nn", 0, 1024)],
            lambda: S.activation(T.nn[:], T.ptab[:, c:c + 1024].indirect(T.all[:]), F.Sign, bias=cx(NUM[4096.0]), scale=-1.0))
        op("t", [("nn", 0, 1024), ("mo", 0, 8)], [bank("tm")],
           *[(lambda x=x: mm(T.tm[:, x:64:8], T.nn[:, 128 * x:128 * x + 128], T.mo[:], True, True)) for x in range(8)])

    def born_dead():
        sop([bank("tm"), cn(NUM[1.0])], [("df", 0, 64)], lambda: S.activation(T.df[:, 0:64], T.tm[:, 0:64], F.Relu, bias=cx(NUM[1.0]), scale=-1.0))
        op("t", [("df", 0, 64), ID[0]], [bank("his")],
           *[(lambda n=n: mm(T.his[:, 32 * n + 8 * q:32 * n + 8 * q + 8], T.idb[:], T.df[:, 8 * n:8 * n + 8], False, False)) for n in range(8)], adds=True)

    def value(r):
        sop([("pk%d" % r, 0, 256), cn(LOW), cn(HIGH)], [("val", 256 * r, 256 * r + 256)],
            lambda: S.activation(T.val[:, 256 * r:256 * r + 256], pk[r][:, 0:256], F.Identity, bias=cx(HIGH), scale=cx(LOW)))

    def aside(t):
        if t < 3: expand("s", (q - t - 1) % N, range(SPREAD[t], 16 if t else 13))
        if t == 3: sop([("rb", 512 * q, 512 * q + 512)], [("rq", 0, 512)], lambda: S.activation(T.rq[:], T.rb[:, 512 * q:512 * q + 512], F.Copy, scale=4096.0))
        if t > 1: value((q + t - 2) % N)
        if t + 1 < RO: own_powers(t + 1)

    def routes_in(r):
        vop([("val", 256 * r, 256 * r + 256), ("ls%d" % r, CL, CL + 16)], [("ptab", 0, 4096)],
            lambda: V.tensor_copy(T.ptab[:].indirect(ls[r][:, CL:CL + 16]), T.val[:, 256 * r:256 * r + 256]))

    def packages(step):
        tell(("pb", PBW, [step]), *[("pk", PBW // 2, [step + 1])][:N - 1 - step])
        if step == 1: tell(("ls", 128, range(1, N)))
    opened("tm", [1, 2, 3])
    fetch(0)
    opened("tm", [4, 5])
    clear_hist()
    vop([bank("key0")], [("bi", 0, 16)], lambda: V.tensor_copy(T.bi[:], T.key0[:, 0:16]))
    digits(False)
    dead(0, 0, 64)
    parts(0)
    one_hots(-1.0, 12)
    like(0, 0, FIRST)
    opened_lists("tm", [1, 2, 3, 4, 5])
    packages(1)
    expand("g", (q - 1) % N, range(SPREAD[0]))
    counts(range(16), False)

    for t in range(RO):
        if t > 0:
            like(t, 0, FIRST)
            low_list()
            parts(t)
            merge(t - 1)
            sop([bank("tm")], [("tb", 0, 256)], lambda: S.activation(T.tb[:], T.tm[:, 0:256], F.Copy))
            dead_seekers(t)
        key_base(t, 0)
        key_base(t, 1)
        difference(t)
        dead(t, 0 if t else 64, 128)
        like(t, FIRST, 128)
        like_sum(0)
        if t > 0:
            clear_hist()
            seeker_words()
        words(t, 0)
        cut = CUT0 if t == 0 else CUT + MORE * (t in SOON)
        like(t, 128, 192)
        dead_too(t, cut, 256)
        if t in SOON: routes_in((q + SOON.index(t)) % N)
        like(t, 192, 256)
        dead(t, 128, cut)
        words(t, 1)
        like_sum(1)
        if t == 0:
            living()
            expand("s", (q - 1) % N, range(13, 16))
            born_dead()
        best(t)
        if t > 0: aside(t)
        one_hots(1.0, SHARE, codes)
        counts(range(6), False)
        spread_codes()
        counts(range(6, 16), True)
        exchange(t)
        if t == 0: aside(t)
        if t < 2:
            packages(t + 2)
            expand("g", (q - t - 2) % N, range(SPREAD[t + 1]))
        update(t)
        merge_own(t)
        if t + 1 < RO: fetch(t + 1)

    dma("y", [("ttab", 0, 1024)], [], T.yt[:], T.ttab[:])
    for i in range(len(SOON), N): routes_in((q + i) % N)
    merge(RO - 1)
    sop([bank("tm")], [("tq", 0, 256)], lambda: S.activation(T.tq[:], T.tm[:, 0:256], F.Sign))
    for h in range(2):
        a, c = 512 * h, 1024 * q + 512 * h
        op("t", [("tq", 0, 256), ("rq", 0, 512)], [bank("wd%d" % h)],
           *[(lambda x=x: mm(wd[h][:, 256 * x:256 * x + 256], T.rq[:, 256 * h + 128 * x:256 * h + 128 * x + 128], T.tq[:], True, True)) for x in range(2)])
        vop([bank("wd%d" % h), ("ptab", c, c + 512)], [("out", a, a + 512)],
            lambda: V.tensor_tensor(T.out[:, a:a + 512], wd[h][:], T.ptab[:, c:c + 512], A.max))
        dma("ys"[h], [("out", a, a + 512)], [], T.yp[:, a:a + 512], T.out[:, a:a + 512])
    g.wait_ge(T.sem.sent, sent[0])
    finish()
